import numpy as np, ml_dtypes
CORES = [40,64,80,88,96,104,120,144]
N = 8
import mx_ref
BF = ml_dtypes.bfloat16
def gentries(a):
    return np.ascontiguousarray(a.reshape(8, 16, -1).transpose(0, 2, 1)).reshape(8, -1)
def gtable(e):
    e = np.asarray(e); return np.ascontiguousarray(e.reshape(8, -1, 16).transpose(0, 2, 1)).reshape(128, -1).astype(np.int32)
def gcols(t, e):
    v = np.concatenate([t.reshape(8, 16, -1, 4), np.zeros((8, 16, 1, 4), BF)], axis=2)
    return np.ascontiguousarray(np.stack([v[g][:, e[g]] for g in range(8)])).reshape(128, -1)
def gpick(z, e):
    return np.concatenate([z[16 * g:16 * g + 16][:, e[g]] for g in range(8)])
def tile(rs):
    return np.stack(rs, axis=2).reshape(128, -1).astype(BF)
def pick(q, e):
    c = np.concatenate([q[0].reshape(128, -1, 4), np.zeros((128, 1, 4), np.uint8)], axis=1); s = np.concatenate([q[1], np.ones((16, 1), np.uint8)], axis=1)
    return (np.ascontiguousarray(c[:, e].reshape(128, -1)), np.ascontiguousarray(s[:, e]))
def join(*qs):
    return (np.concatenate([q[0] for q in qs], axis=1), np.concatenate([q[1] for q in qs], axis=1))
def put(q, e, v):
    c, s = q[0].reshape(128, -1, 4).copy(), q[1].copy(); c[:, e] = v[0].reshape(128, -1, 4); s[:, e] = v[1]
    return (c.reshape(128, -1), s)
def pk(c, s):
    return (np.ascontiguousarray(c), mx_ref.live(s))
def emit(q):
    return q[0], q[1]
def packed(v, rng):
    q = [mx_ref.quantize(np.ascontiguousarray(v[r])) for r in range(N)]
    return np.stack([a for a, b in q]), np.stack([mx_ref.plane(b, rng) for a, b in q])
def values_of_codes():
    e, c = np.zeros((128, 128, 4), np.float32), np.zeros((128, 2, 4), np.uint8)
    e[np.arange(128), np.arange(128), 0] = 1
    c[:127, :, 0] = np.arange(256).reshape(2, 128).T[:127]
    return mx_ref.matmul(mx_ref.quantize(e.reshape(128, 512).astype(BF)), (c.reshape(128, 8), np.full((16, 2), 127, np.uint8))).T.reshape(-1).astype(np.float64)
CODE_VALUE, SCALE_VALUE = values_of_codes(), 2.0 ** (np.arange(256) - 127.0)
def decode(q):
    return (CODE_VALUE[q[0]].reshape(16, 8, -1, 4) * SCALE_VALUE[q[1]][:, None, :, None] + 0.0).reshape(128, -1).astype(np.float32)
def f(rng, *shape):
    return mx_ref.flush((rng.standard_normal(shape, dtype=np.float32) * np.exp2(rng.integers(-2, 3, shape[:-1] + (1,)))).astype(BF))
def wide(rng, *shape, cols=0):
    v = rng.standard_normal(shape, dtype=np.float32) * np.exp2(rng.integers(-12, 13, shape)).astype(np.float32)
    if cols: v *= np.repeat(np.exp2(rng.integers(-cols, cols + 1, shape[:-2] + (1, shape[-1] // 4))) * (rng.random(shape[:-2] + (1, shape[-1] // 4)) > 0.0625), 4, axis=-1).astype(np.float32)
    return mx_ref.flush(v.astype(BF))
C, L, M, R = 288, 4, 56, 3
def big(v):
    v = v.astype(np.float32)
    v[np.abs(v) < np.float32(2.0 ** -16)] = 0
    return v.astype(BF)
def numbers_of(rng):
    return {"x": big(f(rng, N, 128, 4 * C)), "u": np.array(f(rng, N, 128, 512)), "v": np.array(f(rng, N, 128, 512))}
def some_links(rng):
    w = rng.choice([8, 16, 32, C], (8, 1, 1))
    return (np.arange(C) + 1 + (rng.random((8, 2, C)) * w).astype(np.int64)) % C
def links_of(rng):
    return np.stack([gtable(some_links(rng).reshape(8, 2 * C)) for r in range(N)])
def layers(rng):
    return big(f(rng, N, 128, 2048)).reshape(N, 8, 16, 4, 8, 16, 4)
def weights(rng, w):
    c, p = packed(np.ascontiguousarray(w).reshape(N, 128, 2048), rng)
    return {"wc": c, "ws": p}
def setup_inputs(rng):
    return {**numbers_of(rng), "nb": links_of(rng), **weights(rng, layers(rng))}
def setup_inputs_ties(rng):
    d = numbers_of(rng)
    o = rng.permutation(N)
    k = rng.integers(-1, 3, (N, 8, C))
    k[o[1]] = rng.integers(-3, 0, (8, C))
    k[o[2]] = 1
    x = d["x"].reshape(N, 8, 16, C, 4)
    x[:, :, 0] = 0
    x[:, :, 0, :, 0] = k.astype(np.float32).astype(BF)
    u = d["u"].reshape(N, 128, 128, 4)
    u[:, :, ::16] = 0
    for h in range(0, 128, 16): u[:, h, h, 0] = 1
    u[o[0], :, ::16] = 0
    w = layers(rng)
    w[:, :, :, :, :, 0] = 0
    return {"x": x.reshape(N, 128, 4 * C), "u": u.reshape(N, 128, 512), "v": d["v"], "nb": links_of(rng), **weights(rng, w)}
def setup_inputs_near(rng):
    d = numbers_of(rng)
    x = d["x"].astype(np.float32).reshape(N, 8, 16, C, 4)
    x[:, :, 0] = 0
    x[:, :, 8:] = 0
    s = rng.integers(0, 16, (N, 8, C))
    s = ((s[:, :, :, None] >> np.arange(4)) & 1) * np.exp2(np.arange(4) - 23.0)
    u = d["u"].reshape(N, 128, 128, 4)
    u[:, :, ::16] = 0
    nb = np.stack([some_links(rng) for r in range(N)])
    n = np.arange(C)
    first = n // 3 * 3 % (C - C % 3)
    o = rng.permutation(N) % 4
    for r in range(N):
        k = 1.0 if o[r] == 0 else 2.0 ** -30
        if o[r] < 2:
            x[r, :, 0, :, 0] = rng.choice([-1.0, 1.0], (8, C))
            x[r, :, 11, :, 0] = 2.0 ** -10
            x[r, :, 8] = s[r]
            g, e = rng.integers(8), rng.permutation(C)
            nb[r, g, 0, e], nb[r, g, 1, e] = e[first + (n + 1) % 3], e[first + (n + 2) % 3]
            x[r, g, 0, C - 1, 0] = 1.0
            x[r, g, 8, C - 1] = np.exp2(np.arange(4) - 23.0)
        elif o[r] == 2:
            x[r, :, 8, :, 0] = rng.integers(-1, 3, (8, C)) * 2.0 ** -29
            for g in rng.permutation(8)[:4]: x[r, g, 8, rng.integers(C), 0] = rng.choice([-1.0, 1.0]) * 2.0 ** 29
        else:
            x[r, :, 0, :, 0] = rng.choice([0.0, 0.0, 0.0, 0.0, 0.0, 0.0, 1.0, -1.0], (8, C))
            x[r, :, 8] = s[r] * rng.choice([-1.0, 1.0], (8, C, 1))
        for h in range(0, 128, 16):
            u[r, h, h, 0] = 1.0 if o[r] == 3 else 0.0 if o[r] == 2 else k
            u[r, h + 8, h] = k
            if o[r] < 2: u[r, h + 11, h, 0] = k
    w = layers(rng)
    for i in [0, 8, 9, 10, 11, 12, 13, 14, 15]:
        w[:, :, i] = 0
        w[:, :, :, :, :, i] = 0
    return {"x": x.reshape(N, 128, 4 * C).astype(BF), "u": u.reshape(N, 128, 512), "v": d["v"], "nb": np.stack([gtable(nb[r].reshape(8, 2 * C)) for r in range(N)]), **weights(rng, w)}
def setup_inputs_huge(rng):
    d = numbers_of(rng)
    c = rng.choice([-1.0, 1.0], (N, 1, C, 1))
    c[rng.permutation(N)[:N // 2]] = -1.0
    x = 2.0 ** 30 * (0.6 + 0.2 * rng.random((N, 128, C, 4))) * c
    u = d["u"].reshape(N, 128, 128, 4)
    u[:, :, ::16] = (2.0 ** 30 * (1.0 - 0.1 * rng.random((N, 128, 8, 4)))).astype(np.float32).astype(BF)
    w = np.zeros((N, 128, 4, 128, 4), np.float32)
    i = np.arange(128)
    for b in range(4): w[:, i, b, i, b] = -2
    return {"x": x.astype(np.float32).reshape(N, 128, 4 * C).astype(BF), "u": u.reshape(N, 128, 512), "v": d["v"], "nb": links_of(rng), **weights(rng, w.astype(BF))}
def setup_inputs_forms(rng):
    d = numbers_of(rng)
    x = d["x"].astype(np.float32).reshape(N, 8, 16, C, 4)
    a = (1.0 + (2 * rng.integers(0, 64, (N, 8, 8, C, 4)) + 1) * 2.0 ** -7) * np.exp2(-rng.integers(8, 14, (N, 8, 8, C, 4)).astype(np.float64))
    x[:, :, :8] = a * rng.choice([-1.0, 1.0], a.shape)
    x[:, :, 0, :, 0] = rng.choice([1.875, 1.96875], (N, 8, C))
    x[:, :, 1, :, 0] = rng.integers(8, 10, (N, 8, C)) * rng.choice([-1.0, 1.0], (N, 8, C)) * 2.0 ** -16
    u = d["u"].reshape(N, 128, 128, 4)
    u[:, :, ::16] = 0
    for h in range(0, 128, 16): u[:, h + 1, h, 0] = 1
    nb = np.stack([some_links(rng) for r in range(N)])
    o = rng.permutation(N) % 4
    for r in range(N):
        count = rng.permutation([M, M, M, M - 1, M + 1, 1, 0, C])
        for g in range(8):
            if o[r] == 0: nb[r, g, 1] = nb[r, g, 0]
            if o[r] in (1, 2):
                n = rng.integers(0, 2 * L - 1, C)
                n[:2 * L - 2] = np.arange(1, 2 * L - 1)
                n[2 * L - 2] = 2 * L - 2
                if o[r] == 1: n[L - 2] = 2 * L - 2
                else: n[2 * L - 3] = 0
                m = n.copy()
                e = 2 * L - 1 + np.arange(min(int(count[g]), C - 2 * L + 1))
                if o[r] == 1: n[e] = rng.integers(0, 2, len(e)) * (L - 1)
                else: n[e] = rng.integers(0, 2 * L - 2, len(e))
                m[e] = (n[e] + L - 1) % (2 * L - 2)
                k = rng.permutation(C)
                nb[r, g, 0, k], nb[r, g, 1, k] = k[n], k[m]
    return {"x": x.reshape(N, 128, 4 * C).astype(BF), "u": u.reshape(N, 128, 512), "v": d["v"], "nb": np.stack([gtable(nb[r].reshape(8, 2 * C)) for r in range(N)]), **weights(rng, layers(rng))}
def setup_inputs_spread(rng):
    d = setup_inputs(rng)
    d["x"] = big(wide(rng, N, 128, 4 * C, cols=6))
    return d
def check_inputs(d):
    b = []
    for k in ("x", "u", "v"):
        a = np.abs(d[k].astype(np.float32))
        if not (np.isfinite(a).all() and ((a == 0) | (a >= 2.0 ** -30) & (a <= 2.0 ** 30)).all()): b.append("a value of " + k)
    if not ((d["nb"] >= 0) & (d["nb"] < C)).all(): b.append("an entry of nb")
    none, least, most = [emit(mx_ref.quantize(np.full((128, 16), k, np.float32).astype(BF)))[1][0, 0] for k in (0.0, 2.0 ** -30, 2.0 ** 30)]
    for r in range(N):
        if ((d["wc"][r] == 0x7F) | (d["wc"][r] == 0xFF)).any(): b.append("wc: a code that is no number")
        s = mx_ref.live(d["ws"][r])
        if ((s != none) & ((s < least) | (s > most))).any(): b.append("ws: a scale out of range")
    return b
def bubbles(a, s):
    at = lambda t, e: np.take_along_axis(t, e, axis=1)
    c = np.where(s > 0, a[:, C:], a[:, :C])
    p, q = [a[:, :C]], [a[:, C:]]
    for k in range(1, L):
        p.append(at(c, p[-1]))
        q.append(at(c, q[-1]))
    i, j = np.full((8, C), -1), np.full((8, C), -1)
    for n in reversed(range(2 * L - 1)):
        for k in reversed(range(max(0, n - L + 1), min(n, L - 1) + 1)):
            met = p[k] == q[n - k]
            i[met], j[met] = k, n - k
    is_bubble = (i >= 0) & (p[0] != q[0])
    o = np.lexsort((-s, ~is_bubble))[:, :M]
    filled = at(is_bubble, o)
    g, k = np.arange(8)[:, None, None], np.arange(L)
    np0 = np.stack(p, axis=2)[g, o[:, :, None], np.minimum(k, at(i, o)[:, :, None])]
    nq0 = np.stack(q, axis=2)[g, o[:, :, None], np.minimum(k, at(j, o)[:, :, None])]
    one = at(s, at(q[0], o)) > at(s, at(p[0], o))
    new = a.copy()
    h, m = np.nonzero(filled)
    new[h, (o + C * ~one)[h, m]] = np0[h, m, L - 1]
    slots = [np.where(filled[:, :, None], t, -1).reshape(8, L * M) for t in (np0, nq0, np.where(one[:, :, None], nq0, np0))]
    e = np.full((8, C), -1)
    for n in reversed(range(L * M)):
        h = np.flatnonzero(slots[2][:, n] >= 0)
        e[h, slots[2][h, n]] = n
    return slots[0], slots[1], e, new
def reference(x, u, v, nb, wc, ws):
    qu = [mx_ref.quantize(u[r]) for r in range(N)]
    lay = [pk(wc[r], ws[r]) for r in range(N)]
    now = [x[r] for r in range(N)]
    links = [gentries(nb[r]).astype(np.int64) for r in range(N)]
    for t in range(R):
        own, sent, place = [], [], []
        for r in range(N):
            q = mx_ref.quantize(now[r])
            own.append(decode(q))
            s = mx_ref.matmul(qu[r], q)[::16] + np.float32(0.0)
            a, b, e, links[r] = bubbles(links[r], s)
            place.append(e)
            w = own[r].astype(BF)
            sent.append(mx_ref.quantize(((gcols(w, a).astype(np.float32) + gcols(w, b).astype(np.float32)) * np.float32(0.5)).astype(BF)))
        for r in range(N):
            came, made = sent[(r - 1) % N], []
            for b in range(4):
                h = mx_ref.matmul(pick(lay[r], np.arange(128 * b, 128 * b + 128)), came) * np.float32(0.03125)
                made.append(gpick(np.concatenate([h, np.zeros((128, 1), np.float32)], axis=1), place[r]) + own[r][:, b::4])
            now[r] = tile(made)
    y, ol = np.zeros((N, 128, C), np.float32), np.zeros((N, 8, 2 * C), np.float32)
    oc, osc = np.zeros((N, 128, 4 * C), np.uint8), np.zeros((N, 16, C), np.uint8)
    for r in range(N):
        q = mx_ref.quantize(now[r])
        y[r] = mx_ref.matmul(mx_ref.quantize(v[r]), q)
        ol[r] = links[r]
        oc[r], osc[r] = emit(q)
    return {"y": y, "ol": ol, "oc": oc, "osc": osc}

@@ -1,0 +1,500 @@
+from concourse.mybir import dt, AluOpType, AxisListType, ActivationFunctionType
+
+C, L, M, R = 288, 4, 56, 3
+NS = L * M
+BIG = 4194304.0
+EMPTY = 288 * 513
+TINY = 2.0 ** -119
+
+_BUFS = """xt:1152:b ut:512:b uq:128:c us:128:p urq:384:c urs:384:p vt:512:b vq:128:c vs:128:p wq:512:c wp:512:p
+jt:528:b eq:512:c es:512:p rt:512:b rq:128:c rs:128:p fq:1440:c fs:1440:p zt:896:b fh:1216:b ff:1152:b ga:896:b hs:960 yo:288
+pf:16 ion:304:i j16:288:i iof:304 ioo:288 ioe:288 mask16:352 tri:32:b mask4:64 tabk:304 ci:306 cj:306 sm0:128:i zq:224:c zs:224:p
+iot:18 bk:16 be:18 ul:24:o bcl:36:o li:36:i ll:36:o lf:36 lpk:24 lp:352 lk:18:i lof:576
+cf:64 cl:18:o ordf:8 ordl:4:o abg:128 abi:64:i bn:96:i bnl:16:o t3m:256 ks:224 ea:4032 em:36 el:18:o
+tsb:288 sm:544 ww:1152 pp:1728 ne:306 ij:612 bub:18:b bubf:18 abt0:144 ab5:144 pk:96 q3:800
+p3:24 bc:864 nt:576 abt:352 t3t:352 ak:1152 sg0:1152:b sg1:1152:b sg2:1152:b sg3:1152:b sg4:1152:b xq3:288:c xs3:288:p"""
+for _t in range(R):
+    _BUFS += " xq%d:288:c xs%d:288:p al%d:32:o hq%d:288:c hs_%d:288:p hsl%d:32:o yq%d:288:c ys%d:288:p ysl%d:32:o" % ((_t,) * 9)
+_DT = {"b": "bfloat16", "c": "float8_e4m3fn_x4", "p": "uint8", "i": "int32", "o": "uint16", "f": "float32"}
+SCRATCH = {}
+for _b in _BUFS.split():
+    _p = _b.split(":") + ["f"]
+    SCRATCH[_p[0]] = ("sbuf", [128, int(_p[1])], _DT[_p[2]])
+BANKS = ["bs", "br0", "br1", "bk0", "bf0", "bf1", "bf2", "bf3"]
+for _b in BANKS:
+    SCRATCH[_b] = ("psum", [128, 512], "float32")
+PART = {"tr": ("sm", 288), "s4": ("ww", 0), "w1": ("ww", 288), "w2": ("ww", 576), "w3": ("ww", 864), "p01": ("pp", 0), "pr": ("pp", 576),
+        "tpq": ("pp", 1152), "bc3": ("bc", 576), "key": ("nt", 288), "t3g": ("t3m", 128), "t3q": ("t3m", 192), "mk": ("pf", 8)}
+SEMAPHORES = ["qv", "qs", "qt", "qg", "left", "dx", "du", "dn", "dw", "dp", "dv", "done"] + [p + k + str(t) for p in ("got", "rel") for k in "qsl" for t in range(R)]
+
+SHARE = 2
+VE = (2, 6, 10, 14)
+PAIRS = sorted([(i, j) for i in range(L) for j in range(L) if i + j], key=lambda e: (e[0] + e[1], e[0]))[::-1]
+
+CYC, PICK, ACT, WAKE, TRIP, LOAD = 1.0e-3, 1.5e-3, 0.02, 0.2, (8.0, 8.0, 5.0), 2.2
+
+
+def _relays(core, dst, topo):
+    rel = [c for c in topo.cores_of(core) if c != core and topo.may_write(c, dst) and topo.die(c) == topo.die(core)]
+    return [rel[0], rel[1 % len(rel)], rel[1 % len(rel)]]
+
+
+def _piece(T, kind, k, t):
+    if k == 0:
+        return T["%sq%d" % (kind, t)][:, 0:C].bitcast(dt.uint8)
+    if k == 1:
+        return T[("hs_%d" if kind == "h" else kind + "s%d") % t][:, 0:C]
+    return T[{"x": "al%d", "h": "hsl%d", "y": "ysl%d"}[kind] % t][:, 0:32]
+
+
+def _relay_program(g, core, T, topo):
+    n = 0
+    for r in range(len(T.cores)):
+        src, dst = T.cores[r], T.cores[(r + 1) % len(T.cores)]
+        if topo.may_write(src, dst):
+            continue
+        rel = _relays(src, dst, topo)
+        for t in range(R):
+            for k in range(3):
+                if rel[k] == core:
+                    rid, pid = topo.addr(dst, core)
+                    g.wait_ge(T.sem["rel" + "qsl"[k] + str(t)], len(topo.engines(src, core)))
+                    g.remote_dma(_piece(T, "y", k, t), _piece(T, "h", k, t), T.sem["got" + "qsl"[k] + str(t)], T.sem.left, pid, rid, topo.mask(core, dst))
+                    n += len(topo.engines(core, dst))
+    if n:
+        g.wait_ge(T.sem.left, n)
+
+
+def _order(nodes):
+    users = [[] for n in nodes]
+    for i, n in enumerate(nodes):
+        for d in n["deps"]:
+            users[d].append(i)
+    tail = [0.0] * len(nodes)
+    for i in reversed(range(len(nodes))):
+        tail[i] = nodes[i]["occ"] + nodes[i]["lat"] + max([tail[u] + WAKE for u in users[i]] + [0.0])
+    left = [len(n["deps"]) for n in nodes]
+    ready_at = [0.0] * len(nodes)
+    free, ready, out = {}, {}, []
+    for i, n in enumerate(nodes):
+        if not left[i]:
+            ready.setdefault(n["q"], []).append(i)
+    while any(ready.values()):
+        best = None
+        for q, c in ready.items():
+            if c:
+                at = [max(free.get(q, 0.0), ready_at[i]) for i in c]
+                start = min(at)
+                if best is None or start < best[0]:
+                    near = [i for i, a in zip(c, at) if a <= start + 0.02]
+                    best = (start, q, max(near, key=lambda i: tail[i]))
+        start, q, i = best
+        start = max(start, ready_at[i])
+        ready[q].remove(i)
+        out.append(i)
+        free[q] = start + nodes[i]["occ"]
+        for u in users[i]:
+            ready_at[u] = max(ready_at[u], free[q] + nodes[i]["lat"] + WAKE)
+            left[u] -= 1
+            if not left[u]:
+                ready.setdefault(nodes[u]["q"], []).append(u)
+    return out
+
+
+def rank_program(g, core, T, topo):
+    rank = T.rank_of(core)
+    if rank is None:
+        _relay_program(g, core, T, topo)
+        return
+    A = AluOpType
+    F = ActivationFunctionType
+    queue = {"v": g.vector, "s": g.scalar, "t": g.tensor, "g": g, "y": g.sync}
+    qsem = {"v": "qv", "s": "qs", "t": "qt", "g": "qg"}
+    nodes, log = [], {}
+
+    def call(q, fn, rd, wr, occ=0.06, lat=0.0, sem=None, n=1):
+        i, deps = len(nodes), {}
+        for w, regs in ((0, rd), (1, wr)):
+            for name, lo, hi, st in regs:
+                for a in log.get(name, []):
+                    if a["hi"] <= lo or hi <= a["lo"] or (st > 1 and a["st"] == st and (a["lo"] - lo) % st) or a["i"] == i:
+                        continue
+                    same = a["q"] == q and a["c"]
+                    if w == 0 and not a["w"] and (same or name not in BANKS):
+                        continue
+                    deps[a["i"]] = deps.get(a["i"], False) or not (w == 1 and same and (not a["w"] or q == "t"))
+        for w, regs in ((0, rd), (1, wr)):
+            for name, lo, hi, st in regs:
+                old = log.get(name, [])
+                if w:
+                    old = [a for a in old if not (lo <= a["lo"] and a["hi"] <= hi and (st == 1 or (a["st"] == st and (a["lo"] - lo) % st == 0)))]
+                log[name] = old + [{"lo": lo, "hi": hi, "st": st, "q": q, "c": sem is None, "w": w, "i": i}]
+        nodes.append({"q": q, "fn": fn, "deps": deps, "occ": occ, "lat": lat, "sem": sem, "n": n})
+        return i
+
+    def issue():
+        count, clock, token = {}, {q: {} for q in queue}, {}
+        for i in _order(nodes):
+            e = nodes[i]
+            q = e["q"]
+            if q == "net":
+                token[i] = (e["sem"], e["n"], {})
+                continue
+            need = {}
+            for d, awaited in e["deps"].items():
+                if awaited:
+                    sem, val, seen = token[d]
+                    if sem not in need or need[sem][1] < val:
+                        need[sem] = token[d]
+            for sem, val, seen in sorted(need.values(), key=lambda k: -len(k[2])):
+                if clock[q].get(sem, 0) < val:
+                    queue[q].wait_ge(T.sem[sem], val)
+                    clock[q][sem] = val
+                    for s, n in seen.items():
+                        clock[q][s] = max(clock[q].get(s, 0), n)
+            sem = e["sem"] or qsem[q]
+            if sem == "left":
+                e["fn"]()
+            else:
+                e["fn"]().then_inc(T.sem[sem], e["n"])
+            count[sem] = count.get(sem, 0) + e["n"]
+            token[i] = (sem, count[sem], dict(clock[q]))
+        for s in count:
+            g.wait_ge(T.sem[s], count[s])
+
+    def dma(q, sem, out, in_, rd, wr):
+        call(q, lambda: queue[q].dma_start(out, in_), rd, wr, 0.06, LOAD, sem, 16)
+
+    def r(name, lo, hi, st=1):
+        name, o = PART.get(name, (name, 0))
+        return (name, lo + o, hi + o, st)
+
+    def ap(v):
+        if not isinstance(v, tuple):
+            return v
+        return T[v[0]][:, v[1]:v[2]] if v[3] == 1 else T[v[0]][:, v[1]:v[2]:v[3]]
+
+    def wide(v, per=1.0):
+        return max(64, per * len(range(v[1], v[2], v[3]))) * CYC
+
+    def cost(out, off, per):
+        return 0.05 + PICK * len(range(out[1], out[2], out[3])) if off else wide(out, per)
+
+    def side(in_, off):
+        return ap(in_) if off is None else ap(in_).indirect(ap(off))
+
+    def views(*vs):
+        return [v for v in vs if isinstance(v, tuple)]
+
+    def half(*vs):
+        return 0.5 if all(SCRATCH[v[0]][2] == "bfloat16" for v in vs) else 1.0
+
+    def copy(out, in_, off=None):
+        call("v", lambda: g.vector.tensor_copy(ap(out), side(in_, off)), views(in_, off), [out], cost(out, off, half(out, in_)))
+
+    def tt(out, a, b, op, off=None):
+        call("v", lambda: g.vector.tensor_tensor(ap(out), side(a, off), ap(b), op), views(a, b, off), [out], cost(out, off, 1.0 if a[0] in BANKS else 2.0))
+
+    def ts(out, a, s1, op0, s2=None, op1=None, off=None):
+        if op1 is None:
+            call("v", lambda: g.vector.tensor_scalar(ap(out), side(a, off), ap(s1), None, op0), views(a, s1, off), [out], cost(out, off, half(out, a)))
+        else:
+            call("v", lambda: g.vector.tensor_scalar(ap(out), side(a, off), ap(s1), ap(s2), op0, op1), views(a, s1, s2, off), [out], cost(out, off, half(out, a)))
+
+    def fill(v, c):
+        call("v", lambda: g.vector.memset(ap(v), c), [], [v], wide(v, half(v)))
+
+    def gfill(v, c):
+        giota(v, [[0, len(range(v[1], v[2], v[3]))]], c)
+
+    def giota(v, pattern, base):
+        call("g", lambda: g.iota(ap(v), pattern, base, 0, allow_small_or_imprecise_dtypes=True), [], [v], 0.13 + 2 * wide(v))
+
+    def iota(out, pattern, base, cm):
+        call("g", lambda: g.iota(ap(out), pattern, base, cm), [], [out], 0.13 + 2 * wide(out))
+
+    def turn(out, in_):
+        call("v", lambda: g.vector.transpose(ap(out), ap(in_)), [in_], [out], wide(out))
+
+    def least(out, in_):
+        call("v", lambda: g.vector.tensor_reduce(ap(out), ap(in_), AxisListType.X, A.min, apply_absolute_value=True), [in_], [out], wide(in_))
+
+    def scan(out, d0, d1):
+        call("v", lambda: g.vector.tensor_tensor_scan(ap(out), ap(d0), ap(d1), 0.0, A.mult, A.add), [d0, d1], [out], wide(out))
+
+    def act(out, in_, f, bias=None, scale=None, off=None):
+        kw = {}
+        if bias is not None: kw["bias"] = ap(bias)
+        if scale is not None: kw["scale"] = ap(scale)
+        call("s", lambda: g.scalar.activation(ap(out), side(in_, off), f, **kw), views(in_, bias, scale, off), [out], cost(out, off, 1.0) + (0.0 if off else ACT))
+
+    def quant(qn, sn, lo, hi, in_):
+        call("v", lambda: g.vector.quantize_mx(T[qn][:, lo:hi], T[sn][:, lo:hi], ap(in_)), [in_], [r(qn, lo, hi), r(sn, lo, hi)], 0.012 + 0.00106 * (hi - lo))
+
+    def mm(bank, n, st, sts, slo, mv, mvs, mlo, start=True, stop=True):
+        call("t", lambda: g.tensor.matmul_mx(T[bank][:, 0:n], T[st][:, slo:slo + 128], T[sts][:, slo:slo + 128], T[mv][:, mlo:mlo + n], T[mvs][:, mlo:mlo + n], start, stop),
+             [r(st, slo, slo + 128), r(sts, slo, slo + 128), r(mv, mlo, mlo + n), r(mvs, mlo, mlo + n)], [r(bank, 0, 512)], (n + 16) * CYC)
+
+    dma("y", "du", T.ut[:, :], T.u[:, :], [], [r("ut", 0, 512)])
+    dma("s", "dx", T.xt[:, :], T.x[:, :], [], [r("xt", 0, 4 * C)])
+    dma("y", "dn", T.li[:, :], T.nb[:, :], [], [r("li", 0, 36)])
+    dma("s", "dw", T.wq[:, :].bitcast(dt.uint8), T.wc[:, :], [], [r("wq", 0, 512)])
+    dma("y", "dp", T.wp[:, :], T.ws[:, :], [], [r("wp", 0, 512)])
+    dma("y", "dv", T.vt[:, :], T.v[:, :], [], [r("vt", 0, 512)])
+
+    iota(r("sm0", 120, 121), [[0, 1]], 0, 1)
+    iota(r("sm0", 0, 8), [[16, 8]], 0, 0)
+    iota(r("sm0", 8, 16), [[32, 4], [0, 2]], 0, 0)
+    iota(r("sm0", 16, 24), [[32, 4], [0, 2]], 16, 0)
+    iota(r("ion", 0, 304), [[1, 304]], 0, 0)
+    giota(r("iof", 0, 304), [[1, 304]], 0)
+    iota(r("sm0", 24, 42), [[32, 9], [0, 2]], 0, 0)
+    iota(r("sm0", 42, 60), [[1, 18]], 0, 0)
+    iota(r("sm0", 60, 78), [[1, 18]], 24, 0)
+    iota(r("sm0", 80, 84), [[16, 4]], 0, 0)
+    iota(r("sm0", 84, 102), [[16, 18]], 0, 0)
+    copy(r("ul", 0, 24), r("sm0", 0, 24))
+    ts(r("sm0", 121, 122), r("sm0", 120, 121), 15, A.bitwise_and)
+    ts(r("sm0", 122, 123), r("sm0", 120, 121), 2, A.logical_shift_right, 3, A.bitwise_and)
+    ts(r("sm0", 123, 124), r("sm0", 120, 121), 3, A.bitwise_and)
+    ts(r("sm0", 124, 125), r("sm0", 120, 121), 31, A.bitwise_and)
+    ts(r("sm0", 125, 126), r("sm0", 120, 121), 1, A.bitwise_and)
+    copy(r("pf", 0, 5), r("sm0", 121, 126))
+    Q, QQ, ROLE, I32, ODD = [r("pf", k, k + 1) for k in range(5)]
+    ALL4, MO, ME, M01, M23, M4 = [r("mk", k, k + 1) for k in range(6)]
+    quant("uq", "us", 0, 128, r("ut", 0, 512))
+    call("v", lambda: g.vector.tensor_copy(T.urq[:, 0:384].bitcast(dt.uint32), T.uq[:, 0:128].bitcast(dt.uint32).indirect(T.ul[:, 0:24])), [r("uq", 0, 128), r("ul", 0, 24)], [r("urq", 0, 384)], 0.6)
+    call("s", lambda: g.scalar.activation(T.urs[:, 0:384], T.us[:, 0:128].indirect(T.ul[:, 0:24]), F.Copy), [r("us", 0, 128), r("ul", 0, 24)], [r("urs", 0, 384)], 0.6)
+    ts(r("j16", 0, C), r("ion", 0, C), 15, A.bitwise_and)
+    ts(r("mask16", 0, C), r("j16", 0, C), Q, A.is_equal)
+    ts(ALL4, Q, 3.5, A.is_le)
+    tt(MO, ALL4, ODD, A.mult)
+    tt(ME, ALL4, MO, A.subtract)
+    ts(M01, Q, 1.5, A.is_le)
+    tt(M23, ALL4, M01, A.subtract)
+    ts(M4, Q, 4.0, A.is_equal)
+    act(r("ioo", 0, C), r("iof", 0, C), F.Copy, None, MO)
+    act(r("ioe", 0, C), r("iof", 0, C), F.Copy, None, ME)
+    copy(r("lf", 0, 18), r("li", 0, 18))
+    tt(r("lf", 18, 36), r("li", 18, 36), r("li", 0, 18), A.subtract)
+    copy(r("ll", 0, 36), r("li", 0, 36))
+    ts(r("tri", 0, 32), r("iof", 0, 32), I32, A.is_gt, 0.5, A.subtract)
+    ts(r("tri", 0, 32), r("tri", 0, 32), TINY, A.mult)
+    fill(r("ne", 0, 306), 0.0)
+    for name, w in (("ci", 0), ("cj", 1)):
+        v = [-1] + [e[w] for e in PAIRS] + [-1, 0]
+        c = [v[t] - v[t + 1] for t in range(17)]
+        usual = max(sorted(set(c)), key=c.count)
+        fill(r(name, 0, 306), float(usual))
+        for t in range(17):
+            if c[t] != usual:
+                fill(r(name, t, 306, 17), float(c[t]))
+    gfill(r("jt", 0, 528), 1)
+    call("g", lambda: g.affine_select(T.jt[:, 0:520], T.jt[:, 0:520], [[-1, 520]], A.is_equal, 0.0, 3, 4), [r("jt", 0, 520)], [r("jt", 0, 520)], 1.2)
+    for b in range(4):
+        quant("eq", "es", 128 * b, 128 * b + 128, r("jt", 3 - b, 515 - b))
+        gfill(r("fh", 304 * b + C, 304 * b + 304), 0)
+    gfill(r("rt", 0, 512), 0)
+    for a in range(4):
+        for h in range(2):
+            lo = 128 * a + 64 * h
+            call("s", lambda v=T.rt[32 * a:32 * a + 32, lo + h:lo + 64:2]: g.scalar.activation(v, v, F.Identity, bias=1024.0), [r("rt", lo, lo + 64)], [r("rt", lo, lo + 64)])
+    quant("rq", "rs", 0, 128, r("rt", 0, 512))
+    gfill(r("sg4", 2, 4 * C, 4), 0)
+    gfill(r("sg4", 3, 4 * C, 4), 0)
+    gfill(r("pk", 0, 96), 0)
+    ts(r("iot", 0, 18), r("sm0", 24, 42), I32, A.add)
+    copy(r("bcl", 0, 18), r("sm0", 42, 60))
+    ts(r("cf", 54, 55), ROLE, 18.0, A.mult)
+    ts(r("sm0", 102, 120), r("sm0", 60, 78), r("cf", 54, 55), A.add)
+    copy(r("bcl", 18, 36), r("sm0", 102, 120))
+    ts(r("bk", 4, 8), r("sm0", 80, 84), Q, A.add)
+    ts(r("bk", 8, 12), r("bk", 4, 8), 288.0, A.add)
+    ts(r("bk", 0, 4), r("bk", 4, 8), float(M), A.is_ge, -1.0e7, A.mult)
+    ts(r("bk", 4, 8), r("bk", 4, 8), -1024.0, A.mult)
+    tt(r("bk", 0, 4), r("bk", 0, 4), r("bk", 4, 8), A.add)
+    ts(r("abi", 0, 64), r("ion", 0, 64), 3, A.bitwise_and)
+    ts(r("mask4", 0, 64), r("abi", 0, 64), QQ, A.is_equal)
+    gfill(r("abt", C, 352), EMPTY)
+    gfill(r("p3", 0, 24), 0)
+    ts(r("be", 0, 18), r("sm0", 84, 102), Q, A.add, -1024.0, A.mult)
+    act(r("tabk", 0, 304), r("iof", 0, 304), F.Copy, None, 1024.0)
+    gfill(r("t3t", C, 352), 0)
+    for b in range(4):
+        gfill(r("hs", 240 * b + NS, 240 * b + 240), 0)
+    gfill(r("lp", C, 352), 0)
+    gfill(r("mask16", C, 352), 0)
+    gfill(r("lpk", 18, 24), 0)
+    ts(r("cf", 0, 18), r("li", 18, 36), 512.0, A.mult)
+    tt(r("lpk", 0, 18), r("cf", 0, 18), r("li", 0, 18), A.add)
+    tt(r("lp", 0, C), r("lpk", 0, 24), r("mask16", 0, C), A.mult, r("bcl", 0, 18))
+    quant("vq", "vs", 0, 128, r("vt", 0, 512))
+
+    n_of = len(T.cores)
+    dst, src = T.cores[(rank + 1) % n_of], T.cores[(rank - 1) % n_of]
+    direct = topo.may_write(core, dst)
+    hops = [dst] * 3 if direct else _relays(core, dst, topo)
+    came = [src] * 3 if topo.may_write(src, core) else _relays(src, core, topo)
+
+    def evens(out, buf, lo, n):
+        tt(out, r(buf, lo, lo + n, 2), r(buf, lo + 1, lo + n, 2), A.add)
+
+    def squeeze(buf, out):
+        evens(r("tr", 0, 144), buf, 0, 288)
+        evens(r("tr", 144, 216), "tr", 0, 144)
+        evens(r("tr", 216, 252), "tr", 144, 72)
+        evens(out, "tr", 216, 36)
+
+    def send(k, t):
+        rid, pid = topo.addr(hops[k], core)
+        name, n = (("xq%d", C), ("xs%d", C), ("al%d", 32))[k]
+        i = call("g", lambda: g.remote_dma(_piece(T, "y" if direct else "h", k, t), _piece(T, "x", k, t), T.sem[("got" if direct else "rel") + "qsl"[k] + str(t)], T.sem.left, pid, rid, topo.mask(core, hops[k])),
+                 [r(name % t, 0, n)], [], 0.5, 0.0, "left", len(topo.engines(core, hops[k])))
+        far = call("net", None, [], [r(("yq%d", "ys%d", "ysl%d")[k] % t, 0, n)], 0.0, TRIP[k], "got" + "qsl"[k] + str(t), len(topo.engines(came[k], core)))
+        nodes[far]["deps"][i] = True
+
+    for t in range(R):
+        XQ, XS = "xq%d" % t, "xs%d" % t
+        quant(XQ, XS, 0, C, r("xt", 0, 4 * C))
+        for k in range(2):
+            send(k, t)
+        mm("bs", C, "urq", "urs", 0, XQ, XS, 0)
+        mm("br0", C, "urq", "urs", 128, XQ, XS, 0)
+        mm("br1", C, "urq", "urs", 256, XQ, XS, 0)
+        for b in range(4):
+            mm("bf%d" % b, C, "eq", "es", 128 * b, XQ, XS, 0)
+            act(r("ff", C * b, C * b + C), r("bf%d" % b, 0, C), F.Copy)
+        turn(r("tsb", 0, C), r("bs", 0, C))
+        tt(r("sm", 0, C), r("bs", 0, C), r("mask16", 0, C), A.mult)
+        act(r("s4", 0, C), r("bs", 0, C), F.Copy, None, M4)
+        for s in range(18):
+            act(r("sg%d" % (s // 4), s % 4, 4 * C, 4), r("br%d" % (s % 2), 0, C), F.Sign, r("tsb", 16 * s, 16 * s + 1), -1.0)
+        for s in range(18):
+            lo = 128 * (s // 2) + s % 4
+            v = r("sg%d" % (s // 4), lo, min(lo + 128, 4 * C), 4)
+            tt(v, v, r("tri", 0, 32), A.add)
+        squeeze("sm", r("cf", 0, 18))
+        ts(r("cf", 18, 36), r("cf", 0, 18), 0.0, A.is_gt)
+        tt(r("cf", 18, 36), r("cf", 18, 36), r("lf", 18, 36), A.mult)
+        tt(r("cf", 36, 54), r("cf", 18, 36), r("lf", 0, 18), A.add)
+        copy(r("cl", 0, 18), r("cf", 36, 54))
+        CL = r("cl", 0, 18)
+        tt(r("w1", 0, C), r("ioo", 0, C), r("ioe", 0, C), A.add, CL)
+        ts(r("w2", 0, C), r("w1", 0, C), M23, A.mult, off=CL)
+        act(r("p01", 0, 2 * C), r("w1", 0, C), F.Copy, None, M01, r("ll", 0, 36))
+        tt(r("w3", 0, C), r("w2", 0, C), r("s4", 0, C), A.add, CL)
+        tt(r("pr", 0, 2 * C), r("w3", 0, C), r("p01", 0, 2 * C), A.add, r("ll", 0, 36))
+        turn(r("tpq", 0, 2 * C), r("pr", 0, 2 * C))
+        for k, (i, j) in enumerate(PAIRS + [(0, 0)]):
+            tt(r("ne", k + 1, 306, 17), r("tpq", i, C, 16), r("tpq", C + j, 2 * C, 16), A.not_equal)
+        scan(r("ij", 0, 306), r("ne", 0, 306), r("ci", 0, 306))
+        scan(r("ij", 306, 612), r("ne", 0, 306), r("cj", 0, 306))
+        I, IJ = r("ij", 16, 306, 17), r("ij", 16, 612, 17)
+        ts(r("bub", 0, 18), I, 0.0, A.is_ge)
+        ts(r("bubf", 0, 18), I, 0.0, A.is_ge)
+        ts(r("q3", 780, 798), I, 0.0, A.is_lt, BIG, A.mult)
+        tt(r("pk", 0, 18), r("q3", 780, 798), r("iot", 0, 18), A.add)
+        for k in range(5):
+            for s in range(4 * k, min(4 * k + 4, 18)):
+                for lo, hi, op in ((0, 32 * (s // 2), A.is_gt), (32 * (s // 2), C, A.is_ge)):
+                    if lo < hi:
+                        v = r("sg%d" % k, 4 * lo + s % 4, 4 * hi, 4)
+                        if lo == 0 and s // 2 >= SHARE:
+                            act(v, v, F.Relu, None, r("bubf", s, s + 1))
+                        else:
+                            ts(v, v, 0.0, op, r("bub", s, s + 1), A.mult)
+            quant("fq", "fs", C * k, C * k + C, r("sg%d" % k, 0, 4 * C))
+            mm("bk0", C, "rq", "rs", 0, "fq", "fs", C * k, k == 0, k == 4)
+        PQ = [r("tpq", k, 2 * C, 16) for k in range(L)]
+        AB = [r("abt0", 36 * k, 36 * k + 36) for k in range(L)]
+        copy(AB[0], PQ[0])
+        for k in range(1, L):
+            o = 108 * k - 108
+            ts(r("q3", o, o + 36), IJ, float(k), A.is_ge)
+            tt(r("q3", o + 36, o + 72), PQ[k], AB[k - 1], A.subtract)
+            tt(r("q3", o + 72, o + 108), r("q3", o + 36, o + 72), r("q3", o, o + 36), A.mult)
+            tt(AB[k], AB[k - 1], r("q3", o + 72, o + 108), A.add)
+        ts(r("ab5", 0, 144), r("abt0", 0, 144), 512.0, A.mult)
+        for k in range(L):
+            tt(r("pk", 24 + 18 * k, 42 + 18 * k), r("ab5", 36 * k + 18, 36 * k + 36), r("abt0", 36 * k, 36 * k + 18), A.add)
+        act(r("bc", 0, 2 * C), r("pk", 0, 96), F.Copy, off=r("bcl", 0, 36))
+        turn(r("nt", 0, C), r("bc", 0, C))
+        turn(r("abt", 0, C), r("bc", C, 2 * C))
+        tt(r("key", 0, C), r("bk0", 0, C), r("nt", 0, C), A.add)
+        for c in range(4):
+            act(r("ak", C * c, C * c + C), r("key", 0, C), F.Abs, r("bk", c, c + 1))
+            least(r("ordf", c, c + 1), r("ak", C * c, C * c + C))
+        tt(r("ordf", 4, 8), r("ordf", 0, 4), r("bk", 8, 12), A.min)
+        copy(r("ordl", 0, 4), r("ordf", 4, 8))
+        ORD = r("ordl", 0, 4)
+        tt(r("abg", 0, 64), r("abt", 0, 352), r("mask4", 0, 64), A.mult, ORD)
+        evens(r("abg", 64, 96), "abg", 0, 64)
+        evens(r("abi", 0, 16), "abg", 64, 32)
+        ts(r("abi", 16, 32), r("abi", 0, 16), 511, A.bitwise_and)
+        ts(r("abi", 32, 48), r("abi", 0, 16), 9, A.logical_shift_right)
+        copy(r("al%d" % t, 0, 32), r("abi", 16, 48))
+        send(2, t)
+        o = 324
+        tt(r("q3", o, o + 36), AB[3], PQ[0], A.subtract)
+        ts(r("q3", o + 36, o + 54), r("q3", o + 18, o + 36), 512.0, A.mult)
+        tt(r("q3", o + 54, o + 72), r("q3", o, o + 18), r("q3", o + 36, o + 54), A.subtract)
+        tt(r("q3", o + 72, o + 90), r("tpq", C + 4, 2 * C, 16), r("tpq", 4, C, 16), A.is_gt)
+        tt(r("q3", o + 90, o + 108), r("q3", o + 72, o + 90), r("q3", o + 54, o + 72), A.mult)
+        tt(r("q3", o + 108, o + 126), r("ab5", 108, 126), r("tpq", 0, C, 16), A.add)
+        tt(r("q3", o + 126, o + 144), r("q3", o + 108, o + 126), r("q3", o + 90, o + 108), A.add)
+        ts(r("q3", o + 144, o + 162), r("q3", o + 72, o + 90), 262144.0, A.mult)
+        tt(r("p3", 0, 18), r("q3", o + 126, o + 144), r("q3", o + 144, o + 162), A.add)
+        act(r("bc3", 0, C), r("p3", 0, 24), F.Copy, off=r("bcl", 0, 18))
+        turn(r("t3t", 0, C), r("bc3", 0, C))
+        copy(r("t3g", 0, 64), r("t3t", 0, 352), ORD)
+        tt(r("t3m", 0, 64), r("t3t", 0, 352), r("mask4", 0, 64), A.mult, ORD)
+        evens(r("t3m", 64, 96), "t3m", 0, 64)
+        evens(r("bn", 0, 16), "t3m", 64, 32)
+        ts(r("bn", 16, 32), r("bn", 0, 16), 18, A.logical_shift_right)
+        tt(r("bn", 32, 48), r("abi", 32, 48), r("abi", 16, 32), A.subtract)
+        tt(r("bn", 48, 64), r("bn", 32, 48), r("bn", 16, 32), A.mult)
+        tt(r("bn", 64, 80), r("bn", 48, 64), r("abi", 16, 32), A.add)
+        copy(r("bnl", 0, 16), r("bn", 64, 80))
+        tt(r("ks", 0, NS), r("tabk", 0, 304), r("iof", 0, NS), A.add, r("bnl", 0, 14))
+        for k in range(18):
+            if k in VE:
+                ts(r("ea", NS * k, NS * k + NS), r("ks", 0, NS), r("be", k, k + 1), A.add)
+            else:
+                act(r("ea", NS * k, NS * k + NS), r("ks", 0, NS), F.Abs, r("be", k, k + 1))
+            least(r("em", k, k + 1), r("ea", NS * k, NS * k + NS))
+        ts(r("em", 18, 36), r("em", 0, 18), float(NS), A.min)
+        copy(r("el", 0, 18), r("em", 18, 36))
+        tt(r("t3q", 0, 64), r("mask16", 0, 352), r("t3g", 0, 64), A.mult, ORD)
+        W = r("t3q", 0, 64)
+        call("v", lambda W=W: g.vector.tensor_copy(T.lp[:, 0:352].indirect(T.ordl[:, 0:4]), ap(W)), [W, ORD], [r("lp", 0, 352)], 0.25)
+        squeeze("lp", r("lk", 0, 18))
+        ts(r("li", 0, 18), r("lk", 0, 18), 511, A.bitwise_and)
+        ts(r("li", 18, 36), r("lk", 0, 18), 9, A.logical_shift_right, 511, A.bitwise_and)
+        copy(r("ll", 0, 36), r("li", 0, 36))
+        if t < R - 1:
+            copy(r("lf", 0, 18), r("li", 0, 18))
+            tt(r("lf", 18, 36), r("li", 18, 36), r("li", 0, 18), A.subtract)
+        else:
+            act(r("lof", 0, 2 * C), r("iof", 0, 304), F.Copy, off=r("ll", 0, 36))
+            dma("y", "done", T.ol[:, :], T.lof[0:128:16, :], [r("lof", 0, 2 * C)], [])
+        for b in range(4):
+            mm("bf%d" % b, C, "eq", "es", 128 * b, "yq%d" % t, "ys%d" % t, 0)
+            act(r("fh", 304 * b, 304 * b + C), r("bf%d" % b, 0, C), F.Copy, None, 0.5)
+        for b in range(4):
+            H = r("fh", 304 * b, 304 * b + 304)
+            act(r("ga", NS * b, NS * b + NS), H, F.Copy, off=r("ysl%d" % t, 0, 14))
+            tt(r("zt", b, 4 * NS, 4), H, r("ga", NS * b, NS * b + NS), A.add, r("ysl%d" % t, 16, 30))
+        quant("zq", "zs", 0, NS, r("zt", 0, 4 * NS))
+        for b in range(4):
+            mm(BANKS[b], NS, "wq", "wp", 128 * b, "zq", "zs", 0)
+            act(r("hs", 240 * b, 240 * b + NS), r(BANKS[b], 0, NS), F.Copy, None, 0.03125)
+            tt(r("xt", b, 4 * C, 4), r("hs", 240 * b, 240 * b + 240), r("ff", C * b, C * b + C), A.add, r("el", 0, 18))
+
+    quant("xq3", "xs3", 0, C, r("xt", 0, 4 * C))
+    mm("bs", C, "vq", "vs", 0, "xq3", "xs3", 0)
+    act(r("yo", 0, C), r("bs", 0, C), F.Copy)
+    dma("y", "done", T.oc[:, :], T.xq3[:, 0:C].bitcast(dt.uint8), [r("xq3", 0, C)], [])
+    for k in range(4):
+        dma("ys"[k % 2], "done", T.osc[4 * k:4 * k + 4, :], T.xs3[32 * k:32 * k + 4, 0:C], [r("xs3", 0, C)], [])
+    dma("s", "done", T.y[:, :], T.yo[:, :], [r("yo", 0, C)], [])
+    issue()

@@ -2,17 +2,16 @@ from concourse.mybir import dt, AluOpType, AxisListType, ActivationFunctionType
 
 C, L, M, R = 288, 4, 56, 3
 NS = L * M
-BIG = 4194304.0
-EMPTY = 288 * 513
-TINY = 2.0 ** -119
+NZ = 256
+FLAG = 1024.0
 
-_BUFS = """xt:1152:b ut:512:b uq:128:c us:128:p urq:384:c urs:384:p vt:512:b vq:128:c vs:128:p wq:512:c wp:512:p
-jt:528:b eq:512:c es:512:p rt:512:b rq:128:c rs:128:p fq:1440:c fs:1440:p zt:896:b fh:1216:b ff:1152:b ga:896:b hs:960 yo:288
-pf:16 ion:304:i j16:288:i iof:304 ioo:288 ioe:288 mask16:352 tri:32:b mask4:64 tabk:304 ci:306 cj:306 sm0:128:i zq:224:c zs:224:p
-iot:18 bk:16 be:18 ul:24:o bcl:36:o li:36:i ll:36:o lf:36 lpk:24 lp:352 lk:18:i lof:576
-cf:64 cl:18:o ordf:8 ordl:4:o abg:128 abi:64:i bn:96:i bnl:16:o t3m:256 ks:224 ea:4032 em:36 el:18:o
-tsb:288 sm:544 ww:1152 pp:1728 ne:306 ij:612 bub:18:b bubf:18 abt0:144 ab5:144 pk:96 q3:800
-p3:24 bc:864 nt:576 abt:352 t3t:352 ak:1152 sg0:1152:b sg1:1152:b sg2:1152:b sg3:1152:b sg4:1152:b xq3:288:c xs3:288:p"""
+_BUFS = """xt:1152:b ut:512:b uq:128:c us:128:p urq:128:c urs:128:p vt:512:b vq:128:c vs:128:p wq:512:c wp:512:p
+jt:528:b eq:512:c es:512:p rt:1024:b rq:256:c rs:256:p fq:960:c fs:960:p zt:1024:b fh:1216:b ff:1152:b ga:1024:b hs:1088 yo:288
+zq:256:c zs:256:p xq3:288:c xs3:288:p sg:3840:b junk:2464:b jc:1440:b
+pi:16:i pf:32 iof:304 iob:304:b j16:288:b mask16:288:b keep:288:b ci:288:b cj:288:b io:1152 ki:160:i kf:160 ko:160:o li:36:i
+ll:36:o lf:36 fa:36 fb:36 fc:36 cl:18:o sm:288 so:288 sr:288 sb:288 ww:864 pq:576 tpq:576 ne:288:b ij:576:b q3:400 mt:288 tb:288
+tr:288 st:304 fl:288:b cn:288:b acc:16 ordl:16:o gt:128 tg:128 rsum:36 sm2:288 po:288 pos:32 pl:18:o ab:128 bnl:16:o bnr:256:b
+bns:224:b dl:224:b ea:4032:b eo:4032:b el:18:o em:18 dk:108 tk:96 lof:576"""
 for _t in range(R):
     _BUFS += " xq%d:288:c xs%d:288:p al%d:32:o hq%d:288:c hs_%d:288:p hsl%d:32:o yq%d:288:c ys%d:288:p ysl%d:32:o" % ((_t,) * 9)
 _DT = {"b": "bfloat16", "c": "float8_e4m3fn_x4", "p": "uint8", "i": "int32", "o": "uint16", "f": "float32"}
@@ -20,18 +19,20 @@ SCRATCH = {}
 for _b in _BUFS.split():
     _p = _b.split(":") + ["f"]
     SCRATCH[_p[0]] = ("sbuf", [128, int(_p[1])], _DT[_p[2]])
-BANKS = ["bs", "br0", "br1", "bk0", "bf0", "bf1", "bf2", "bf3"]
+BANKS = ["bv", "bs", "bk", "bx", "bf0", "bf1", "bf2", "bf3"]
 for _b in BANKS:
     SCRATCH[_b] = ("psum", [128, 512], "float32")
-PART = {"tr": ("sm", 288), "s4": ("ww", 0), "w1": ("ww", 288), "w2": ("ww", 576), "w3": ("ww", 864), "p01": ("pp", 0), "pr": ("pp", 576),
-        "tpq": ("pp", 1152), "bc3": ("bc", 576), "key": ("nt", 288), "t3g": ("t3m", 128), "t3q": ("t3m", 192), "mk": ("pf", 8)}
-SEMAPHORES = ["qv", "qs", "qt", "qg", "left", "dx", "du", "dn", "dw", "dp", "dv", "done"] + [p + k + str(t) for p in ("got", "rel") for k in "qsl" for t in range(R)]
+PART = {"w1": ("ww", 0), "w2": ("ww", 288), "w3": ("ww", 576)}
+SEMAPHORES = (["qv", "qs", "qt", "qg", "left", "dx", "du", "dn", "dw", "dp", "dv", "done"]
+              + [p + k + str(t) for p in ("got", "rel") for k in "qsl" for t in range(R)] + ["d" + k + str(t) for k in "abc" for t in range(R)])
 
-SHARE = 2
-VE = (2, 6, 10, 14)
+VC = (9, 10, 11)
+VE = (1, 3, 5, 7, 9, 11, 13, 15)
 PAIRS = sorted([(i, j) for i in range(L) for j in range(L) if i + j], key=lambda e: (e[0] + e[1], e[0]))[::-1]
+ROW = 7
+TILES = [(0, 288, (17, 16)), (288, 240, (15, 14, 13, 12)), (528, 176, (11, 10, 9, 8)), (704, 128, (7, 6, 5, 4)), (832, 128, (3, 2, 1))]
 
-CYC, PICK, ACT, WAKE, TRIP, LOAD = 1.0e-3, 1.5e-3, 0.02, 0.2, (8.0, 8.0, 5.0), 2.2
+CYC, PICK, SCAT, ACT, WAKE, TRIP, LOAD = 1.0e-3, 1.5e-3, 3.5e-3, 0.02, 0.2, (8.0, 8.0, 4.5), 2.2
 
 
 def _relays(core, dst, topo):
@@ -207,33 +208,38 @@ def rank_program(g, core, T, topo):
     def gfill(v, c):
         giota(v, [[0, len(range(v[1], v[2], v[3]))]], c)
 
-    def giota(v, pattern, base):
-        call("g", lambda: g.iota(ap(v), pattern, base, 0, allow_small_or_imprecise_dtypes=True), [], [v], 0.13 + 2 * wide(v))
+    def giota(v, pattern, base, cm=0):
+        call("g", lambda: g.iota(ap(v), pattern, base, cm, allow_small_or_imprecise_dtypes=True), [], [v], 0.13 + 2 * CYC * len(range(v[1], v[2], v[3])))
 
     def iota(out, pattern, base, cm):
-        call("g", lambda: g.iota(ap(out), pattern, base, cm), [], [out], 0.13 + 2 * wide(out))
+        call("g", lambda: g.iota(ap(out), pattern, base, cm), [], [out], 0.13 + 2 * CYC * len(range(out[1], out[2], out[3])))
+
+    def select(v, pattern, op, base, cm):
+        call("g", lambda: g.affine_select(ap(v), ap(v), pattern, op, 0.0, base, cm), [v], [v], 0.17 + 2 * CYC * len(range(v[1], v[2], v[3])))
 
     def turn(out, in_):
         call("v", lambda: g.vector.transpose(ap(out), ap(in_)), [in_], [out], wide(out))
 
-    def least(out, in_):
-        call("v", lambda: g.vector.tensor_reduce(ap(out), ap(in_), AxisListType.X, A.min, apply_absolute_value=True), [in_], [out], wide(in_))
+    def total(out, in_):
+        call("v", lambda: g.vector.tensor_reduce(ap(out), ap(in_), AxisListType.X, A.add), [in_], [out], wide(in_))
 
-    def scan(out, d0, d1):
-        call("v", lambda: g.vector.tensor_tensor_scan(ap(out), ap(d0), ap(d1), 0.0, A.mult, A.add), [d0, d1], [out], wide(out))
+    def scan(out, d0, d1, first=0.0, op0=A.mult, op1=A.add):
+        call("v", lambda: g.vector.tensor_tensor_scan(ap(out), ap(d0), ap(d1), first, op0, op1), [d0, d1], [out], wide(out, half(out, d0, d1)))
 
-    def act(out, in_, f, bias=None, scale=None, off=None):
+    def act(out, in_, f, bias=None, scale=None, off=None, acc=None):
         kw = {}
         if bias is not None: kw["bias"] = ap(bias)
         if scale is not None: kw["scale"] = ap(scale)
-        call("s", lambda: g.scalar.activation(ap(out), side(in_, off), f, **kw), views(in_, bias, scale, off), [out], cost(out, off, 1.0) + (0.0 if off else ACT))
+        if acc is not None: kw["accum_out"] = ap(acc)
+        call("s", lambda: g.scalar.activation(ap(out), side(in_, off), f, **kw), views(in_, bias, scale, off), views(out, acc),
+             cost(out, off, 1.0) + (0.0 if off else ACT) + (ACT if acc else 0.0))
 
     def quant(qn, sn, lo, hi, in_):
         call("v", lambda: g.vector.quantize_mx(T[qn][:, lo:hi], T[sn][:, lo:hi], ap(in_)), [in_], [r(qn, lo, hi), r(sn, lo, hi)], 0.012 + 0.00106 * (hi - lo))
 
     def mm(bank, n, st, sts, slo, mv, mvs, mlo, start=True, stop=True):
         call("t", lambda: g.tensor.matmul_mx(T[bank][:, 0:n], T[st][:, slo:slo + 128], T[sts][:, slo:slo + 128], T[mv][:, mlo:mlo + n], T[mvs][:, mlo:mlo + n], start, stop),
-             [r(st, slo, slo + 128), r(sts, slo, slo + 128), r(mv, mlo, mlo + n), r(mvs, mlo, mlo + n)], [r(bank, 0, 512)], (n + 16) * CYC)
+             [r(st, slo, slo + 128), r(sts, slo, slo + 128), r(mv, mlo, mlo + n), r(mvs, mlo, mlo + n)], [r(bank, 0, 512)], (n + 16) * CYC * 0.6)
 
     dma("y", "du", T.ut[:, :], T.u[:, :], [], [r("ut", 0, 512)])
     dma("s", "dx", T.xt[:, :], T.x[:, :], [], [r("xt", 0, 4 * C)])
@@ -242,92 +248,100 @@ def rank_program(g, core, T, topo):
     dma("y", "dp", T.wp[:, :], T.ws[:, :], [], [r("wp", 0, 512)])
     dma("y", "dv", T.vt[:, :], T.v[:, :], [], [r("vt", 0, 512)])
 
-    iota(r("sm0", 120, 121), [[0, 1]], 0, 1)
-    iota(r("sm0", 0, 8), [[16, 8]], 0, 0)
-    iota(r("sm0", 8, 16), [[32, 4], [0, 2]], 0, 0)
-    iota(r("sm0", 16, 24), [[32, 4], [0, 2]], 16, 0)
-    iota(r("ion", 0, 304), [[1, 304]], 0, 0)
-    giota(r("iof", 0, 304), [[1, 304]], 0)
-    iota(r("sm0", 24, 42), [[32, 9], [0, 2]], 0, 0)
-    iota(r("sm0", 42, 60), [[1, 18]], 0, 0)
-    iota(r("sm0", 60, 78), [[1, 18]], 24, 0)
-    iota(r("sm0", 80, 84), [[16, 4]], 0, 0)
-    iota(r("sm0", 84, 102), [[16, 18]], 0, 0)
-    copy(r("ul", 0, 24), r("sm0", 0, 24))
-    ts(r("sm0", 121, 122), r("sm0", 120, 121), 15, A.bitwise_and)
-    ts(r("sm0", 122, 123), r("sm0", 120, 121), 2, A.logical_shift_right, 3, A.bitwise_and)
-    ts(r("sm0", 123, 124), r("sm0", 120, 121), 3, A.bitwise_and)
-    ts(r("sm0", 124, 125), r("sm0", 120, 121), 31, A.bitwise_and)
-    ts(r("sm0", 125, 126), r("sm0", 120, 121), 1, A.bitwise_and)
-    copy(r("pf", 0, 5), r("sm0", 121, 126))
-    Q, QQ, ROLE, I32, ODD = [r("pf", k, k + 1) for k in range(5)]
-    ALL4, MO, ME, M01, M23, M4 = [r("mk", k, k + 1) for k in range(6)]
+    iota(r("pi", 0, 1), [[0, 1]], 0, 1)
+    for k, (sh, mask) in enumerate(((0, 15), (0, 16), (4, 7), (0, 3), (2, 3), (0, 1), (4, 1), (1, 7))):
+        ts(r("pi", 1 + k, 2 + k), r("pi", 0, 1), sh, A.logical_shift_right, mask, A.bitwise_and)
+    copy(r("pf", 0, 8), r("pi", 1, 9))
+    Q, H16, GRP, QL, QH, ODD, H, QHALF = [r("pf", k, k + 1) for k in range(8)]
+    PW, RI, SEL, T1, T2, THR = [r("pf", k, k + 1) for k in range(8, 14)]
+    giota(r("kf", 0, 18), [[16, 18]], 0)
+    K16 = r("kf", 0, 18)
+    UL, NEL, SBL, ORL, SELL, PERM, DKL, TKL = [r("ko", a, b) for a, b in ((0, 8), (8, 26), (26, 44), (44, 45), (46, 50), (50, 64), (64, 67), (68, 71))]
+    copy(UL, r("kf", 0, 8))
     quant("uq", "us", 0, 128, r("ut", 0, 512))
-    call("v", lambda: g.vector.tensor_copy(T.urq[:, 0:384].bitcast(dt.uint32), T.uq[:, 0:128].bitcast(dt.uint32).indirect(T.ul[:, 0:24])), [r("uq", 0, 128), r("ul", 0, 24)], [r("urq", 0, 384)], 0.6)
-    call("s", lambda: g.scalar.activation(T.urs[:, 0:384], T.us[:, 0:128].indirect(T.ul[:, 0:24]), F.Copy), [r("us", 0, 128), r("ul", 0, 24)], [r("urs", 0, 384)], 0.6)
-    ts(r("j16", 0, C), r("ion", 0, C), 15, A.bitwise_and)
+    call("v", lambda: g.vector.tensor_copy(T.urq[:, 0:128].bitcast(dt.uint32), T.uq[:, 0:128].bitcast(dt.uint32).indirect(ap(UL))), [r("uq", 0, 128), UL], [r("urq", 0, 128)], 0.25)
+    call("s", lambda: g.scalar.activation(T.urs[:, 0:128], T.us[:, 0:128].indirect(ap(UL)), F.Copy), [r("us", 0, 128), UL], [r("urs", 0, 128)], 0.25)
+    giota(r("j16", 0, C), [[0, 18], [1, 16]], 0)
+    giota(r("iof", 0, 304), [[1, 304]], 0)
     ts(r("mask16", 0, C), r("j16", 0, C), Q, A.is_equal)
-    ts(ALL4, Q, 3.5, A.is_le)
-    tt(MO, ALL4, ODD, A.mult)
-    tt(ME, ALL4, MO, A.subtract)
-    ts(M01, Q, 1.5, A.is_le)
-    tt(M23, ALL4, M01, A.subtract)
-    ts(M4, Q, 4.0, A.is_equal)
-    act(r("ioo", 0, C), r("iof", 0, C), F.Copy, None, MO)
-    act(r("ioe", 0, C), r("iof", 0, C), F.Copy, None, ME)
-    copy(r("lf", 0, 18), r("li", 0, 18))
-    tt(r("lf", 18, 36), r("li", 18, 36), r("li", 0, 18), A.subtract)
+    ts(r("keep", 0, C), r("j16", 0, C), 0.0, A.is_gt)
+    copy(r("lf", 0, 36), r("li", 0, 36))
     copy(r("ll", 0, 36), r("li", 0, 36))
-    ts(r("tri", 0, 32), r("iof", 0, 32), I32, A.is_gt, 0.5, A.subtract)
-    ts(r("tri", 0, 32), r("tri", 0, 32), TINY, A.mult)
-    fill(r("ne", 0, 306), 0.0)
-    for name, w in (("ci", 0), ("cj", 1)):
-        v = [-1] + [e[w] for e in PAIRS] + [-1, 0]
-        c = [v[t] - v[t + 1] for t in range(17)]
+    fill(r("fa", 0, 36, 2), 0.0)
+    tt(r("fa", 1, 36, 2), r("li", 18, 36), r("li", 0, 18), A.subtract)
+    copy(r("fb", 1, 36, 2), r("li", 0, 18))
+    for name, w, col in (("ci", 0, RI), ("cj", 1, PW)):
+        v = [-64] + [e[w] for e in PAIRS] + [0]
+        c = [v[t] - v[t + 1] for t in range(16)]
         usual = max(sorted(set(c)), key=c.count)
-        fill(r(name, 0, 306), float(usual))
-        for t in range(17):
+        fill(r(name, 0, C), float(usual))
+        for t in range(16):
             if c[t] != usual:
-                fill(r(name, t, 306, 17), float(c[t]))
+                fill(r(name, t, C, 16), float(c[t]))
+        o = 16 + 16 * w
+        if w == 0:
+            ts(r("q3", 0, 16), r("j16", 0, 16), Q, A.is_ge)
+        tt(r("q3", o, o + 16), r("q3", 0, 16), r(name, 0, 16), A.mult)
+        total(col, r("q3", o, o + 16))
+    ts(r("pf", 16, 20), r("j16", 0, 4), PW, A.is_equal)
+    for k in range(L):
+        act(r("io", C * k, C * k + C), r("iof", 0, C), F.Copy, None, r("pf", 16 + k, 17 + k))
+    ts(T2, RI, float(ROW), A.add, 0.0, A.max)
+    ts(NEL, K16, T2, A.add)
+    ts(SBL, K16, 15.0, A.add)
+    copy(ORL, QHALF)
+    ts(SEL, QL, 32.0, A.mult, H16, A.add)
+    ts(r("ko", 46, 47), QH, SEL, A.add)
+    ts(r("pf", 20, 21), QH, -1.0, A.mult, 6.0, A.add)
+    ts(r("ko", 47, 48), r("pf", 20, 21), SEL, A.add)
+    ts(r("ko", 48, 49), SEL, 7.0, A.add)
+    ts(r("ko", 49, 50), SEL, 6.0, A.add)
+    MB, NB, NC = r("kf", 20, 25), r("kf", 26, 44), r("kf", 44, 62)
+    ts(r("kf", 64, 68), r("kf", 0, 4), Q, A.add, 0.5, A.add)
+    ts(r("kf", 68, 72), r("kf", 64, 68), float(M), A.is_ge, 1000.0, A.mult)
+    tt(r("kf", 20, 24), r("kf", 64, 68), r("kf", 68, 72), A.add)
+    fill(r("kf", 24, 25), M - 0.5)
+    ts(NC, K16, Q, A.add, -144.0, A.add)
+    ts(NB, NC, -512.0, A.mult)
+    ts(r("kf", 72, 86), r("kf", 0, 14), Q, A.add, -1.0, A.mult)
+    ts(r("ki", 0, 14), r("kf", 72, 86), float(NS - 1), A.add)
+    ts(r("ki", 16, 30), r("ki", 0, 14), 3, A.bitwise_and)
+    ts(r("ki", 32, 46), r("ki", 0, 14), 2, A.logical_shift_right)
+    ts(r("kf", 72, 86), r("ki", 16, 30), 64.0, A.mult)
+    tt(r("kf", 86, 100), r("kf", 72, 86), r("ki", 32, 46), A.add)
+    copy(PERM, r("kf", 86, 100))
+    JJ = r("kf", 100, 103)
+    ts(JJ, r("kf", 0, 3), Q, A.add)
+    ts(r("pf", 21, 22), H, -34.0, A.mult, 71.0, A.add)
+    ts(r("pf", 22, 23), ODD, H, A.not_equal, r("pf", 21, 22), A.mult)
+    ts(DKL, JJ, r("pf", 22, 23), A.add, 107.0, A.min)
+    ts(r("kf", 104, 107), JJ, 18.0, A.is_ge, -18.0, A.mult)
+    ts(r("kf", 108, 111), JJ, 36.0, A.is_ge, -18.0, A.mult)
+    tt(r("kf", 112, 115), r("kf", 104, 107), r("kf", 108, 111), A.add)
+    tt(r("kf", 116, 119), r("kf", 112, 115), JJ, A.add)
+    copy(TKL, r("kf", 116, 119))
+    fill(r("dk", 0, 108), 0.0)
+    fill(r("pos", 0, 32), 0.0)
+    fill(r("acc", 0, 16), 0.0)
+    fill(r("rsum", 0, 1), 0.0)
     gfill(r("jt", 0, 528), 1)
-    call("g", lambda: g.affine_select(T.jt[:, 0:520], T.jt[:, 0:520], [[-1, 520]], A.is_equal, 0.0, 3, 4), [r("jt", 0, 520)], [r("jt", 0, 520)], 1.2)
+    select(r("jt", 0, 520), [[-1, 520]], A.is_equal, 3, 4)
     for b in range(4):
         quant("eq", "es", 128 * b, 128 * b + 128, r("jt", 3 - b, 515 - b))
         gfill(r("fh", 304 * b + C, 304 * b + 304), 0)
-    gfill(r("rt", 0, 512), 0)
-    for a in range(4):
-        for h in range(2):
-            lo = 128 * a + 64 * h
-            call("s", lambda v=T.rt[32 * a:32 * a + 32, lo + h:lo + 64:2]: g.scalar.activation(v, v, F.Identity, bias=1024.0), [r("rt", lo, lo + 64)], [r("rt", lo, lo + 64)])
-    quant("rq", "rs", 0, 128, r("rt", 0, 512))
-    gfill(r("sg4", 2, 4 * C, 4), 0)
-    gfill(r("sg4", 3, 4 * C, 4), 0)
-    gfill(r("pk", 0, 96), 0)
-    ts(r("iot", 0, 18), r("sm0", 24, 42), I32, A.add)
-    copy(r("bcl", 0, 18), r("sm0", 42, 60))
-    ts(r("cf", 54, 55), ROLE, 18.0, A.mult)
-    ts(r("sm0", 102, 120), r("sm0", 60, 78), r("cf", 54, 55), A.add)
-    copy(r("bcl", 18, 36), r("sm0", 102, 120))
-    ts(r("bk", 4, 8), r("sm0", 80, 84), Q, A.add)
-    ts(r("bk", 8, 12), r("bk", 4, 8), 288.0, A.add)
-    ts(r("bk", 0, 4), r("bk", 4, 8), float(M), A.is_ge, -1.0e7, A.mult)
-    ts(r("bk", 4, 8), r("bk", 4, 8), -1024.0, A.mult)
-    tt(r("bk", 0, 4), r("bk", 0, 4), r("bk", 4, 8), A.add)
-    ts(r("abi", 0, 64), r("ion", 0, 64), 3, A.bitwise_and)
-    ts(r("mask4", 0, 64), r("abi", 0, 64), QQ, A.is_equal)
-    gfill(r("abt", C, 352), EMPTY)
-    gfill(r("p3", 0, 24), 0)
-    ts(r("be", 0, 18), r("sm0", 84, 102), Q, A.add, -1024.0, A.mult)
-    act(r("tabk", 0, 304), r("iof", 0, 304), F.Copy, None, 1024.0)
-    gfill(r("t3t", C, 352), 0)
-    for b in range(4):
-        gfill(r("hs", 240 * b + NS, 240 * b + 240), 0)
-    gfill(r("lp", C, 352), 0)
-    gfill(r("mask16", C, 352), 0)
-    gfill(r("lpk", 18, 24), 0)
-    ts(r("cf", 0, 18), r("li", 18, 36), 512.0, A.mult)
-    tt(r("lpk", 0, 18), r("cf", 0, 18), r("li", 0, 18), A.add)
-    tt(r("lp", 0, C), r("lpk", 0, 24), r("mask16", 0, C), A.mult, r("bcl", 0, 18))
+    giota(r("rt", 0, 1024), [[0, 2], [1, 8], [0, 64]], 0)
+    ts(r("rt", 0, 1024), r("rt", 0, 1024), GRP, A.is_equal)
+    select(r("rt", 2, 512, 4), [[-1, 128]], A.is_gt, 0, 1)
+    select(r("rt", 3, 512, 4), [[1, 128]], A.is_gt, 0, -1)
+    quant("rq", "rs", 0, 256, r("rt", 0, 1024))
+    for lo, n, blocks in TILES[:3]:
+        fill(r("sg", 4 * (lo + 16 * blocks[-1]), 4 * (lo + n)), 0.0)
+    fill(r("sg", 4 * 768, 4 * 960), 0.0)
+    quant("fq", "fs", 832, 960, r("sg", 4 * 832, 4 * 960))
+    gfill(r("mt", 0, C), 0)
+    gfill(r("st", C, 304), C + int(FLAG))
+    giota(r("iob", 0, 304), [[1, 304]], -144)
+    gfill(r("dl", 0, NS), 1)
     quant("vq", "vs", 0, 128, r("vt", 0, 512))
 
     n_of = len(T.cores)
@@ -335,15 +349,6 @@ def rank_program(g, core, T, topo):
     direct = topo.may_write(core, dst)
     hops = [dst] * 3 if direct else _relays(core, dst, topo)
     came = [src] * 3 if topo.may_write(src, core) else _relays(src, core, topo)
-
-    def evens(out, buf, lo, n):
-        tt(out, r(buf, lo, lo + n, 2), r(buf, lo + 1, lo + n, 2), A.add)
-
-    def squeeze(buf, out):
-        evens(r("tr", 0, 144), buf, 0, 288)
-        evens(r("tr", 144, 216), "tr", 0, 144)
-        evens(r("tr", 216, 252), "tr", 144, 72)
-        evens(out, "tr", 216, 36)
 
     def send(k, t):
         rid, pid = topo.addr(hops[k], core)
@@ -358,122 +363,123 @@ def rank_program(g, core, T, topo):
         quant(XQ, XS, 0, C, r("xt", 0, 4 * C))
         for k in range(2):
             send(k, t)
+        mm("bv", C, "urq", "urs", 0, XQ, XS, 0)
         mm("bs", C, "urq", "urs", 0, XQ, XS, 0)
-        mm("br0", C, "urq", "urs", 128, XQ, XS, 0)
-        mm("br1", C, "urq", "urs", 256, XQ, XS, 0)
         for b in range(4):
             mm("bf%d" % b, C, "eq", "es", 128 * b, XQ, XS, 0)
             act(r("ff", C * b, C * b + C), r("bf%d" % b, 0, C), F.Copy)
-        turn(r("tsb", 0, C), r("bs", 0, C))
-        tt(r("sm", 0, C), r("bs", 0, C), r("mask16", 0, C), A.mult)
-        act(r("s4", 0, C), r("bs", 0, C), F.Copy, None, M4)
-        for s in range(18):
-            act(r("sg%d" % (s // 4), s % 4, 4 * C, 4), r("br%d" % (s % 2), 0, C), F.Sign, r("tsb", 16 * s, 16 * s + 1), -1.0)
-        for s in range(18):
-            lo = 128 * (s // 2) + s % 4
-            v = r("sg%d" % (s // 4), lo, min(lo + 128, 4 * C), 4)
-            tt(v, v, r("tri", 0, 32), A.add)
-        squeeze("sm", r("cf", 0, 18))
-        ts(r("cf", 18, 36), r("cf", 0, 18), 0.0, A.is_gt)
-        tt(r("cf", 18, 36), r("cf", 18, 36), r("lf", 18, 36), A.mult)
-        tt(r("cf", 36, 54), r("cf", 18, 36), r("lf", 0, 18), A.add)
-        copy(r("cl", 0, 18), r("cf", 36, 54))
+        tt(r("sm", 0, C), r("bv", 0, C), r("mask16", 0, C), A.mult)
+        scan(r("so", 0, C), r("keep", 0, C), r("sm", 0, C))
+        ts(r("fb", 0, 36, 2), r("so", 15, C, 16), 0.0, A.is_gt)
+        scan(r("fc", 0, 36), r("fa", 0, 36), r("fb", 0, 36))
         CL = r("cl", 0, 18)
-        tt(r("w1", 0, C), r("ioo", 0, C), r("ioe", 0, C), A.add, CL)
-        ts(r("w2", 0, C), r("w1", 0, C), M23, A.mult, off=CL)
-        act(r("p01", 0, 2 * C), r("w1", 0, C), F.Copy, None, M01, r("ll", 0, 36))
-        tt(r("w3", 0, C), r("w2", 0, C), r("s4", 0, C), A.add, CL)
-        tt(r("pr", 0, 2 * C), r("w3", 0, C), r("p01", 0, 2 * C), A.add, r("ll", 0, 36))
-        turn(r("tpq", 0, 2 * C), r("pr", 0, 2 * C))
-        for k, (i, j) in enumerate(PAIRS + [(0, 0)]):
-            tt(r("ne", k + 1, 306, 17), r("tpq", i, C, 16), r("tpq", C + j, 2 * C, 16), A.not_equal)
-        scan(r("ij", 0, 306), r("ne", 0, 306), r("ci", 0, 306))
-        scan(r("ij", 306, 612), r("ne", 0, 306), r("cj", 0, 306))
-        I, IJ = r("ij", 16, 306, 17), r("ij", 16, 612, 17)
-        ts(r("bub", 0, 18), I, 0.0, A.is_ge)
-        ts(r("bubf", 0, 18), I, 0.0, A.is_ge)
-        ts(r("q3", 780, 798), I, 0.0, A.is_lt, BIG, A.mult)
-        tt(r("pk", 0, 18), r("q3", 780, 798), r("iot", 0, 18), A.add)
-        for k in range(5):
-            for s in range(4 * k, min(4 * k + 4, 18)):
-                for lo, hi, op in ((0, 32 * (s // 2), A.is_gt), (32 * (s // 2), C, A.is_ge)):
-                    if lo < hi:
-                        v = r("sg%d" % k, 4 * lo + s % 4, 4 * hi, 4)
-                        if lo == 0 and s // 2 >= SHARE:
-                            act(v, v, F.Relu, None, r("bubf", s, s + 1))
-                        else:
-                            ts(v, v, 0.0, op, r("bub", s, s + 1), A.mult)
-            quant("fq", "fs", C * k, C * k + C, r("sg%d" % k, 0, 4 * C))
-            mm("bk0", C, "rq", "rs", 0, "fq", "fs", C * k, k == 0, k == 4)
-        PQ = [r("tpq", k, 2 * C, 16) for k in range(L)]
-        AB = [r("abt0", 36 * k, 36 * k + 36) for k in range(L)]
-        copy(AB[0], PQ[0])
+        copy(CL, r("fc", 1, 36, 2))
+        act(r("sr", 0, C), r("bs", 0, C), F.Copy)
+        dma("y", "da%d" % t, T["io"][0:128:16, 0:C], T.sr[0:128:16, 0:C], [r("sr", 0, C)], [r("io", 0, C)])
+        act(r("sb", 0, C), r("so", 0, C), F.Copy, off=SBL)
+        tt(r("sg", 2, 4 * C, 4), r("bv", 0, C), r("sb", 0, C), A.is_lt)
+        tt(r("sg", 3, 4 * C, 4), r("bv", 0, C), r("sb", 0, C), A.is_le)
+        for x, (lo, n, blocks) in enumerate(TILES):
+            for e, k in enumerate(blocks):
+                v, s = r("sg", 4 * lo + e, 4 * (lo + 16 * k), 4), r("so", 16 * k + 15, 16 * k + 16)
+                if k in VC:
+                    ts(v, r("bv", 0, 16 * k), s, A.is_lt)
+                    act(r("junk", 8 * k * (k - 1), 8 * k * (k + 1)), v, F.Copy, acc=r("rsum", k, k + 1))
+                else:
+                    act(v, r("bs", 0, 16 * k), F.Sign, s, -1.0)
+                    act(v, v, F.Relu, acc=r("rsum", k, k + 1))
+            if x < 3:
+                quant("fq", "fs", lo, lo + n, r("sg", 4 * lo, 4 * (lo + n)))
+        quant("fq", "fs", 704, 880, r("sg", 4 * 704, 4 * 880))
+        for x, (lo, n, blocks) in enumerate(TILES):
+            mm("bk", n, "rq", "rs", 128 if x else 0, "fq", "fs", lo, x == 0, x == 4)
+        tt(r("rsum", 18, 36), K16, r("rsum", 0, 18), A.subtract)
+        tt(r("sm2", 0, C), r("bk", 0, C), r("mask16", 0, C), A.mult)
+        scan(r("po", 0, C), r("keep", 0, C), r("sm2", 0, C))
+        tt(r("pos", 0, 18), r("po", 15, C, 16), r("rsum", 18, 36), A.add)
+        copy(r("pl", 0, 18), r("pos", 0, 18))
+        tt(r("w1", 0, C), r("io", 3 * C, 4 * C), r("io", 2 * C, 3 * C), A.add, CL)
+        tt(r("w2", 0, C), r("w1", 0, C), r("io", C, 2 * C), A.add, CL)
+        tt(r("w3", 0, C), r("w2", 0, C), r("io", 0, C), A.add, CL)
+        act(r("pq", C, 2 * C), r("w3", 0, C), F.Copy, off=r("ll", 18, 36))
+        copy(r("pq", 0, C), r("w3", 0, C), r("ll", 0, 18))
+        turn(r("tpq", 0, C), r("pq", 0, C))
+        turn(r("tpq", C, 2 * C), r("pq", C, 2 * C))
+        tt(r("ne", 0, C), r("tpq", 0, C), r("tpq", C, 2 * C), A.not_equal, NEL)
+        scan(r("ij", 0, C), r("ne", 0, C), r("ci", 0, C))
+        scan(r("ij", C, 2 * C), r("ne", 0, C), r("cj", 0, C))
+        P = [r("tpq", ROW + k, C, 16) for k in range(L)]
+        U = [r("tpq", C + ROW + k, 2 * C, 16) for k in range(L)]
+        I = r("ij", 15, C, 16)
+
+        def role(name, k):
+            return r(name, k, C, 16)
+
         for k in range(1, L):
-            o = 108 * k - 108
-            ts(r("q3", o, o + 36), IJ, float(k), A.is_ge)
-            tt(r("q3", o + 36, o + 72), PQ[k], AB[k - 1], A.subtract)
-            tt(r("q3", o + 72, o + 108), r("q3", o + 36, o + 72), r("q3", o, o + 36), A.mult)
-            tt(AB[k], AB[k - 1], r("q3", o + 72, o + 108), A.add)
-        ts(r("ab5", 0, 144), r("abt0", 0, 144), 512.0, A.mult)
-        for k in range(L):
-            tt(r("pk", 24 + 18 * k, 42 + 18 * k), r("ab5", 36 * k + 18, 36 * k + 36), r("abt0", 36 * k, 36 * k + 18), A.add)
-        act(r("bc", 0, 2 * C), r("pk", 0, 96), F.Copy, off=r("bcl", 0, 36))
-        turn(r("nt", 0, C), r("bc", 0, C))
-        turn(r("abt", 0, C), r("bc", C, 2 * C))
-        tt(r("key", 0, C), r("bk0", 0, C), r("nt", 0, C), A.add)
-        for c in range(4):
-            act(r("ak", C * c, C * c + C), r("key", 0, C), F.Abs, r("bk", c, c + 1))
-            least(r("ordf", c, c + 1), r("ak", C * c, C * c + C))
-        tt(r("ordf", 4, 8), r("ordf", 0, 4), r("bk", 8, 12), A.min)
-        copy(r("ordl", 0, 4), r("ordf", 4, 8))
-        ORD = r("ordl", 0, 4)
-        tt(r("abg", 0, 64), r("abt", 0, 352), r("mask4", 0, 64), A.mult, ORD)
-        evens(r("abg", 64, 96), "abg", 0, 64)
-        evens(r("abi", 0, 16), "abg", 64, 32)
-        ts(r("abi", 16, 32), r("abi", 0, 16), 511, A.bitwise_and)
-        ts(r("abi", 32, 48), r("abi", 0, 16), 9, A.logical_shift_right)
-        copy(r("al%d" % t, 0, 32), r("abi", 16, 48))
+            o = 72 * k - 72
+            tt(r("q3", o, o + 18), P[k], P[k - 1], A.subtract)
+            tt(r("q3", o + 18, o + 36), U[k - 1], U[k], A.subtract)
+            ts(r("q3", o + 36, o + 72), r("ij", 15, 2 * C, 16), float(k), A.is_ge)
+            tt(role("mt", k), r("q3", o, o + 18), r("q3", o + 36, o + 54), A.mult)
+            tt(role("mt", 7 - k), r("q3", o + 18, o + 36), r("q3", o + 54, o + 72), A.mult)
+        tt(role("mt", 7), r("tpq", C, 2 * C, 16), r("tpq", 0, C, 16), A.is_gt)
+        tt(r("q3", 216, 234), P[0], U[0], A.not_equal)
+        ts(r("q3", 234, 252), r("q3", 216, 234), FLAG, A.mult)
+        tt(r("q3", 252, 270), r("q3", 234, 252), P[0], A.add)
+        ts(r("q3", 270, 288), I, 0.0, A.is_lt, -FLAG, A.mult)
+        tt(role("mt", 0), r("q3", 252, 270), r("q3", 270, 288), A.add)
+        scan(r("tb", 0, C), r("keep", 0, C), r("mt", 0, C))
+        turn(r("tr", 0, C), r("tb", 0, C))
+        call("v", lambda: g.vector.tensor_copy(T.st[:, 0:C].indirect(T.pl[:, 0:18]), T.tr[:, 0:C]), [r("tr", 0, C), r("pl", 0, 18)], [r("st", 0, C)], 0.05 + SCAT * C)
+        ts(r("fl", 0, C), r("st", 0, C), FLAG / 2, A.is_ge)
+        scan(r("cn", 0, C), r("fl", 0, C), r("fl", 0, C), 0.0, A.add, A.max)
+        for c in range(5):
+            act(r("jc", C * c, C * c + C), r("cn", 0, C), F.Sign, r("kf", 20 + c, 21 + c), -1.0, acc=r("acc", 8 * (c // 4) + c % 4, 8 * (c // 4) + c % 4 + 1))
+        ts(r("ordl", 0, 16), r("acc", 0, 8), 0.5, A.mult, C / 2, A.add, ORL)
+        copy(r("gt", 0, 128), r("st", 0, 304), r("ordl", 0, 8))
+        turn(r("tg", 0, 128), r("gt", 0, 128))
+        ts(r("al%d" % t, 0, 32), r("tg", 0, 128), -FLAG, A.add, off=r("ko", 46, 48))
         send(2, t)
-        o = 324
-        tt(r("q3", o, o + 36), AB[3], PQ[0], A.subtract)
-        ts(r("q3", o + 36, o + 54), r("q3", o + 18, o + 36), 512.0, A.mult)
-        tt(r("q3", o + 54, o + 72), r("q3", o, o + 18), r("q3", o + 36, o + 54), A.subtract)
-        tt(r("q3", o + 72, o + 90), r("tpq", C + 4, 2 * C, 16), r("tpq", 4, C, 16), A.is_gt)
-        tt(r("q3", o + 90, o + 108), r("q3", o + 72, o + 90), r("q3", o + 54, o + 72), A.mult)
-        tt(r("q3", o + 108, o + 126), r("ab5", 108, 126), r("tpq", 0, C, 16), A.add)
-        tt(r("q3", o + 126, o + 144), r("q3", o + 108, o + 126), r("q3", o + 90, o + 108), A.add)
-        ts(r("q3", o + 144, o + 162), r("q3", o + 72, o + 90), 262144.0, A.mult)
-        tt(r("p3", 0, 18), r("q3", o + 126, o + 144), r("q3", o + 144, o + 162), A.add)
-        act(r("bc3", 0, C), r("p3", 0, 24), F.Copy, off=r("bcl", 0, 18))
-        turn(r("t3t", 0, C), r("bc3", 0, C))
-        copy(r("t3g", 0, 64), r("t3t", 0, 352), ORD)
-        tt(r("t3m", 0, 64), r("t3t", 0, 352), r("mask4", 0, 64), A.mult, ORD)
-        evens(r("t3m", 64, 96), "t3m", 0, 64)
-        evens(r("bn", 0, 16), "t3m", 64, 32)
-        ts(r("bn", 16, 32), r("bn", 0, 16), 18, A.logical_shift_right)
-        tt(r("bn", 32, 48), r("abi", 32, 48), r("abi", 16, 32), A.subtract)
-        tt(r("bn", 48, 64), r("bn", 32, 48), r("bn", 16, 32), A.mult)
-        tt(r("bn", 64, 80), r("bn", 48, 64), r("abi", 16, 32), A.add)
-        copy(r("bnl", 0, 16), r("bn", 64, 80))
-        tt(r("ks", 0, NS), r("tabk", 0, 304), r("iof", 0, NS), A.add, r("bnl", 0, 14))
+        copy(r("ab", 0, 64), r("tg", 0, 128), SELL)
+        tt(r("ab", 64, 80), r("ab", 32, 48), r("ab", 48, 64), A.subtract)
+        tt(r("ab", 80, 96), r("ab", 16, 32), r("ab", 0, 16), A.subtract)
+        tt(r("ab", 96, 112), r("ab", 64, 80), r("ab", 80, 96), A.mult)
+        tt(r("ab", 112, 128), r("ab", 96, 112), r("ab", 0, 16), A.add)
+        ts(r("bnl", 0, 16), r("ab", 112, 128), -FLAG, A.add)
+        act(r("bnr", 0, NZ), r("iob", 0, 304), F.Copy, off=r("bnl", 0, 16))
+        act(r("bns", 0, NS), r("bnr", 0, NZ), F.Copy, off=PERM)
         for k in range(18):
+            v = r("ea", NS * k, NS * k + NS)
             if k in VE:
-                ts(r("ea", NS * k, NS * k + NS), r("ks", 0, NS), r("be", k, k + 1), A.add)
+                ts(v, r("bns", 0, NS), r("kf", 44 + k, 45 + k), A.not_equal, 512.0, A.mult)
             else:
-                act(r("ea", NS * k, NS * k + NS), r("ks", 0, NS), F.Abs, r("be", k, k + 1))
-            least(r("em", k, k + 1), r("ea", NS * k, NS * k + NS))
-        ts(r("em", 18, 36), r("em", 0, 18), float(NS), A.min)
-        copy(r("el", 0, 18), r("em", 18, 36))
-        tt(r("t3q", 0, 64), r("mask16", 0, 352), r("t3g", 0, 64), A.mult, ORD)
-        W = r("t3q", 0, 64)
-        call("v", lambda W=W: g.vector.tensor_copy(T.lp[:, 0:352].indirect(T.ordl[:, 0:4]), ap(W)), [W, ORD], [r("lp", 0, 352)], 0.25)
-        squeeze("lp", r("lk", 0, 18))
-        ts(r("li", 0, 18), r("lk", 0, 18), 511, A.bitwise_and)
-        ts(r("li", 18, 36), r("lk", 0, 18), 9, A.logical_shift_right, 511, A.bitwise_and)
-        copy(r("ll", 0, 36), r("li", 0, 36))
+                act(v, r("bns", 0, NS), F.Abs, r("kf", 26 + k, 27 + k), 512.0)
+            scan(r("eo", NS * k, NS * k + NS), r("dl", 0, NS), v, 1024.0, A.add, A.min)
+        E = r("eo", NS - 1, 18 * NS, NS)
+        ts(r("ki", 48, 66), E, float(NS), A.min)
+        ts(r("kf", 120, 138), E, float(NS), A.min, 64.0, A.mult)
+        ts(r("ki", 66, 84), r("ki", 48, 66), 2, A.logical_shift_right)
+        ts(r("kf", 138, 156), r("ki", 66, 84), -255.0, A.mult)
+        tt(r("em", 0, 18), r("kf", 120, 138), r("kf", 138, 156), A.add)
+        copy(r("el", 0, 18), r("em", 0, 18))
+        o = 288
+        ts(r("q3", o, o + 18), role("tb", 0), FLAG / 2, A.is_ge)
+        tt(r("q3", o + 18, o + 36), r("q3", o, o + 18), role("mt", 7), A.mult)
+        tt(r("q3", o + 36, o + 54), r("q3", o, o + 18), r("q3", o + 18, o + 36), A.subtract)
+        tt(r("q3", o + 54, o + 72), role("tb", 3), role("tb", 0), A.subtract)
+        tt(r("q3", o + 72, o + 90), role("tb", 3), role("tb", 6), A.subtract)
+        tt(r("dk", 0, 18), r("q3", o + 54, o + 72), r("q3", o + 18, o + 36), A.mult)
+        tt(r("dk", 18, 36), r("q3", o + 72, o + 90), r("q3", o + 36, o + 54), A.mult)
+        dma("y", "db%d" % t, T.dk[16:128, 36:72], T.dk[0:112, 0:36], [r("dk", 0, 36)], [r("dk", 36, 72)])
+        dma("y", "dc%d" % t, T.dk[0:112, 72:108], T.dk[16:128, 0:36], [r("dk", 0, 36)], [r("dk", 72, 108)])
+        ts(THR, r("acc", 8, 9), 0.5, A.mult, C / 2, A.add)
+        ts(r("tk", 0, 48), r("pos", 0, 32), THR, A.is_le, off=TKL)
+        tt(r("tk", 48, 96), r("dk", 0, 108), r("tk", 0, 48), A.mult, DKL)
+        tt(r("lf", 0, 36), r("lf", 0, 36), r("tk", 48, 84), A.add)
+        copy(r("ll", 0, 36), r("lf", 0, 36))
         if t < R - 1:
-            copy(r("lf", 0, 18), r("li", 0, 18))
-            tt(r("lf", 18, 36), r("li", 18, 36), r("li", 0, 18), A.subtract)
+            copy(r("fb", 1, 36, 2), r("lf", 0, 18))
+            tt(r("fa", 1, 36, 2), r("lf", 18, 36), r("lf", 0, 18), A.subtract)
         else:
             act(r("lof", 0, 2 * C), r("iof", 0, 304), F.Copy, off=r("ll", 0, 36))
             dma("y", "done", T.ol[:, :], T.lof[0:128:16, :], [r("lof", 0, 2 * C)], [])
@@ -481,18 +487,18 @@ def rank_program(g, core, T, topo):
             mm("bf%d" % b, C, "eq", "es", 128 * b, "yq%d" % t, "ys%d" % t, 0)
             act(r("fh", 304 * b, 304 * b + C), r("bf%d" % b, 0, C), F.Copy, None, 0.5)
         for b in range(4):
-            H = r("fh", 304 * b, 304 * b + 304)
-            act(r("ga", NS * b, NS * b + NS), H, F.Copy, off=r("ysl%d" % t, 0, 14))
-            tt(r("zt", b, 4 * NS, 4), H, r("ga", NS * b, NS * b + NS), A.add, r("ysl%d" % t, 16, 30))
-        quant("zq", "zs", 0, NS, r("zt", 0, 4 * NS))
+            HB = r("fh", 304 * b, 304 * b + 304)
+            act(r("ga", NZ * b, NZ * b + NZ), HB, F.Copy, off=r("ysl%d" % t, 0, 16))
+            tt(r("zt", b, 4 * NZ, 4), HB, r("ga", NZ * b, NZ * b + NZ), A.add, r("ysl%d" % t, 16, 32))
+        quant("zq", "zs", 0, NZ, r("zt", 0, 4 * NZ))
         for b in range(4):
-            mm(BANKS[b], NS, "wq", "wp", 128 * b, "zq", "zs", 0)
-            act(r("hs", 240 * b, 240 * b + NS), r(BANKS[b], 0, NS), F.Copy, None, 0.03125)
-            tt(r("xt", b, 4 * C, 4), r("hs", 240 * b, 240 * b + 240), r("ff", C * b, C * b + C), A.add, r("el", 0, 18))
+            mm(BANKS[b], NZ, "wq", "wp", 128 * b, "zq", "zs", 0)
+            act(r("hs", NZ * b, NZ * b + NZ), r(BANKS[b], 0, NZ), F.Copy, None, 0.03125)
+            tt(r("xt", b, 4 * C, 4), r("hs", NZ * b, NZ * b + NZ), r("ff", C * b, C * b + C), A.add, r("el", 0, 18))
 
     quant("xq3", "xs3", 0, C, r("xt", 0, 4 * C))
-    mm("bs", C, "vq", "vs", 0, "xq3", "xs3", 0)
-    act(r("yo", 0, C), r("bs", 0, C), F.Copy)
+    mm("bv", C, "vq", "vs", 0, "xq3", "xs3", 0)
+    act(r("yo", 0, C), r("bv", 0, C), F.Copy)
     dma("y", "done", T.oc[:, :], T.xq3[:, 0:C].bitcast(dt.uint8), [r("xq3", 0, C)], [])
     for k in range(4):
         dma("ys"[k % 2], "done", T.osc[4 * k:4 * k + 4, :], T.xs3[32 * k:32 * k + 4, 0:C], [r("xs3", 0, C)], [])

@@ -1,17 +1,21 @@
+import numpy as np
 from concourse.mybir import dt, AluOpType, AxisListType, ActivationFunctionType
 
 C, L, M, R = 288, 4, 56, 3
 NS = L * M
 NZ = 256
-FLAG = 1024.0
+NE = 248
+FLAG = 2.0 ** 20
+FAR = 1024.0
+MID = 144.0
 
 _BUFS = """xt:1152:b ut:512:b uq:128:c us:128:p urq:128:c urs:128:p vt:512:b vq:128:c vs:128:p wq:512:c wp:512:p
 jt:528:b eq:512:c es:512:p rt:1024:b rq:256:c rs:256:p fq:960:c fs:960:p zt:1024:b fh:1216:b ff:1152:b ga:1024:b hs:1088 yo:288
 zq:256:c zs:256:p xq3:288:c xs3:288:p sg:3840:b junk:2464:b jc:1440:b
-pi:16:i pf:32 iof:304 iob:304:b j16:288:b mask16:288:b keep:288:b ci:288:b cj:288:b io:1152 ki:160:i kf:160 ko:160:o li:36:i
-ll:36:o lf:36 fa:36 fb:36 fc:36 cl:18:o sm:288 so:288 sr:288 sb:288 ww:864 pq:576 tpq:576 ne:288:b ij:576:b q3:400 mt:288 tb:288
-tr:288 st:304 fl:288:b cn:288:b acc:16 ordl:16:o gt:128 tg:128 rsum:36 sm2:288 po:288 pos:32 pl:18:o ab:128 bnl:16:o bnr:256:b
-bns:224:b dl:224:b ea:4032:b eo:4032:b el:18:o em:18 dk:108 tk:96 lof:576"""
+pi:16:i pf:32 iob:304:b j16:288:b mask16:288:b keep:288:b ci:288:b cj:288:b io:1152 ki:160:i kf:180 ko:160:o li:36:i
+ll:36:o lf:36 fa:36 fb:36 fc:36 cl:18:o sm:288 so:288 sr:288 sb:288 ww:864 pq:576 tpq:576 ne:288:b ij:576:b q3:400 mt:288 tb:288:b
+tr:288:b st:304:b fl:288:b cn:288:b acc:16 ordl:32:o gt:128:b tg:128:b jd:288:b rsum:36 sm2:288 po:288 cap:288 gp:288 pl:18:o ab:160 bnl:16:o bnr:256:b
+dl:248:b ea:4464:b eo:4464:b el:18:o em:18 dk:108 tk:96 lof:576"""
 for _t in range(R):
     _BUFS += " xq%d:288:c xs%d:288:p al%d:32:o hq%d:288:c hs_%d:288:p hsl%d:32:o yq%d:288:c ys%d:288:p ysl%d:32:o" % ((_t,) * 9)
 _DT = {"b": "bfloat16", "c": "float8_e4m3fn_x4", "p": "uint8", "i": "int32", "o": "uint16", "f": "float32"}
@@ -26,13 +30,16 @@ PART = {"w1": ("ww", 0), "w2": ("ww", 288), "w3": ("ww", 576)}
 SEMAPHORES = (["qv", "qs", "qt", "qg", "left", "dx", "du", "dn", "dw", "dp", "dv", "done"]
               + [p + k + str(t) for p in ("got", "rel") for k in "qsl" for t in range(R)] + ["d" + k + str(t) for k in "abc" for t in range(R)])
 
+KEPT = 3
+FIRST = 6
 VC = (9, 10, 11)
 VE = (1, 3, 5, 7, 9, 11, 13, 15)
 PAIRS = sorted([(i, j) for i in range(L) for j in range(L) if i + j], key=lambda e: (e[0] + e[1], e[0]))[::-1]
 ROW = 7
 TILES = [(0, 288, (17, 16)), (288, 240, (15, 14, 13, 12)), (528, 176, (11, 10, 9, 8)), (704, 128, (7, 6, 5, 4)), (832, 128, (3, 2, 1))]
 
-CYC, PICK, SCAT, ACT, WAKE, TRIP, LOAD = 1.0e-3, 1.5e-3, 3.5e-3, 0.02, 0.2, (8.0, 8.0, 4.5), 2.2
+CYC, PICK, SCAT, ACT, WAKE, TRIP, LOAD = 1.0e-3, 1.5e-3, 3.5e-3, 0.02, 0.2, (8.0, 8.0, 3.4), 2.2
+NEAR, TURNS, TRIES, SPREAD, SOME = 0.05, 20, 1000, 0.2, 0.1
 
 
 def _relays(core, dst, topo):
@@ -66,17 +73,11 @@ def _relay_program(g, core, T, topo):
         g.wait_ge(T.sem.left, n)
 
 
-def _order(nodes):
-    users = [[] for n in nodes]
-    for i, n in enumerate(nodes):
-        for d in n["deps"]:
-            users[d].append(i)
-    tail = [0.0] * len(nodes)
-    for i in reversed(range(len(nodes))):
-        tail[i] = nodes[i]["occ"] + nodes[i]["lat"] + max([tail[u] + WAKE for u in users[i]] + [0.0])
+def _list_order(nodes, users, rank):
     left = [len(n["deps"]) for n in nodes]
-    ready_at = [0.0] * len(nodes)
-    free, ready, out = {}, {}, []
+    ready_at = [n.get("late", 0.0) for n in nodes]
+    began = [0.0] * len(nodes)
+    free, ready, out, end = {}, {}, [], 0.0
     for i, n in enumerate(nodes):
         if not left[i]:
             ready.setdefault(n["q"], []).append(i)
@@ -84,22 +85,57 @@ def _order(nodes):
         best = None
         for q, c in ready.items():
             if c:
-                at = [max(free.get(q, 0.0), ready_at[i]) for i in c]
-                start = min(at)
+                start = max(free.get(q, 0.0), min(ready_at[i] for i in c))
                 if best is None or start < best[0]:
-                    near = [i for i, a in zip(c, at) if a <= start + 0.02]
-                    best = (start, q, max(near, key=lambda i: tail[i]))
-        start, q, i = best
+                    best = (start, q)
+        start, q = best
+        i = max([i for i in ready[q] if ready_at[i] <= start + NEAR], key=lambda i: rank[i])
         start = max(start, ready_at[i])
         ready[q].remove(i)
         out.append(i)
+        began[i] = start
         free[q] = start + nodes[i]["occ"]
+        end = max(end, free[q] + nodes[i]["lat"])
         for u in users[i]:
-            ready_at[u] = max(ready_at[u], free[q] + nodes[i]["lat"] + WAKE)
+            ready_at[u] = max(ready_at[u], free[q] + nodes[i]["lat"] + nodes[u].get("late", 0.0) + (WAKE if nodes[u]["deps"][i] else 0.0))
             left[u] -= 1
             if not left[u]:
                 ready.setdefault(nodes[u]["q"], []).append(u)
-    return out
+    return out, began, end
+
+
+_ORDERS = {}
+
+
+def _order(nodes):
+    key = tuple((n["q"], n["occ"], tuple(n["deps"])) for n in nodes)
+    if key in _ORDERS:
+        return _ORDERS[key]
+    users = [[] for n in nodes]
+    for i, n in enumerate(nodes):
+        for d in n["deps"]:
+            users[d].append(i)
+    tail = [0.0] * len(nodes)
+    for i in reversed(range(len(nodes))):
+        tail[i] = nodes[i]["occ"] + nodes[i]["lat"] + max([tail[u] + WAKE for u in users[i]] + [0.0])
+    rng = np.random.default_rng(7)
+    rank = np.array(tail)
+    best = _list_order(nodes, users, tail)
+    back = [{"q": n["q"], "occ": n["occ"], "lat": 0.0, "deps": {u: nodes[u]["deps"][i] for u in users[i]}, "late": n["lat"]} for i, n in enumerate(nodes)]
+    o = best
+    for k in range(TURNS):
+        b = _list_order(back, [list(n["deps"]) for n in nodes], [o[1][i] + n["occ"] + n["lat"] for i, n in enumerate(nodes)])
+        other = np.array([b[1][i] + n["occ"] for i, n in enumerate(nodes)])
+        o = _list_order(nodes, users, list(other))
+        if o[2] <= best[2]:
+            best, rank = o, other
+    for k in range(TRIES):
+        other = rank + rng.normal(0.0, SPREAD, len(nodes)) * (rng.random(len(nodes)) < SOME)
+        o = _list_order(nodes, users, list(other))
+        if o[2] <= best[2]:
+            best, rank = o, other
+    _ORDERS[key] = best[0]
+    return best[0]
 
 
 def rank_program(g, core, T, topo):
@@ -244,9 +280,7 @@ def rank_program(g, core, T, topo):
     dma("y", "du", T.ut[:, :], T.u[:, :], [], [r("ut", 0, 512)])
     dma("s", "dx", T.xt[:, :], T.x[:, :], [], [r("xt", 0, 4 * C)])
     dma("y", "dn", T.li[:, :], T.nb[:, :], [], [r("li", 0, 36)])
-    dma("s", "dw", T.wq[:, :].bitcast(dt.uint8), T.wc[:, :], [], [r("wq", 0, 512)])
-    dma("y", "dp", T.wp[:, :], T.ws[:, :], [], [r("wp", 0, 512)])
-    dma("y", "dv", T.vt[:, :], T.v[:, :], [], [r("vt", 0, 512)])
+    LATER = [r("uq", 0, 128), r("xq0", 0, C)]
 
     iota(r("pi", 0, 1), [[0, 1]], 0, 1)
     for k, (sh, mask) in enumerate(((0, 15), (0, 16), (4, 7), (0, 3), (2, 3), (0, 1), (4, 1), (1, 7))):
@@ -262,7 +296,7 @@ def rank_program(g, core, T, topo):
     call("v", lambda: g.vector.tensor_copy(T.urq[:, 0:128].bitcast(dt.uint32), T.uq[:, 0:128].bitcast(dt.uint32).indirect(ap(UL))), [r("uq", 0, 128), UL], [r("urq", 0, 128)], 0.25)
     call("s", lambda: g.scalar.activation(T.urs[:, 0:128], T.us[:, 0:128].indirect(ap(UL)), F.Copy), [r("us", 0, 128), UL], [r("urs", 0, 128)], 0.25)
     giota(r("j16", 0, C), [[0, 18], [1, 16]], 0)
-    giota(r("iof", 0, 304), [[1, 304]], 0)
+    giota(r("iob", 0, 304), [[1, 304]], -int(MID))
     ts(r("mask16", 0, C), r("j16", 0, C), Q, A.is_equal)
     ts(r("keep", 0, C), r("j16", 0, C), 0.0, A.is_gt)
     copy(r("lf", 0, 36), r("li", 0, 36))
@@ -277,7 +311,7 @@ def rank_program(g, core, T, topo):
         fill(r(name, 0, C), float(usual))
         for t in range(16):
             if c[t] != usual:
-                fill(r(name, t, C, 16), float(c[t]))
+                act(r(name, t, C, 16), r(name, t, C, 16), F.Identity, float(c[t]), 0.0)
         o = 16 + 16 * w
         if w == 0:
             ts(r("q3", 0, 16), r("j16", 0, 16), Q, A.is_ge)
@@ -285,11 +319,14 @@ def rank_program(g, core, T, topo):
         total(col, r("q3", o, o + 16))
     ts(r("pf", 16, 20), r("j16", 0, 4), PW, A.is_equal)
     for k in range(L):
-        act(r("io", C * k, C * k + C), r("iof", 0, C), F.Copy, None, r("pf", 16 + k, 17 + k))
+        act(r("io", C * k, C * k + C), r("iob", 0, C), F.Copy, None, r("pf", 16 + k, 17 + k))
     ts(T2, RI, float(ROW), A.add, 0.0, A.max)
     ts(NEL, K16, T2, A.add)
     ts(SBL, K16, 15.0, A.add)
-    copy(ORL, QHALF)
+    ts(ORL, QHALF, 6.5, A.is_ge)
+    ORV = r("ko", 72, 73)
+    ts(r("pf", 23, 24), QHALF, 0.5, A.is_ge, 144.0, A.mult)
+    ts(ORV, r("pf", 23, 24), 143.0, A.add)
     ts(SEL, QL, 32.0, A.mult, H16, A.add)
     ts(r("ko", 46, 47), QH, SEL, A.add)
     ts(r("pf", 20, 21), QH, -1.0, A.mult, 6.0, A.add)
@@ -299,17 +336,12 @@ def rank_program(g, core, T, topo):
     MB, NB, NC = r("kf", 20, 25), r("kf", 26, 44), r("kf", 44, 62)
     ts(r("kf", 64, 68), r("kf", 0, 4), Q, A.add, 0.5, A.add)
     ts(r("kf", 68, 72), r("kf", 64, 68), float(M), A.is_ge, 1000.0, A.mult)
-    tt(r("kf", 20, 24), r("kf", 64, 68), r("kf", 68, 72), A.add)
-    fill(r("kf", 24, 25), M - 0.5)
-    ts(NC, K16, Q, A.add, -144.0, A.add)
+    tt(r("kf", 156, 160), r("kf", 64, 68), r("kf", 68, 72), A.add)
+    ts(r("kf", 20, 24), r("kf", 156, 160), FLAG, A.mult)
+    fill(r("kf", 24, 25), (M - 0.5) * FLAG)
+    fill(r("fl", 0, C), FLAG)
+    ts(NC, K16, Q, A.add, -MID, A.add)
     ts(NB, NC, -512.0, A.mult)
-    ts(r("kf", 72, 86), r("kf", 0, 14), Q, A.add, -1.0, A.mult)
-    ts(r("ki", 0, 14), r("kf", 72, 86), float(NS - 1), A.add)
-    ts(r("ki", 16, 30), r("ki", 0, 14), 3, A.bitwise_and)
-    ts(r("ki", 32, 46), r("ki", 0, 14), 2, A.logical_shift_right)
-    ts(r("kf", 72, 86), r("ki", 16, 30), 64.0, A.mult)
-    tt(r("kf", 86, 100), r("kf", 72, 86), r("ki", 32, 46), A.add)
-    copy(PERM, r("kf", 86, 100))
     JJ = r("kf", 100, 103)
     ts(JJ, r("kf", 0, 3), Q, A.add)
     ts(r("pf", 21, 22), H, -34.0, A.mult, 71.0, A.add)
@@ -319,9 +351,13 @@ def rank_program(g, core, T, topo):
     ts(r("kf", 108, 111), JJ, 36.0, A.is_ge, -18.0, A.mult)
     tt(r("kf", 112, 115), r("kf", 104, 107), r("kf", 108, 111), A.add)
     tt(r("kf", 116, 119), r("kf", 112, 115), JJ, A.add)
-    copy(TKL, r("kf", 116, 119))
+    ts(TKL, r("kf", 116, 119), 16.0, A.mult, 15.0, A.add)
     fill(r("dk", 0, 108), 0.0)
-    fill(r("pos", 0, 32), 0.0)
+    ts(r("cap", 0, C), r("mask16", 0, C), FAR, A.mult)
+    ts(r("kf", 160, 178), K16, -FAR, A.add)
+    ts(r("pf", 24, 25), Q, 0.0, A.not_equal)
+    ts(r("pf", 25, 26), Q, 0.0, A.is_equal)
+    ts(r("pf", 26, 28), r("mask16", 0, 2), FAR, A.mult)
     fill(r("acc", 0, 16), 0.0)
     fill(r("rsum", 0, 1), 0.0)
     gfill(r("jt", 0, 528), 1)
@@ -329,8 +365,9 @@ def rank_program(g, core, T, topo):
     for b in range(4):
         quant("eq", "es", 128 * b, 128 * b + 128, r("jt", 3 - b, 515 - b))
         gfill(r("fh", 304 * b + C, 304 * b + 304), 0)
-    giota(r("rt", 0, 1024), [[0, 2], [1, 8], [0, 64]], 0)
-    ts(r("rt", 0, 1024), r("rt", 0, 1024), GRP, A.is_equal)
+    giota(r("rt", 512, 1024), [[1, 8], [0, 64]], 0)
+    ts(r("rt", 512, 1024), r("rt", 512, 1024), GRP, A.is_equal)
+    act(r("rt", 0, 512), r("rt", 512, 1024), F.Copy)
     select(r("rt", 2, 512, 4), [[-1, 128]], A.is_gt, 0, 1)
     select(r("rt", 3, 512, 4), [[1, 128]], A.is_gt, 0, -1)
     quant("rq", "rs", 0, 256, r("rt", 0, 1024))
@@ -339,10 +376,10 @@ def rank_program(g, core, T, topo):
     fill(r("sg", 4 * 768, 4 * 960), 0.0)
     quant("fq", "fs", 832, 960, r("sg", 4 * 832, 4 * 960))
     gfill(r("mt", 0, C), 0)
-    gfill(r("st", C, 304), C + int(FLAG))
-    giota(r("iob", 0, 304), [[1, 304]], -144)
-    gfill(r("dl", 0, NS), 1)
-    quant("vq", "vs", 0, 128, r("vt", 0, 512))
+    gfill(r("st", C, 304), C - int(MID))
+    gfill(r("dl", 0, NE), -4)
+    gfill(r("dl", 64, NE, 64), 251)
+    gfill(r("ab", 64, 96, 2), 0)
 
     n_of = len(T.cores)
     dst, src = T.cores[(rank + 1) % n_of], T.cores[(rank - 1) % n_of]
@@ -361,11 +398,16 @@ def rank_program(g, core, T, topo):
     for t in range(R):
         XQ, XS = "xq%d" % t, "xs%d" % t
         quant(XQ, XS, 0, C, r("xt", 0, 4 * C))
+        if t == 0:
+            dma("y", "dw", T.wq[:, :].bitcast(dt.uint8), T.wc[:, :], LATER, [r("wq", 0, 512)])
+            dma("y", "dp", T.wp[:, :], T.ws[:, :], LATER, [r("wp", 0, 512)])
+            dma("y", "dv", T.vt[:, :], T.v[:, :], LATER, [r("vt", 0, 512)])
+            quant("vq", "vs", 0, 128, r("vt", 0, 512))
         for k in range(2):
             send(k, t)
         mm("bv", C, "urq", "urs", 0, XQ, XS, 0)
         mm("bs", C, "urq", "urs", 0, XQ, XS, 0)
-        for b in range(4):
+        for b in range(KEPT):
             mm("bf%d" % b, C, "eq", "es", 128 * b, XQ, XS, 0)
             act(r("ff", C * b, C * b + C), r("bf%d" % b, 0, C), F.Copy)
         tt(r("sm", 0, C), r("bv", 0, C), r("mask16", 0, C), A.mult)
@@ -393,11 +435,12 @@ def rank_program(g, core, T, topo):
         quant("fq", "fs", 704, 880, r("sg", 4 * 704, 4 * 880))
         for x, (lo, n, blocks) in enumerate(TILES):
             mm("bk", n, "rq", "rs", 128 if x else 0, "fq", "fs", lo, x == 0, x == 4)
-        tt(r("rsum", 18, 36), K16, r("rsum", 0, 18), A.subtract)
-        tt(r("sm2", 0, C), r("bk", 0, C), r("mask16", 0, C), A.mult)
+        tt(r("rsum", 18, 36), r("kf", 160, 178), r("rsum", 0, 18), A.subtract)
+        for e in range(2):
+            ts(r("cap", e, C, 16), r("rsum", 18, 36), r("pf", 24 + e, 25 + e), A.mult, r("pf", 26 + e, 27 + e), A.add)
+        tt(r("sm2", 0, C), r("bk", 0, C), r("cap", 0, C), A.min)
         scan(r("po", 0, C), r("keep", 0, C), r("sm2", 0, C))
-        tt(r("pos", 0, 18), r("po", 15, C, 16), r("rsum", 18, 36), A.add)
-        copy(r("pl", 0, 18), r("pos", 0, 18))
+        ts(r("pl", 0, 18), r("po", 15, C, 16), FAR, A.add)
         tt(r("w1", 0, C), r("io", 3 * C, 4 * C), r("io", 2 * C, 3 * C), A.add, CL)
         tt(r("w2", 0, C), r("w1", 0, C), r("io", C, 2 * C), A.add, CL)
         tt(r("w3", 0, C), r("w2", 0, C), r("io", 0, C), A.add, CL)
@@ -423,47 +466,49 @@ def rank_program(g, core, T, topo):
             tt(role("mt", k), r("q3", o, o + 18), r("q3", o + 36, o + 54), A.mult)
             tt(role("mt", 7 - k), r("q3", o + 18, o + 36), r("q3", o + 54, o + 72), A.mult)
         tt(role("mt", 7), r("tpq", C, 2 * C, 16), r("tpq", 0, C, 16), A.is_gt)
-        tt(r("q3", 216, 234), P[0], U[0], A.not_equal)
-        ts(r("q3", 234, 252), r("q3", 216, 234), FLAG, A.mult)
+        tt(r("q3", 216, 234), P[0], U[0], A.is_equal)
+        act(r("q3", 234, 252), r("q3", 216, 234), F.Copy, None, -FLAG)
         tt(r("q3", 252, 270), r("q3", 234, 252), P[0], A.add)
         ts(r("q3", 270, 288), I, 0.0, A.is_lt, -FLAG, A.mult)
         tt(role("mt", 0), r("q3", 252, 270), r("q3", 270, 288), A.add)
         scan(r("tb", 0, C), r("keep", 0, C), r("mt", 0, C))
         turn(r("tr", 0, C), r("tb", 0, C))
         call("v", lambda: g.vector.tensor_copy(T.st[:, 0:C].indirect(T.pl[:, 0:18]), T.tr[:, 0:C]), [r("tr", 0, C), r("pl", 0, 18)], [r("st", 0, C)], 0.05 + SCAT * C)
-        ts(r("fl", 0, C), r("st", 0, C), FLAG / 2, A.is_ge)
-        scan(r("cn", 0, C), r("fl", 0, C), r("fl", 0, C), 0.0, A.add, A.max)
-        for c in range(5):
+        scan(r("cn", 0, C), r("st", 0, C), r("fl", 0, C), 0.0, A.add, A.add)
+        for c in (0, 1, 4):
             act(r("jc", C * c, C * c + C), r("cn", 0, C), F.Sign, r("kf", 20 + c, 21 + c), -1.0, acc=r("acc", 8 * (c // 4) + c % 4, 8 * (c // 4) + c % 4 + 1))
+        for c in (2, 3):
+            ts(r("jc", C * c, C * c + C), r("cn", 0, C), r("kf", 20 + c, 21 + c), A.is_le, 0.5, A.subtract)
+            scan(r("jd", 144 * c - C, 144 * c - 144), r("jc", C * c, C * c + 144), r("jc", C * c + 144, C * c + C), 0.0, A.add, A.add)
         ts(r("ordl", 0, 16), r("acc", 0, 8), 0.5, A.mult, C / 2, A.add, ORL)
-        copy(r("gt", 0, 128), r("st", 0, 304), r("ordl", 0, 8))
+        ts(r("ordl", 16, 32), r("jd", 0, C), C / 2, A.add, off=ORV)
+        copy(r("gt", 0, 128), r("st", 0, 304), r("ordl", 12, 20))
         turn(r("tg", 0, 128), r("gt", 0, 128))
-        ts(r("al%d" % t, 0, 32), r("tg", 0, 128), -FLAG, A.add, off=r("ko", 46, 48))
+        ts(r("al%d" % t, 0, 32), r("tg", 0, 128), MID, A.add, off=r("ko", 46, 48))
         send(2, t)
         copy(r("ab", 0, 64), r("tg", 0, 128), SELL)
-        tt(r("ab", 64, 80), r("ab", 32, 48), r("ab", 48, 64), A.subtract)
-        tt(r("ab", 80, 96), r("ab", 16, 32), r("ab", 0, 16), A.subtract)
-        tt(r("ab", 96, 112), r("ab", 64, 80), r("ab", 80, 96), A.mult)
-        tt(r("ab", 112, 128), r("ab", 96, 112), r("ab", 0, 16), A.add)
-        ts(r("bnl", 0, 16), r("ab", 112, 128), -FLAG, A.add)
-        act(r("bnr", 0, NZ), r("iob", 0, 304), F.Copy, off=r("bnl", 0, 16))
-        act(r("bns", 0, NS), r("bnr", 0, NZ), F.Copy, off=PERM)
+        tt(r("ab", 96, 128, 2), r("ab", 32, 48), r("ab", 48, 64), A.subtract)
+        tt(r("ab", 65, 96, 2), r("ab", 16, 32), r("ab", 0, 16), A.subtract)
+        act(r("ab", 97, 128, 2), r("ab", 0, 16), F.Copy)
+        scan(r("ab", 128, 160), r("ab", 64, 96), r("ab", 96, 128))
+        ts(r("bnl", 0, 16), r("ab", 129, 160, 2), MID, A.add)
+        copy(r("bnr", 0, NZ), r("iob", 0, 304), r("bnl", 0, 16))
         for k in range(18):
-            v = r("ea", NS * k, NS * k + NS)
+            v = r("ea", NE * k, NE * k + NE)
             if k in VE:
-                ts(v, r("bns", 0, NS), r("kf", 44 + k, 45 + k), A.not_equal, 512.0, A.mult)
+                ts(v, r("bnr", 0, NE), r("kf", 44 + k, 45 + k), A.not_equal, 512.0, A.mult)
             else:
-                act(v, r("bns", 0, NS), F.Abs, r("kf", 26 + k, 27 + k), 512.0)
-            scan(r("eo", NS * k, NS * k + NS), r("dl", 0, NS), v, 1024.0, A.add, A.min)
-        E = r("eo", NS - 1, 18 * NS, NS)
-        ts(r("ki", 48, 66), E, float(NS), A.min)
-        ts(r("kf", 120, 138), E, float(NS), A.min, 64.0, A.mult)
+                act(v, r("bnr", 0, NE), F.Abs, r("kf", 26 + k, 27 + k), 512.0)
+            scan(r("eo", NE * k, NE * k + NE), r("dl", 0, NE), v, 1024.0, A.add, A.min)
+        E = r("eo", NE - 1, 18 * NE, NE)
+        ts(r("ki", 48, 66), E, 1.0, A.min, NS - 1.0, A.add)
+        ts(r("kf", 120, 138), E, 1.0, A.min, 64.0, A.mult)
         ts(r("ki", 66, 84), r("ki", 48, 66), 2, A.logical_shift_right)
-        ts(r("kf", 138, 156), r("ki", 66, 84), -255.0, A.mult)
+        ts(r("kf", 138, 156), r("ki", 66, 84), -255.0, A.mult, 64.0 * (NS - 1), A.add)
         tt(r("em", 0, 18), r("kf", 120, 138), r("kf", 138, 156), A.add)
         copy(r("el", 0, 18), r("em", 0, 18))
         o = 288
-        ts(r("q3", o, o + 18), role("tb", 0), FLAG / 2, A.is_ge)
+        ts(r("q3", o, o + 18), role("tb", 0), -FLAG / 2, A.is_ge)
         tt(r("q3", o + 18, o + 36), r("q3", o, o + 18), role("mt", 7), A.mult)
         tt(r("q3", o + 36, o + 54), r("q3", o, o + 18), r("q3", o + 18, o + 36), A.subtract)
         tt(r("q3", o + 54, o + 72), role("tb", 3), role("tb", 0), A.subtract)
@@ -472,8 +517,8 @@ def rank_program(g, core, T, topo):
         tt(r("dk", 18, 36), r("q3", o + 72, o + 90), r("q3", o + 36, o + 54), A.mult)
         dma("y", "db%d" % t, T.dk[16:128, 36:72], T.dk[0:112, 0:36], [r("dk", 0, 36)], [r("dk", 36, 72)])
         dma("y", "dc%d" % t, T.dk[0:112, 72:108], T.dk[16:128, 0:36], [r("dk", 0, 36)], [r("dk", 72, 108)])
-        ts(THR, r("acc", 8, 9), 0.5, A.mult, C / 2, A.add)
-        ts(r("tk", 0, 48), r("pos", 0, 32), THR, A.is_le, off=TKL)
+        ts(THR, r("acc", 8, 9), 0.5, A.mult, C / 2 - FAR, A.add)
+        ts(r("tk", 0, 48), r("po", 0, C), THR, A.is_le, off=TKL)
         tt(r("tk", 48, 96), r("dk", 0, 108), r("tk", 0, 48), A.mult, DKL)
         tt(r("lf", 0, 36), r("lf", 0, 36), r("tk", 48, 84), A.add)
         copy(r("ll", 0, 36), r("lf", 0, 36))
@@ -481,26 +526,34 @@ def rank_program(g, core, T, topo):
             copy(r("fb", 1, 36, 2), r("lf", 0, 18))
             tt(r("fa", 1, 36, 2), r("lf", 18, 36), r("lf", 0, 18), A.subtract)
         else:
-            act(r("lof", 0, 2 * C), r("iof", 0, 304), F.Copy, off=r("ll", 0, 36))
+            act(r("lof", 0, 2 * C), r("iob", 0, 304), F.Identity, MID, off=r("ll", 0, 36))
             dma("y", "done", T.ol[:, :], T.lof[0:128:16, :], [r("lof", 0, 2 * C)], [])
         for b in range(4):
             mm("bf%d" % b, C, "eq", "es", 128 * b, "yq%d" % t, "ys%d" % t, 0)
             act(r("fh", 304 * b, 304 * b + C), r("bf%d" % b, 0, C), F.Copy, None, 0.5)
         for b in range(4):
             HB = r("fh", 304 * b, 304 * b + 304)
-            act(r("ga", NZ * b, NZ * b + NZ), HB, F.Copy, off=r("ysl%d" % t, 0, 16))
-            tt(r("zt", b, 4 * NZ, 4), HB, r("ga", NZ * b, NZ * b + NZ), A.add, r("ysl%d" % t, 16, 32))
+            for lo, hi in ((0, 16),) if b else ((0, FIRST), (FIRST, 16)):
+                act(r("ga", NZ * b + 16 * lo, NZ * b + 16 * hi), HB, F.Copy, off=r("ysl%d" % t, lo, hi))
+                tt(r("zt", 64 * lo + b, 64 * hi, 4), HB, r("ga", NZ * b + 16 * lo, NZ * b + 16 * hi), A.add, r("ysl%d" % t, 16 + lo, 16 + hi))
         quant("zq", "zs", 0, NZ, r("zt", 0, 4 * NZ))
         for b in range(4):
             mm(BANKS[b], NZ, "wq", "wp", 128 * b, "zq", "zs", 0)
             act(r("hs", NZ * b, NZ * b + NZ), r(BANKS[b], 0, NZ), F.Copy, None, 0.03125)
-            tt(r("xt", b, 4 * C, 4), r("hs", NZ * b, NZ * b + NZ), r("ff", C * b, C * b + C), A.add, r("el", 0, 18))
+            if b < KEPT:
+                tt(r("xt", b, 4 * C, 4), r("hs", NZ * b, NZ * b + NZ), r("ff", C * b, C * b + C), A.add, r("el", 0, 18))
+            else:
+                act(r("gp", 0, C), r("hs", NZ * b, NZ * b + NZ), F.Copy, off=r("el", 0, 18))
+                mm("bf%d" % b, C, "eq", "es", 128 * b, XQ, XS, 0)
+                tt(r("xt", b, 4 * C, 4), r("bf%d" % b, 0, C), r("gp", 0, C), A.add)
 
     quant("xq3", "xs3", 0, C, r("xt", 0, 4 * C))
-    mm("bv", C, "vq", "vs", 0, "xq3", "xs3", 0)
-    act(r("yo", 0, C), r("bv", 0, C), F.Copy)
+    mm("bv", C // 2, "vq", "vs", 0, "xq3", "xs3", 0)
+    mm("bs", C // 2, "vq", "vs", 0, "xq3", "xs3", C // 2)
+    copy(r("yo", 0, C // 2), r("bv", 0, C // 2))
+    act(r("yo", C // 2, C), r("bs", 0, C // 2), F.Copy)
     dma("y", "done", T.oc[:, :], T.xq3[:, 0:C].bitcast(dt.uint8), [r("xq3", 0, C)], [])
     for k in range(4):
         dma("ys"[k % 2], "done", T.osc[4 * k:4 * k + 4, :], T.xs3[32 * k:32 * k + 4, 0:C], [r("xs3", 0, C)], [])
-    dma("s", "done", T.y[:, :], T.yo[:, :], [r("yo", 0, C)], [])
+    dma("y", "done", T.y[:, :], T.yo[:, :], [r("yo", 0, C)], [])
     issue()

@@ -4,6 +4,7 @@ from concourse.mybir import dt, AluOpType, AxisListType, ActivationFunctionType
 C, L, M, R = 288, 4, 56, 3
 NS = L * M
 NZ = 256
+HALF = C // 2
 NE = 248
 FLAG = 2.0 ** 20
 FAR = 1024.0
@@ -15,7 +16,7 @@ zq:256:c zs:256:p xq3:288:c xs3:288:p sg:3840:b junk:2464:b jc:1440:b
 pi:16:i pf:32 iob:304:b j16:288:b mask16:288:b keep:288:b ci:288:b cj:288:b io:1152 ki:160:i kf:180 ko:160:o li:36:i
 ll:36:o lf:36 fa:36 fb:36 fc:36 cl:18:o sm:288 so:288 sr:288 sb:288 ww:864 pq:576 tpq:576 ne:288:b ij:576:b q3:400 mt:288 tb:288:b
 tr:288:b st:304:b fl:288:b cn:288:b acc:16 ordl:32:o gt:128:b tg:128:b jd:288:b rsum:36 sm2:288 po:288 cap:288 gp:288 pl:18:o ab:160 bnl:16:o bnr:256:b
-dl:248:b ea:4464:b eo:4464:b el:18:o em:18 dk:108 tk:96 lof:576"""
+dl:250:b ea:4500:b eo:4500:b ks:256 tabk:304 slot:256 el:18:o em:18 dk:108 tk:96 lof:576"""
 for _t in range(R):
     _BUFS += " xq%d:288:c xs%d:288:p al%d:32:o hq%d:288:c hs_%d:288:p hsl%d:32:o yq%d:288:c ys%d:288:p ysl%d:32:o" % ((_t,) * 9)
 _DT = {"b": "bfloat16", "c": "float8_e4m3fn_x4", "p": "uint8", "i": "int32", "o": "uint16", "f": "float32"}
@@ -31,15 +32,16 @@ SEMAPHORES = (["qv", "qs", "qt", "qg", "left", "dx", "du", "dn", "dw", "dp", "dv
               + [p + k + str(t) for p in ("got", "rel") for k in "qsl" for t in range(R)] + ["d" + k + str(t) for k in "abc" for t in range(R)])
 
 KEPT = 3
-FIRST = 6
+FIRST = 2
 VC = (9, 10, 11)
 VE = (1, 3, 5, 7, 9, 11, 13, 15)
 PAIRS = sorted([(i, j) for i in range(L) for j in range(L) if i + j], key=lambda e: (e[0] + e[1], e[0]))[::-1]
 ROW = 7
 TILES = [(0, 288, (17, 16)), (288, 240, (15, 14, 13, 12)), (528, 176, (11, 10, 9, 8)), (704, 128, (7, 6, 5, 4)), (832, 128, (3, 2, 1))]
 
-CYC, PICK, SCAT, ACT, WAKE, TRIP, LOAD = 1.0e-3, 1.5e-3, 3.5e-3, 0.02, 0.2, (8.0, 8.0, 3.4), 2.2
-NEAR, TURNS, TRIES, SPREAD, SOME = 0.05, 20, 1000, 0.2, 0.1
+CYC, PICK, SCAT, ACT, WAKE, TRIP, LOAD = 1.0e-3, 1.5e-3, 3.5e-3, 0.02, 0.2, (8.0, 8.0, 3.6), 2.2
+NEAR, TURNS, TRIES, SPREAD, SOME = 0.05, 20, 4000, 0.4, 0.02
+CASES = ((0.4, 1.0, 1.0, 0.2), (0.4, 0.87, 0.85, 0.2), (1.3, 1.15, 1.25, 0.25))
 
 
 def _relays(core, dst, topo):
@@ -129,11 +131,47 @@ def _order(nodes):
         o = _list_order(nodes, users, list(other))
         if o[2] <= best[2]:
             best, rank = o, other
+    cases = []
+    for late, pace, picks, wake in CASES:
+        occ = [(n["occ"] + (picks - 1.0) * n["pick"]) * pace for n in nodes]
+        cases.append(([[(d, wake if w else 0.0) for d, w in n["deps"].items()] for n in nodes], occ,
+                      [n["lat"] + (late if n["q"] == "net" else 0.0) for n in nodes], 1.0 / pace))
+    which = ["vstgy".find(n["q"]) for n in nodes]
+
+    def ends(o):
+        s = o[2]
+        for edges, occ, lat, weight in cases:
+            done, free = [0.0] * len(nodes), [0.0] * 6
+            for i in o[0]:
+                at = free[which[i]]
+                for d, w in edges[i]:
+                    if done[d] + w > at:
+                        at = done[d] + w
+                free[which[i]] = at = at + occ[i]
+                done[i] = at + lat[i]
+            s += max(done) * weight
+        return s
+
+    least = ends(best)
     for k in range(TRIES):
-        other = rank + rng.normal(0.0, SPREAD, len(nodes)) * (rng.random(len(nodes)) < SOME)
-        o = _list_order(nodes, users, list(other))
-        if o[2] <= best[2]:
-            best, rank = o, other
+        if k % 2:
+            other = list(rank + rng.normal(0.0, SPREAD, len(nodes)) * (rng.random(len(nodes)) < SOME))
+        else:
+            other = list(rank)
+            for i in rng.integers(0, len(nodes), 3):
+                other[i] += rng.random() * 4 * SPREAD
+                todo = [i]
+                while todo:
+                    j = todo.pop()
+                    for d in nodes[j]["deps"]:
+                        if other[d] <= other[j]:
+                            other[d] = other[j] + 0.01
+                            todo.append(d)
+        o = _list_order(nodes, users, other)
+        other = np.array(other)
+        s = ends(o)
+        if s <= least:
+            best, rank, least = o, other, s
     _ORDERS[key] = best[0]
     return best[0]
 
@@ -147,6 +185,7 @@ def rank_program(g, core, T, topo):
     F = ActivationFunctionType
     queue = {"v": g.vector, "s": g.scalar, "t": g.tensor, "g": g, "y": g.sync}
     qsem = {"v": "qv", "s": "qs", "t": "qt", "g": "qg"}
+    picked = [0.0]
     nodes, log = [], {}
 
     def call(q, fn, rd, wr, occ=0.06, lat=0.0, sem=None, n=1):
@@ -166,7 +205,8 @@ def rank_program(g, core, T, topo):
                 if w:
                     old = [a for a in old if not (lo <= a["lo"] and a["hi"] <= hi and (st == 1 or (a["st"] == st and (a["lo"] - lo) % st == 0)))]
                 log[name] = old + [{"lo": lo, "hi": hi, "st": st, "q": q, "c": sem is None, "w": w, "i": i}]
-        nodes.append({"q": q, "fn": fn, "deps": deps, "occ": occ, "lat": lat, "sem": sem, "n": n})
+        nodes.append({"q": q, "fn": fn, "deps": deps, "occ": occ, "lat": lat, "sem": sem, "n": n, "pick": picked[0]})
+        picked[0] = 0.0
         return i
 
     def issue():
@@ -199,8 +239,11 @@ def rank_program(g, core, T, topo):
         for s in count:
             g.wait_ge(T.sem[s], count[s])
 
-    def dma(q, sem, out, in_, rd, wr):
-        call(q, lambda: queue[q].dma_start(out, in_), rd, wr, 0.06, LOAD, sem, 16)
+    def dma(q, sem, out, in_, rd, wr, after=()):
+        i = call(q, lambda: queue[q].dma_start(out, in_), rd, wr, 0.06, LOAD, sem, 16)
+        for d in after:
+            nodes[i]["deps"][d] = True
+        return i
 
     def r(name, lo, hi, st=1):
         name, o = PART.get(name, (name, 0))
@@ -215,7 +258,8 @@ def rank_program(g, core, T, topo):
         return max(64, per * len(range(v[1], v[2], v[3]))) * CYC
 
     def cost(out, off, per):
-        return 0.05 + PICK * len(range(out[1], out[2], out[3])) if off else wide(out, per)
+        picked[0] = PICK * len(range(out[1], out[2], out[3])) if off else 0.0
+        return 0.05 + picked[0] if off else wide(out, per)
 
     def side(in_, off):
         return ap(in_) if off is None else ap(in_).indirect(ap(off))
@@ -250,8 +294,8 @@ def rank_program(g, core, T, topo):
     def iota(out, pattern, base, cm):
         call("g", lambda: g.iota(ap(out), pattern, base, cm), [], [out], 0.13 + 2 * CYC * len(range(out[1], out[2], out[3])))
 
-    def select(v, pattern, op, base, cm):
-        call("g", lambda: g.affine_select(ap(v), ap(v), pattern, op, 0.0, base, cm), [v], [v], 0.17 + 2 * CYC * len(range(v[1], v[2], v[3])))
+    def select(v, pattern, op, base, cm, in_=None):
+        call("g", lambda: g.affine_select(ap(v), ap(in_ or v), pattern, op, 0.0, base, cm), [in_ or v], [v], 0.17 + 2 * CYC * len(range(v[1], v[2], v[3])))
 
     def turn(out, in_):
         call("v", lambda: g.vector.transpose(ap(out), ap(in_)), [in_], [out], wide(out))
@@ -280,7 +324,6 @@ def rank_program(g, core, T, topo):
     dma("y", "du", T.ut[:, :], T.u[:, :], [], [r("ut", 0, 512)])
     dma("s", "dx", T.xt[:, :], T.x[:, :], [], [r("xt", 0, 4 * C)])
     dma("y", "dn", T.li[:, :], T.nb[:, :], [], [r("li", 0, 36)])
-    LATER = [r("uq", 0, 128), r("xq0", 0, C)]
 
     iota(r("pi", 0, 1), [[0, 1]], 0, 1)
     for k, (sh, mask) in enumerate(((0, 15), (0, 16), (4, 7), (0, 3), (2, 3), (0, 1), (4, 1), (1, 7))):
@@ -337,11 +380,11 @@ def rank_program(g, core, T, topo):
     ts(r("kf", 64, 68), r("kf", 0, 4), Q, A.add, 0.5, A.add)
     ts(r("kf", 68, 72), r("kf", 64, 68), float(M), A.is_ge, 1000.0, A.mult)
     tt(r("kf", 156, 160), r("kf", 64, 68), r("kf", 68, 72), A.add)
-    ts(r("kf", 20, 24), r("kf", 156, 160), FLAG, A.mult)
-    fill(r("kf", 24, 25), (M - 0.5) * FLAG)
-    fill(r("fl", 0, C), FLAG)
+    act(r("kf", 20, 24), r("kf", 156, 160), F.Copy, None, FLAG)
+    act(r("kf", 24, 25), Q, F.Identity, (M - 0.5) * FLAG, 0.0)
+    gfill(r("fl", 0, C), int(FLAG))
     ts(NC, K16, Q, A.add, -MID, A.add)
-    ts(NB, NC, -512.0, A.mult)
+    act(NB, NC, F.Copy, None, -512.0)
     JJ = r("kf", 100, 103)
     ts(JJ, r("kf", 0, 3), Q, A.add)
     ts(r("pf", 21, 22), H, -34.0, A.mult, 71.0, A.add)
@@ -352,24 +395,28 @@ def rank_program(g, core, T, topo):
     tt(r("kf", 112, 115), r("kf", 104, 107), r("kf", 108, 111), A.add)
     tt(r("kf", 116, 119), r("kf", 112, 115), JJ, A.add)
     ts(TKL, r("kf", 116, 119), 16.0, A.mult, 15.0, A.add)
-    fill(r("dk", 0, 108), 0.0)
-    ts(r("cap", 0, C), r("mask16", 0, C), FAR, A.mult)
-    ts(r("kf", 160, 178), K16, -FAR, A.add)
-    ts(r("pf", 24, 25), Q, 0.0, A.not_equal)
-    ts(r("pf", 25, 26), Q, 0.0, A.is_equal)
-    ts(r("pf", 26, 28), r("mask16", 0, 2), FAR, A.mult)
-    fill(r("acc", 0, 16), 0.0)
-    fill(r("rsum", 0, 1), 0.0)
+    gfill(r("dk", 0, 108), 0)
+    act(r("cap", 0, C), r("mask16", 0, C), F.Copy, None, FAR)
+    act(r("kf", 160, 178), K16, F.Identity, -FAR)
+    act(r("pf", 24, 25), r("mask16", 0, 1), F.Identity, -1.0)
+    act(r("pf", 25, 26), r("mask16", 0, 1), F.Copy, None, -1.0)
+    act(r("pf", 26, 30), r("mask16", 0, 4), F.Copy, None, FAR)
+    act(r("pf", 30, 31), r("mask16", 2, 3), F.Identity, 1.0, -1.0)
+    act(r("pf", 31, 32), r("mask16", 2, 3), F.Copy)
+    for e in range(2):
+        act(r("cap", 2 + e, C, 16), r("kf", 160, 178), F.Identity, r("pf", 28 + e, 29 + e), r("pf", 30 + e, 31 + e))
+    gfill(r("acc", 0, 16), 0)
+    gfill(r("rsum", 0, 1), 0)
     gfill(r("jt", 0, 528), 1)
     select(r("jt", 0, 520), [[-1, 520]], A.is_equal, 3, 4)
     for b in range(4):
         quant("eq", "es", 128 * b, 128 * b + 128, r("jt", 3 - b, 515 - b))
         gfill(r("fh", 304 * b + C, 304 * b + 304), 0)
-    giota(r("rt", 512, 1024), [[1, 8], [0, 64]], 0)
-    ts(r("rt", 512, 1024), r("rt", 512, 1024), GRP, A.is_equal)
-    act(r("rt", 0, 512), r("rt", 512, 1024), F.Copy)
-    select(r("rt", 2, 512, 4), [[-1, 128]], A.is_gt, 0, 1)
-    select(r("rt", 3, 512, 4), [[1, 128]], A.is_gt, 0, -1)
+    giota(r("gt", 0, 128), [[1, 8], [0, 16]], 0)
+    for e in (512, 513, 514, 515, 0, 1):
+        ts(r("rt", e, e // 4 * 4 + 512, 4), r("gt", 0, 128), GRP, A.is_equal)
+    select(r("rt", 2, 512, 4), [[-1, 128]], A.is_gt, 0, 1, r("rt", 512, 1024, 4))
+    select(r("rt", 3, 512, 4), [[1, 128]], A.is_gt, 0, -1, r("rt", 512, 1024, 4))
     quant("rq", "rs", 0, 256, r("rt", 0, 1024))
     for lo, n, blocks in TILES[:3]:
         fill(r("sg", 4 * (lo + 16 * blocks[-1]), 4 * (lo + n)), 0.0)
@@ -379,6 +426,10 @@ def rank_program(g, core, T, topo):
     gfill(r("st", C, 304), C - int(MID))
     gfill(r("dl", 0, NE), -4)
     gfill(r("dl", 64, NE, 64), 251)
+    gfill(r("dl", NE, NE + 1), NS - 1)
+    gfill(r("ea", NE, 18 * (NE + 2), NE + 2), 1024)
+    giota(r("slot", 0, NZ), [[1, 4], [4, 64]], 0)
+    act(r("tabk", 0, 304), r("iob", 0, 304), F.Copy, None, 512.0)
     gfill(r("ab", 64, 96, 2), 0)
 
     n_of = len(T.cores)
@@ -387,37 +438,41 @@ def rank_program(g, core, T, topo):
     hops = [dst] * 3 if direct else _relays(core, dst, topo)
     came = [src] * 3 if topo.may_write(src, core) else _relays(src, core, topo)
 
-    def send(k, t):
+    def send(k, t, after=()):
         rid, pid = topo.addr(hops[k], core)
         name, n = (("xq%d", C), ("xs%d", C), ("al%d", 32))[k]
         i = call("g", lambda: g.remote_dma(_piece(T, "y" if direct else "h", k, t), _piece(T, "x", k, t), T.sem[("got" if direct else "rel") + "qsl"[k] + str(t)], T.sem.left, pid, rid, topo.mask(core, hops[k])),
                  [r(name % t, 0, n)], [], 0.5, 0.0, "left", len(topo.engines(core, hops[k])))
+        for d in after:
+            nodes[i]["deps"][d] = True
         far = call("net", None, [], [r(("yq%d", "ys%d", "ysl%d")[k] % t, 0, n)], 0.0, TRIP[k], "got" + "qsl"[k] + str(t), len(topo.engines(came[k], core)))
         nodes[far]["deps"][i] = True
 
     for t in range(R):
         XQ, XS = "xq%d" % t, "xs%d" % t
-        quant(XQ, XS, 0, C, r("xt", 0, 4 * C))
-        if t == 0:
-            dma("y", "dw", T.wq[:, :].bitcast(dt.uint8), T.wc[:, :], LATER, [r("wq", 0, 512)])
-            dma("y", "dp", T.wp[:, :], T.ws[:, :], LATER, [r("wp", 0, 512)])
-            dma("y", "dv", T.vt[:, :], T.v[:, :], LATER, [r("vt", 0, 512)])
-            quant("vq", "vs", 0, 128, r("vt", 0, 512))
-        for k in range(2):
-            send(k, t)
+        for lo, bank in ((HALF, "bk"), (0, "bx")):
+            quant(XQ, XS, lo, lo + HALF, r("xt", 4 * lo, 4 * (lo + HALF)))
+            mm(bank, HALF, "urq", "urs", 0, XQ, XS, lo)
+            tt(r("sm", lo, lo + HALF), r(bank, 0, HALF), r("mask16", 0, HALF), A.mult)
+            scan(r("so", lo, lo + HALF), r("keep", 0, HALF), r("sm", lo, lo + HALF))
         mm("bv", C, "urq", "urs", 0, XQ, XS, 0)
         mm("bs", C, "urq", "urs", 0, XQ, XS, 0)
         for b in range(KEPT):
             mm("bf%d" % b, C, "eq", "es", 128 * b, XQ, XS, 0)
             act(r("ff", C * b, C * b + C), r("bf%d" % b, 0, C), F.Copy)
-        tt(r("sm", 0, C), r("bv", 0, C), r("mask16", 0, C), A.mult)
-        scan(r("so", 0, C), r("keep", 0, C), r("sm", 0, C))
         ts(r("fb", 0, 36, 2), r("so", 15, C, 16), 0.0, A.is_gt)
         scan(r("fc", 0, 36), r("fa", 0, 36), r("fb", 0, 36))
         CL = r("cl", 0, 18)
         copy(CL, r("fc", 1, 36, 2))
         act(r("sr", 0, C), r("bs", 0, C), F.Copy)
-        dma("y", "da%d" % t, T["io"][0:128:16, 0:C], T.sr[0:128:16, 0:C], [r("sr", 0, C)], [r("io", 0, C)])
+        LATER = [dma("y", "da%d" % t, T["io"][0:128:16, 0:C], T.sr[0:128:16, 0:C], [r("sr", 0, C)], [r("io", 0, C)])]
+        if t == 0:
+            dma("y", "dw", T.wq[:, :].bitcast(dt.uint8), T.wc[:, :], [], [r("wq", 0, 512)], LATER)
+            dma("y", "dp", T.wp[:, :], T.ws[:, :], [], [r("wp", 0, 512)], LATER)
+            dma("y", "dv", T.vt[:, :], T.v[:, :], [], [r("vt", 0, 512)], LATER)
+            quant("vq", "vs", 0, 128, r("vt", 0, 512))
+        for k in range(2):
+            send(k, t, LATER)
         act(r("sb", 0, C), r("so", 0, C), F.Copy, off=SBL)
         tt(r("sg", 2, 4 * C, 4), r("bv", 0, C), r("sb", 0, C), A.is_lt)
         tt(r("sg", 3, 4 * C, 4), r("bv", 0, C), r("sb", 0, C), A.is_le)
@@ -435,11 +490,11 @@ def rank_program(g, core, T, topo):
         quant("fq", "fs", 704, 880, r("sg", 4 * 704, 4 * 880))
         for x, (lo, n, blocks) in enumerate(TILES):
             mm("bk", n, "rq", "rs", 128 if x else 0, "fq", "fs", lo, x == 0, x == 4)
-        tt(r("rsum", 18, 36), r("kf", 160, 178), r("rsum", 0, 18), A.subtract)
         for e in range(2):
-            ts(r("cap", e, C, 16), r("rsum", 18, 36), r("pf", 24 + e, 25 + e), A.mult, r("pf", 26 + e, 27 + e), A.add)
-        tt(r("sm2", 0, C), r("bk", 0, C), r("cap", 0, C), A.min)
-        scan(r("po", 0, C), r("keep", 0, C), r("sm2", 0, C))
+            act(r("cap", e, C, 16), r("rsum", 0, 18), F.Identity, r("pf", 26 + e, 27 + e), r("pf", 24 + e, 25 + e))
+        for lo in (0, HALF):
+            tt(r("sm2", lo, lo + HALF), r("bk", lo, lo + HALF), r("cap", lo, lo + HALF), A.min)
+            scan(r("po", lo, lo + HALF), r("keep", 0, HALF), r("sm2", lo, lo + HALF))
         ts(r("pl", 0, 18), r("po", 15, C, 16), FAR, A.add)
         tt(r("w1", 0, C), r("io", 3 * C, 4 * C), r("io", 2 * C, 3 * C), A.add, CL)
         tt(r("w2", 0, C), r("w1", 0, C), r("io", C, 2 * C), A.add, CL)
@@ -473,6 +528,7 @@ def rank_program(g, core, T, topo):
         tt(role("mt", 0), r("q3", 252, 270), r("q3", 270, 288), A.add)
         scan(r("tb", 0, C), r("keep", 0, C), r("mt", 0, C))
         turn(r("tr", 0, C), r("tb", 0, C))
+        picked[0] = SCAT * C
         call("v", lambda: g.vector.tensor_copy(T.st[:, 0:C].indirect(T.pl[:, 0:18]), T.tr[:, 0:C]), [r("tr", 0, C), r("pl", 0, 18)], [r("st", 0, C)], 0.05 + SCAT * C)
         scan(r("cn", 0, C), r("st", 0, C), r("fl", 0, C), 0.0, A.add, A.add)
         for c in (0, 1, 4):
@@ -482,7 +538,8 @@ def rank_program(g, core, T, topo):
             scan(r("jd", 144 * c - C, 144 * c - 144), r("jc", C * c, C * c + 144), r("jc", C * c + 144, C * c + C), 0.0, A.add, A.add)
         ts(r("ordl", 0, 16), r("acc", 0, 8), 0.5, A.mult, C / 2, A.add, ORL)
         ts(r("ordl", 16, 32), r("jd", 0, C), C / 2, A.add, off=ORV)
-        copy(r("gt", 0, 128), r("st", 0, 304), r("ordl", 12, 20))
+        act(r("gt", 0, 64), r("st", 0, 304), F.Copy, off=r("ordl", 12, 16))
+        copy(r("gt", 64, 128), r("st", 0, 304), r("ordl", 16, 20))
         turn(r("tg", 0, 128), r("gt", 0, 128))
         ts(r("al%d" % t, 0, 32), r("tg", 0, 128), MID, A.add, off=r("ko", 46, 48))
         send(2, t)
@@ -492,19 +549,21 @@ def rank_program(g, core, T, topo):
         act(r("ab", 97, 128, 2), r("ab", 0, 16), F.Copy)
         scan(r("ab", 128, 160), r("ab", 64, 96), r("ab", 96, 128))
         ts(r("bnl", 0, 16), r("ab", 129, 160, 2), MID, A.add)
-        copy(r("bnr", 0, NZ), r("iob", 0, 304), r("bnl", 0, 16))
+        act(r("bnr", 0, NZ), r("iob", 0, 304), F.Copy, off=r("bnl", 0, 16))
+        tt(r("ks", 0, NZ), r("tabk", 0, 304), r("slot", 0, NZ), A.add, r("bnl", 0, 16))
         for k in range(18):
-            v = r("ea", NE * k, NE * k + NE)
+            o = (NE + 2) * k
             if k in VE:
-                ts(v, r("bnr", 0, NE), r("kf", 44 + k, 45 + k), A.not_equal, 512.0, A.mult)
+                ts(r("ea", o, o + NE), r("bnr", 0, NE), r("kf", 44 + k, 45 + k), A.not_equal, 512.0, A.mult)
+                scan(r("eo", o, o + NE + 1), r("dl", 0, NE + 1), r("ea", o, o + NE + 1), 1024.0, A.add, A.min)
             else:
-                act(v, r("bnr", 0, NE), F.Abs, r("kf", 26 + k, 27 + k), 512.0)
-            scan(r("eo", NE * k, NE * k + NE), r("dl", 0, NE), v, 1024.0, A.add, A.min)
-        E = r("eo", NE - 1, 18 * NE, NE)
-        ts(r("ki", 48, 66), E, 1.0, A.min, NS - 1.0, A.add)
-        ts(r("kf", 120, 138), E, 1.0, A.min, 64.0, A.mult)
+                act(r("ea", o, o + NE), r("ks", 0, NE), F.Abs, r("kf", 26 + k, 27 + k))
+                scan(r("eo", o + NE // 2 + 1, o + NE + 1), r("ea", o, o + NE // 2), r("ea", o + NE // 2, o + NE), 1024.0, A.min, A.min)
+        E = r("eo", NE, 18 * (NE + 2), NE + 2)
+        ts(r("ki", 48, 66), E, float(NS), A.min)
+        ts(r("kf", 120, 138), E, float(NS), A.min, 64.0, A.mult)
         ts(r("ki", 66, 84), r("ki", 48, 66), 2, A.logical_shift_right)
-        ts(r("kf", 138, 156), r("ki", 66, 84), -255.0, A.mult, 64.0 * (NS - 1), A.add)
+        ts(r("kf", 138, 156), r("ki", 66, 84), -255.0, A.mult)
         tt(r("em", 0, 18), r("kf", 120, 138), r("kf", 138, 156), A.add)
         copy(r("el", 0, 18), r("em", 0, 18))
         o = 288
@@ -533,13 +592,20 @@ def rank_program(g, core, T, topo):
             act(r("fh", 304 * b, 304 * b + C), r("bf%d" % b, 0, C), F.Copy, None, 0.5)
         for b in range(4):
             HB = r("fh", 304 * b, 304 * b + 304)
-            for lo, hi in ((0, 16),) if b else ((0, FIRST), (FIRST, 16)):
-                act(r("ga", NZ * b + 16 * lo, NZ * b + 16 * hi), HB, F.Copy, off=r("ysl%d" % t, lo, hi))
-                tt(r("zt", 64 * lo + b, 64 * hi, 4), HB, r("ga", NZ * b + 16 * lo, NZ * b + 16 * hi), A.add, r("ysl%d" % t, 16 + lo, 16 + hi))
-        quant("zq", "zs", 0, NZ, r("zt", 0, 4 * NZ))
+            act(r("ga", NZ * b, NZ * b + 192), HB, F.Copy, off=r("ysl%d" % t, 0, 12))
+            tt(r("zt", b, 768, 4), HB, r("ga", NZ * b, NZ * b + 192), A.add, r("ysl%d" % t, 16, 28))
+            if b < FIRST:
+                ts(r("zt", 768 + b, 4 * NZ, 4), HB, 2.0, A.mult, off=r("ysl%d" % t, 12, 16))
+            else:
+                act(r("zt", 768 + b, 4 * NZ, 4), HB, F.Copy, None, 2.0, r("ysl%d" % t, 12, 16))
+        for lo, bank in ((0, "bf0"), (128, "bf1")):
+            quant("zq", "zs", lo, lo + 128, r("zt", 4 * lo, 4 * lo + 512))
+            mm(bank, 128, "wq", "wp", 0, "zq", "zs", lo)
+            act(r("hs", lo, lo + 128), r(bank, 0, 128), F.Copy, None, 0.03125)
         for b in range(4):
-            mm(BANKS[b], NZ, "wq", "wp", 128 * b, "zq", "zs", 0)
-            act(r("hs", NZ * b, NZ * b + NZ), r(BANKS[b], 0, NZ), F.Copy, None, 0.03125)
+            if b:
+                mm(BANKS[b - 1], NZ, "wq", "wp", 128 * b, "zq", "zs", 0)
+                act(r("hs", NZ * b, NZ * b + NZ), r(BANKS[b - 1], 0, NZ), F.Copy, None, 0.03125)
             if b < KEPT:
                 tt(r("xt", b, 4 * C, 4), r("hs", NZ * b, NZ * b + NZ), r("ff", C * b, C * b + C), A.add, r("el", 0, 18))
             else:
@@ -547,11 +613,11 @@ def rank_program(g, core, T, topo):
                 mm("bf%d" % b, C, "eq", "es", 128 * b, XQ, XS, 0)
                 tt(r("xt", b, 4 * C, 4), r("bf%d" % b, 0, C), r("gp", 0, C), A.add)
 
-    quant("xq3", "xs3", 0, C, r("xt", 0, 4 * C))
-    mm("bv", C // 2, "vq", "vs", 0, "xq3", "xs3", 0)
-    mm("bs", C // 2, "vq", "vs", 0, "xq3", "xs3", C // 2)
-    copy(r("yo", 0, C // 2), r("bv", 0, C // 2))
-    act(r("yo", C // 2, C), r("bs", 0, C // 2), F.Copy)
+    for lo, bank in ((0, "bk"), (HALF, "bx")):
+        quant("xq3", "xs3", lo, lo + HALF, r("xt", 4 * lo, 4 * (lo + HALF)))
+        mm(bank, HALF, "vq", "vs", 0, "xq3", "xs3", lo)
+    act(r("yo", 0, HALF), r("bk", 0, HALF), F.Copy)
+    copy(r("yo", HALF, C), r("bx", 0, HALF))
     dma("y", "done", T.oc[:, :], T.xq3[:, 0:C].bitcast(dt.uint8), [r("xq3", 0, C)], [])
     for k in range(4):
         dma("ys"[k % 2], "done", T.osc[4 * k:4 * k + 4, :], T.xs3[32 * k:32 * k + 4, 0:C], [r("xs3", 0, C)], [])

import numpy as np
from concourse.mybir import dt, AluOpType, AxisListType, ActivationFunctionType

C, L, M, R = 288, 4, 56, 3
NS = L * M
NZ = 256
HALF = C // 2
NE = 248
FLAG = 2.0 ** 20
FAR = 1024.0
MID = 144.0

_BUFS = """xt:1152:b ut:512:b uq:128:c us:128:p urq:128:c urs:128:p vt:512:b vq:128:c vs:128:p wq:512:c wp:512:p
jt:528:b eq:512:c es:512:p rt:1024:b rq:256:c rs:256:p fq:960:c fs:960:p zt:1024:b fh:1216:b ff:1152:b ga:1024:b hs:1088 yo:288
zq:256:c zs:256:p xq3:288:c xs3:288:p sg:3840:b junk:2464:b jc:1440:b
pi:16:i pf:32 iob:304:b j16:288:b mask16:288:b keep:288:b ci:288:b cj:288:b io:1152 ki:160:i kf:180 ko:160:o li:36:i
ll:36:o lf:36 fa:36 fb:36 fc:36 cl:18:o sm:288 so:288 sr:288 sb:288 ww:864 pq:576 tpq:576 ne:288:b ij:576:b q3:400 mt:288 tb:288:b
tr:288:b st:304:b fl:288:b cn:288:b acc:16 ordl:32:o gt:128:b tg:128:b jd:288:b rsum:36 sm2:288 po:288 cap:288 gp:288 pl:18:o ab:160 bnl:16:o bnr:256:b
dl:250:b ea:4500:b eo:4500:b ks:256 tabk:304 slot:256 el:18:o em:18 dk:108 tk:96 lof:576"""
for _t in range(R):
    _BUFS += " xq%d:288:c xs%d:288:p al%d:32:o hq%d:288:c hs_%d:288:p hsl%d:32:o yq%d:288:c ys%d:288:p ysl%d:32:o" % ((_t,) * 9)
_DT = {"b": "bfloat16", "c": "float8_e4m3fn_x4", "p": "uint8", "i": "int32", "o": "uint16", "f": "float32"}
SCRATCH = {}
for _b in _BUFS.split():
    _p = _b.split(":") + ["f"]
    SCRATCH[_p[0]] = ("sbuf", [128, int(_p[1])], _DT[_p[2]])
BANKS = ["bv", "bs", "bk", "bx", "bf0", "bf1", "bf2", "bf3"]
for _b in BANKS:
    SCRATCH[_b] = ("psum", [128, 512], "float32")
PART = {"w1": ("ww", 0), "w2": ("ww", 288), "w3": ("ww", 576)}
SEMAPHORES = (["qv", "qs", "qt", "qg", "left", "dx", "du", "dn", "dw", "dp", "dv", "done"]
              + [p + k + str(t) for p in ("got", "rel") for k in "qsl" for t in range(R)] + ["d" + k + str(t) for k in "abc" for t in range(R)])

KEPT = 3
FIRST = 2
VC = (9, 10, 11)
VE = (1, 3, 5, 7, 9, 11, 13, 15)
PAIRS = sorted([(i, j) for i in range(L) for j in range(L) if i + j], key=lambda e: (e[0] + e[1], e[0]))[::-1]
ROW = 7
TILES = [(0, 288, (17, 16)), (288, 240, (15, 14, 13, 12)), (528, 176, (11, 10, 9, 8)), (704, 128, (7, 6, 5, 4)), (832, 128, (3, 2, 1))]

CYC, PICK, SCAT, ACT, WAKE, TRIP, LOAD = 1.0e-3, 1.5e-3, 3.5e-3, 0.02, 0.2, (8.0, 8.0, 3.6), 2.2
NEAR, TURNS, TRIES, SPREAD, SOME = 0.05, 20, 4000, 0.4, 0.02
CASES = ((0.4, 1.0, 1.0, 0.2), (0.4, 0.87, 0.85, 0.2), (1.3, 1.15, 1.25, 0.25))


def _relays(core, dst, topo):
    rel = [c for c in topo.cores_of(core) if c != core and topo.may_write(c, dst) and topo.die(c) == topo.die(core)]
    return [rel[0], rel[1 % len(rel)], rel[1 % len(rel)]]


def _piece(T, kind, k, t):
    if k == 0:
        return T["%sq%d" % (kind, t)][:, 0:C].bitcast(dt.uint8)
    if k == 1:
        return T[("hs_%d" if kind == "h" else kind + "s%d") % t][:, 0:C]
    return T[{"x": "al%d", "h": "hsl%d", "y": "ysl%d"}[kind] % t][:, 0:32]


def _relay_program(g, core, T, topo):
    n = 0
    for r in range(len(T.cores)):
        src, dst = T.cores[r], T.cores[(r + 1) % len(T.cores)]
        if topo.may_write(src, dst):
            continue
        rel = _relays(src, dst, topo)
        for t in range(R):
            for k in range(3):
                if rel[k] == core:
                    rid, pid = topo.addr(dst, core)
                    g.wait_ge(T.sem["rel" + "qsl"[k] + str(t)], len(topo.engines(src, core)))
                    g.remote_dma(_piece(T, "y", k, t), _piece(T, "h", k, t), T.sem["got" + "qsl"[k] + str(t)], T.sem.left, pid, rid, topo.mask(core, dst))
                    n += len(topo.engines(core, dst))
    if n:
        g.wait_ge(T.sem.left, n)


def _list_order(nodes, users, rank):
    left = [len(n["deps"]) for n in nodes]
    ready_at = [n.get("late", 0.0) for n in nodes]
    began = [0.0] * len(nodes)
    free, ready, out, end = {}, {}, [], 0.0
    for i, n in enumerate(nodes):
        if not left[i]:
            ready.setdefault(n["q"], []).append(i)
    while any(ready.values()):
        best = None
        for q, c in ready.items():
            if c:
                start = max(free.get(q, 0.0), min(ready_at[i] for i in c))
                if best is None or start < best[0]:
                    best = (start, q)
        start, q = best
        i = max([i for i in ready[q] if ready_at[i] <= start + NEAR], key=lambda i: rank[i])
        start = max(start, ready_at[i])
        ready[q].remove(i)
        out.append(i)
        began[i] = start
        free[q] = start + nodes[i]["occ"]
        end = max(end, free[q] + nodes[i]["lat"])
        for u in users[i]:
            ready_at[u] = max(ready_at[u], free[q] + nodes[i]["lat"] + nodes[u].get("late", 0.0) + (WAKE if nodes[u]["deps"][i] else 0.0))
            left[u] -= 1
            if not left[u]:
                ready.setdefault(nodes[u]["q"], []).append(u)
    return out, began, end


_ORDERS = {}


def _order(nodes):
    key = tuple((n["q"], n["occ"], tuple(n["deps"])) for n in nodes)
    if key in _ORDERS:
        return _ORDERS[key]
    users = [[] for n in nodes]
    for i, n in enumerate(nodes):
        for d in n["deps"]:
            users[d].append(i)
    tail = [0.0] * len(nodes)
    for i in reversed(range(len(nodes))):
        tail[i] = nodes[i]["occ"] + nodes[i]["lat"] + max([tail[u] + WAKE for u in users[i]] + [0.0])
    rng = np.random.default_rng(7)
    rank = np.array(tail)
    best = _list_order(nodes, users, tail)
    back = [{"q": n["q"], "occ": n["occ"], "lat": 0.0, "deps": {u: nodes[u]["deps"][i] for u in users[i]}, "late": n["lat"]} for i, n in enumerate(nodes)]
    o = best
    for k in range(TURNS):
        b = _list_order(back, [list(n["deps"]) for n in nodes], [o[1][i] + n["occ"] + n["lat"] for i, n in enumerate(nodes)])
        other = np.array([b[1][i] + n["occ"] for i, n in enumerate(nodes)])
        o = _list_order(nodes, users, list(other))
        if o[2] <= best[2]:
            best, rank = o, other
    cases = []
    for late, pace, picks, wake in CASES:
        occ = [(n["occ"] + (picks - 1.0) * n["pick"]) * pace for n in nodes]
        cases.append(([[(d, wake if w else 0.0) for d, w in n["deps"].items()] for n in nodes], occ,
                      [n["lat"] + (late if n["q"] == "net" else 0.0) for n in nodes], 1.0 / pace))
    which = ["vstgy".find(n["q"]) for n in nodes]

    def ends(o):
        s = o[2]
        for edges, occ, lat, weight in cases:
            done, free = [0.0] * len(nodes), [0.0] * 6
            for i in o[0]:
                at = free[which[i]]
                for d, w in edges[i]:
                    if done[d] + w > at:
                        at = done[d] + w
                free[which[i]] = at = at + occ[i]
                done[i] = at + lat[i]
            s += max(done) * weight
        return s

    least = ends(best)
    for k in range(TRIES):
        if k % 2:
            other = list(rank + rng.normal(0.0, SPREAD, len(nodes)) * (rng.random(len(nodes)) < SOME))
        else:
            other = list(rank)
            for i in rng.integers(0, len(nodes), 3):
                other[i] += rng.random() * 4 * SPREAD
                todo = [i]
                while todo:
                    j = todo.pop()
                    for d in nodes[j]["deps"]:
                        if other[d] <= other[j]:
                            other[d] = other[j] + 0.01
                            todo.append(d)
        o = _list_order(nodes, users, other)
        other = np.array(other)
        s = ends(o)
        if s <= least:
            best, rank, least = o, other, s
    _ORDERS[key] = best[0]
    return best[0]


def rank_program(g, core, T, topo):
    rank = T.rank_of(core)
    if rank is None:
        _relay_program(g, core, T, topo)
        return
    A = AluOpType
    F = ActivationFunctionType
    queue = {"v": g.vector, "s": g.scalar, "t": g.tensor, "g": g, "y": g.sync}
    qsem = {"v": "qv", "s": "qs", "t": "qt", "g": "qg"}
    picked = [0.0]
    nodes, log = [], {}

    def call(q, fn, rd, wr, occ=0.06, lat=0.0, sem=None, n=1):
        i, deps = len(nodes), {}
        for w, regs in ((0, rd), (1, wr)):
            for name, lo, hi, st in regs:
                for a in log.get(name, []):
                    if a["hi"] <= lo or hi <= a["lo"] or (st > 1 and a["st"] == st and (a["lo"] - lo) % st) or a["i"] == i:
                        continue
                    same = a["q"] == q and a["c"]
                    if w == 0 and not a["w"] and (same or name not in BANKS):
                        continue
                    deps[a["i"]] = deps.get(a["i"], False) or not (w == 1 and same and (not a["w"] or q == "t"))
        for w, regs in ((0, rd), (1, wr)):
            for name, lo, hi, st in regs:
                old = log.get(name, [])
                if w:
                    old = [a for a in old if not (lo <= a["lo"] and a["hi"] <= hi and (st == 1 or (a["st"] == st and (a["lo"] - lo) % st == 0)))]
                log[name] = old + [{"lo": lo, "hi": hi, "st": st, "q": q, "c": sem is None, "w": w, "i": i}]
        nodes.append({"q": q, "fn": fn, "deps": deps, "occ": occ, "lat": lat, "sem": sem, "n": n, "pick": picked[0]})
        picked[0] = 0.0
        return i

    def issue():
        count, clock, token = {}, {q: {} for q in queue}, {}
        for i in _order(nodes):
            e = nodes[i]
            q = e["q"]
            if q == "net":
                token[i] = (e["sem"], e["n"], {})
                continue
            need = {}
            for d, awaited in e["deps"].items():
                if awaited:
                    sem, val, seen = token[d]
                    if sem not in need or need[sem][1] < val:
                        need[sem] = token[d]
            for sem, val, seen in sorted(need.values(), key=lambda k: -len(k[2])):
                if clock[q].get(sem, 0) < val:
                    queue[q].wait_ge(T.sem[sem], val)
                    clock[q][sem] = val
                    for s, n in seen.items():
                        clock[q][s] = max(clock[q].get(s, 0), n)
            sem = e["sem"] or qsem[q]
            if sem == "left":
                e["fn"]()
            else:
                e["fn"]().then_inc(T.sem[sem], e["n"])
            count[sem] = count.get(sem, 0) + e["n"]
            token[i] = (sem, count[sem], dict(clock[q]))
        for s in count:
            g.wait_ge(T.sem[s], count[s])

    def dma(q, sem, out, in_, rd, wr, after=()):
        i = call(q, lambda: queue[q].dma_start(out, in_), rd, wr, 0.06, LOAD, sem, 16)
        for d in after:
            nodes[i]["deps"][d] = True
        return i

    def r(name, lo, hi, st=1):
        name, o = PART.get(name, (name, 0))
        return (name, lo + o, hi + o, st)

    def ap(v):
        if not isinstance(v, tuple):
            return v
        return T[v[0]][:, v[1]:v[2]] if v[3] == 1 else T[v[0]][:, v[1]:v[2]:v[3]]

    def wide(v, per=1.0):
        return max(64, per * len(range(v[1], v[2], v[3]))) * CYC

    def cost(out, off, per):
        picked[0] = PICK * len(range(out[1], out[2], out[3])) if off else 0.0
        return 0.05 + picked[0] if off else wide(out, per)

    def side(in_, off):
        return ap(in_) if off is None else ap(in_).indirect(ap(off))

    def views(*vs):
        return [v for v in vs if isinstance(v, tuple)]

    def half(*vs):
        return 0.5 if all(SCRATCH[v[0]][2] == "bfloat16" for v in vs) else 1.0

    def copy(out, in_, off=None):
        call("v", lambda: g.vector.tensor_copy(ap(out), side(in_, off)), views(in_, off), [out], cost(out, off, half(out, in_)))

    def tt(out, a, b, op, off=None):
        call("v", lambda: g.vector.tensor_tensor(ap(out), side(a, off), ap(b), op), views(a, b, off), [out], cost(out, off, 1.0 if a[0] in BANKS else 2.0))

    def ts(out, a, s1, op0, s2=None, op1=None, off=None):
        if op1 is None:
            call("v", lambda: g.vector.tensor_scalar(ap(out), side(a, off), ap(s1), None, op0), views(a, s1, off), [out], cost(out, off, half(out, a)))
        else:
            call("v", lambda: g.vector.tensor_scalar(ap(out), side(a, off), ap(s1), ap(s2), op0, op1), views(a, s1, s2, off), [out], cost(out, off, half(out, a)))

    def fill(v, c):
        call("v", lambda: g.vector.memset(ap(v), c), [], [v], wide(v, half(v)))

    def gfill(v, c):
        giota(v, [[0, len(range(v[1], v[2], v[3]))]], c)

    def giota(v, pattern, base, cm=0):
        call("g", lambda: g.iota(ap(v), pattern, base, cm, allow_small_or_imprecise_dtypes=True), [], [v], 0.13 + 2 * CYC * len(range(v[1], v[2], v[3])))

    def iota(out, pattern, base, cm):
        call("g", lambda: g.iota(ap(out), pattern, base, cm), [], [out], 0.13 + 2 * CYC * len(range(out[1], out[2], out[3])))

    def select(v, pattern, op, base, cm, in_=None):
        call("g", lambda: g.affine_select(ap(v), ap(in_ or v), pattern, op, 0.0, base, cm), [in_ or v], [v], 0.17 + 2 * CYC * len(range(v[1], v[2], v[3])))

    def turn(out, in_):
        call("v", lambda: g.vector.transpose(ap(out), ap(in_)), [in_], [out], wide(out))

    def total(out, in_):
        call("v", lambda: g.vector.tensor_reduce(ap(out), ap(in_), AxisListType.X, A.add), [in_], [out], wide(in_))

    def scan(out, d0, d1, first=0.0, op0=A.mult, op1=A.add):
        call("v", lambda: g.vector.tensor_tensor_scan(ap(out), ap(d0), ap(d1), first, op0, op1), [d0, d1], [out], wide(out, half(out, d0, d1)))

    def act(out, in_, f, bias=None, scale=None, off=None, acc=None):
        kw = {}
        if bias is not None: kw["bias"] = ap(bias)
        if scale is not None: kw["scale"] = ap(scale)
        if acc is not None: kw["accum_out"] = ap(acc)
        call("s", lambda: g.scalar.activation(ap(out), side(in_, off), f, **kw), views(in_, bias, scale, off), views(out, acc),
             cost(out, off, 1.0) + (0.0 if off else ACT) + (ACT if acc else 0.0))

    def quant(qn, sn, lo, hi, in_):
        call("v", lambda: g.vector.quantize_mx(T[qn][:, lo:hi], T[sn][:, lo:hi], ap(in_)), [in_], [r(qn, lo, hi), r(sn, lo, hi)], 0.012 + 0.00106 * (hi - lo))

    def mm(bank, n, st, sts, slo, mv, mvs, mlo, start=True, stop=True):
        call("t", lambda: g.tensor.matmul_mx(T[bank][:, 0:n], T[st][:, slo:slo + 128], T[sts][:, slo:slo + 128], T[mv][:, mlo:mlo + n], T[mvs][:, mlo:mlo + n], start, stop),
             [r(st, slo, slo + 128), r(sts, slo, slo + 128), r(mv, mlo, mlo + n), r(mvs, mlo, mlo + n)], [r(bank, 0, 512)], (n + 16) * CYC * 0.6)

    dma("y", "du", T.ut[:, :], T.u[:, :], [], [r("ut", 0, 512)])
    dma("s", "dx", T.xt[:, :], T.x[:, :], [], [r("xt", 0, 4 * C)])
    dma("y", "dn", T.li[:, :], T.nb[:, :], [], [r("li", 0, 36)])

    iota(r("pi", 0, 1), [[0, 1]], 0, 1)
    for k, (sh, mask) in enumerate(((0, 15), (0, 16), (4, 7), (0, 3), (2, 3), (0, 1), (4, 1), (1, 7))):
        ts(r("pi", 1 + k, 2 + k), r("pi", 0, 1), sh, A.logical_shift_right, mask, A.bitwise_and)
    copy(r("pf", 0, 8), r("pi", 1, 9))
    Q, H16, GRP, QL, QH, ODD, H, QHALF = [r("pf", k, k + 1) for k in range(8)]
    PW, RI, SEL, T1, T2, THR = [r("pf", k, k + 1) for k in range(8, 14)]
    giota(r("kf", 0, 18), [[16, 18]], 0)
    K16 = r("kf", 0, 18)
    UL, NEL, SBL, ORL, SELL, PERM, DKL, TKL = [r("ko", a, b) for a, b in ((0, 8), (8, 26), (26, 44), (44, 45), (46, 50), (50, 64), (64, 67), (68, 71))]
    copy(UL, r("kf", 0, 8))
    quant("uq", "us", 0, 128, r("ut", 0, 512))
    call("v", lambda: g.vector.tensor_copy(T.urq[:, 0:128].bitcast(dt.uint32), T.uq[:, 0:128].bitcast(dt.uint32).indirect(ap(UL))), [r("uq", 0, 128), UL], [r("urq", 0, 128)], 0.25)
    call("s", lambda: g.scalar.activation(T.urs[:, 0:128], T.us[:, 0:128].indirect(ap(UL)), F.Copy), [r("us", 0, 128), UL], [r("urs", 0, 128)], 0.25)
    giota(r("j16", 0, C), [[0, 18], [1, 16]], 0)
    giota(r("iob", 0, 304), [[1, 304]], -int(MID))
    ts(r("mask16", 0, C), r("j16", 0, C), Q, A.is_equal)
    ts(r("keep", 0, C), r("j16", 0, C), 0.0, A.is_gt)
    copy(r("lf", 0, 36), r("li", 0, 36))
    copy(r("ll", 0, 36), r("li", 0, 36))
    fill(r("fa", 0, 36, 2), 0.0)
    tt(r("fa", 1, 36, 2), r("li", 18, 36), r("li", 0, 18), A.subtract)
    copy(r("fb", 1, 36, 2), r("li", 0, 18))
    for name, w, col in (("ci", 0, RI), ("cj", 1, PW)):
        v = [-64] + [e[w] for e in PAIRS] + [0]
        c = [v[t] - v[t + 1] for t in range(16)]
        usual = max(sorted(set(c)), key=c.count)
        fill(r(name, 0, C), float(usual))
        for t in range(16):
            if c[t] != usual:
                act(r(name, t, C, 16), r(name, t, C, 16), F.Identity, float(c[t]), 0.0)
        o = 16 + 16 * w
        if w == 0:
            ts(r("q3", 0, 16), r("j16", 0, 16), Q, A.is_ge)
        tt(r("q3", o, o + 16), r("q3", 0, 16), r(name, 0, 16), A.mult)
        total(col, r("q3", o, o + 16))
    ts(r("pf", 16, 20), r("j16", 0, 4), PW, A.is_equal)
    for k in range(L):
        act(r("io", C * k, C * k + C), r("iob", 0, C), F.Copy, None, r("pf", 16 + k, 17 + k))
    ts(T2, RI, float(ROW), A.add, 0.0, A.max)
    ts(NEL, K16, T2, A.add)
    ts(SBL, K16, 15.0, A.add)
    ts(ORL, QHALF, 6.5, A.is_ge)
    ORV = r("ko", 72, 73)
    ts(r("pf", 23, 24), QHALF, 0.5, A.is_ge, 144.0, A.mult)
    ts(ORV, r("pf", 23, 24), 143.0, A.add)
    ts(SEL, QL, 32.0, A.mult, H16, A.add)
    ts(r("ko", 46, 47), QH, SEL, A.add)
    ts(r("pf", 20, 21), QH, -1.0, A.mult, 6.0, A.add)
    ts(r("ko", 47, 48), r("pf", 20, 21), SEL, A.add)
    ts(r("ko", 48, 49), SEL, 7.0, A.add)
    ts(r("ko", 49, 50), SEL, 6.0, A.add)
    MB, NB, NC = r("kf", 20, 25), r("kf", 26, 44), r("kf", 44, 62)
    ts(r("kf", 64, 68), r("kf", 0, 4), Q, A.add, 0.5, A.add)
    ts(r("kf", 68, 72), r("kf", 64, 68), float(M), A.is_ge, 1000.0, A.mult)
    tt(r("kf", 156, 160), r("kf", 64, 68), r("kf", 68, 72), A.add)
    act(r("kf", 20, 24), r("kf", 156, 160), F.Copy, None, FLAG)
    act(r("kf", 24, 25), Q, F.Identity, (M - 0.5) * FLAG, 0.0)
    gfill(r("fl", 0, C), int(FLAG))
    ts(NC, K16, Q, A.add, -MID, A.add)
    act(NB, NC, F.Copy, None, -512.0)
    JJ = r("kf", 100, 103)
    ts(JJ, r("kf", 0, 3), Q, A.add)
    ts(r("pf", 21, 22), H, -34.0, A.mult, 71.0, A.add)
    ts(r("pf", 22, 23), ODD, H, A.not_equal, r("pf", 21, 22), A.mult)
    ts(DKL, JJ, r("pf", 22, 23), A.add, 107.0, A.min)
    ts(r("kf", 104, 107), JJ, 18.0, A.is_ge, -18.0, A.mult)
    ts(r("kf", 108, 111), JJ, 36.0, A.is_ge, -18.0, A.mult)
    tt(r("kf", 112, 115), r("kf", 104, 107), r("kf", 108, 111), A.add)
    tt(r("kf", 116, 119), r("kf", 112, 115), JJ, A.add)
    ts(TKL, r("kf", 116, 119), 16.0, A.mult, 15.0, A.add)
    gfill(r("dk", 0, 108), 0)
    act(r("cap", 0, C), r("mask16", 0, C), F.Copy, None, FAR)
    act(r("kf", 160, 178), K16, F.Identity, -FAR)
    act(r("pf", 24, 25), r("mask16", 0, 1), F.Identity, -1.0)
    act(r("pf", 25, 26), r("mask16", 0, 1), F.Copy, None, -1.0)
    act(r("pf", 26, 30), r("mask16", 0, 4), F.Copy, None, FAR)
    act(r("pf", 30, 31), r("mask16", 2, 3), F.Identity, 1.0, -1.0)
    act(r("pf", 31, 32), r("mask16", 2, 3), F.Copy)
    for e in range(2):
        act(r("cap", 2 + e, C, 16), r("kf", 160, 178), F.Identity, r("pf", 28 + e, 29 + e), r("pf", 30 + e, 31 + e))
    gfill(r("acc", 0, 16), 0)
    gfill(r("rsum", 0, 1), 0)
    gfill(r("jt", 0, 528), 1)
    select(r("jt", 0, 520), [[-1, 520]], A.is_equal, 3, 4)
    for b in range(4):
        quant("eq", "es", 128 * b, 128 * b + 128, r("jt", 3 - b, 515 - b))
        gfill(r("fh", 304 * b + C, 304 * b + 304), 0)
    giota(r("gt", 0, 128), [[1, 8], [0, 16]], 0)
    for e in (512, 513, 514, 515, 0, 1):
        ts(r("rt", e, e // 4 * 4 + 512, 4), r("gt", 0, 128), GRP, A.is_equal)
    select(r("rt", 2, 512, 4), [[-1, 128]], A.is_gt, 0, 1, r("rt", 512, 1024, 4))
    select(r("rt", 3, 512, 4), [[1, 128]], A.is_gt, 0, -1, r("rt", 512, 1024, 4))
    quant("rq", "rs", 0, 256, r("rt", 0, 1024))
    for lo, n, blocks in TILES[:3]:
        fill(r("sg", 4 * (lo + 16 * blocks[-1]), 4 * (lo + n)), 0.0)
    fill(r("sg", 4 * 768, 4 * 960), 0.0)
    quant("fq", "fs", 832, 960, r("sg", 4 * 832, 4 * 960))
    gfill(r("mt", 0, C), 0)
    gfill(r("st", C, 304), C - int(MID))
    gfill(r("dl", 0, NE), -4)
    gfill(r("dl", 64, NE, 64), 251)
    gfill(r("dl", NE, NE + 1), NS - 1)
    gfill(r("ea", NE, 18 * (NE + 2), NE + 2), 1024)
    giota(r("slot", 0, NZ), [[1, 4], [4, 64]], 0)
    act(r("tabk", 0, 304), r("iob", 0, 304), F.Copy, None, 512.0)
    gfill(r("ab", 64, 96, 2), 0)

    n_of = len(T.cores)
    dst, src = T.cores[(rank + 1) % n_of], T.cores[(rank - 1) % n_of]
    direct = topo.may_write(core, dst)
    hops = [dst] * 3 if direct else _relays(core, dst, topo)
    came = [src] * 3 if topo.may_write(src, core) else _relays(src, core, topo)

    def send(k, t, after=()):
        rid, pid = topo.addr(hops[k], core)
        name, n = (("xq%d", C), ("xs%d", C), ("al%d", 32))[k]
        i = call("g", lambda: g.remote_dma(_piece(T, "y" if direct else "h", k, t), _piece(T, "x", k, t), T.sem[("got" if direct else "rel") + "qsl"[k] + str(t)], T.sem.left, pid, rid, topo.mask(core, hops[k])),
                 [r(name % t, 0, n)], [], 0.5, 0.0, "left", len(topo.engines(core, hops[k])))
        for d in after:
            nodes[i]["deps"][d] = True
        far = call("net", None, [], [r(("yq%d", "ys%d", "ysl%d")[k] % t, 0, n)], 0.0, TRIP[k], "got" + "qsl"[k] + str(t), len(topo.engines(came[k], core)))
        nodes[far]["deps"][i] = True

    for t in range(R):
        XQ, XS = "xq%d" % t, "xs%d" % t
        for lo, bank in ((HALF, "bk"), (0, "bx")):
            quant(XQ, XS, lo, lo + HALF, r("xt", 4 * lo, 4 * (lo + HALF)))
            mm(bank, HALF, "urq", "urs", 0, XQ, XS, lo)
            tt(r("sm", lo, lo + HALF), r(bank, 0, HALF), r("mask16", 0, HALF), A.mult)
            scan(r("so", lo, lo + HALF), r("keep", 0, HALF), r("sm", lo, lo + HALF))
        mm("bv", C, "urq", "urs", 0, XQ, XS, 0)
        mm("bs", C, "urq", "urs", 0, XQ, XS, 0)
        for b in range(KEPT):
            mm("bf%d" % b, C, "eq", "es", 128 * b, XQ, XS, 0)
            act(r("ff", C * b, C * b + C), r("bf%d" % b, 0, C), F.Copy)
        ts(r("fb", 0, 36, 2), r("so", 15, C, 16), 0.0, A.is_gt)
        scan(r("fc", 0, 36), r("fa", 0, 36), r("fb", 0, 36))
        CL = r("cl", 0, 18)
        copy(CL, r("fc", 1, 36, 2))
        act(r("sr", 0, C), r("bs", 0, C), F.Copy)
        LATER = [dma("y", "da%d" % t, T["io"][0:128:16, 0:C], T.sr[0:128:16, 0:C], [r("sr", 0, C)], [r("io", 0, C)])]
        if t == 0:
            dma("y", "dw", T.wq[:, :].bitcast(dt.uint8), T.wc[:, :], [], [r("wq", 0, 512)], LATER)
            dma("y", "dp", T.wp[:, :], T.ws[:, :], [], [r("wp", 0, 512)], LATER)
            dma("y", "dv", T.vt[:, :], T.v[:, :], [], [r("vt", 0, 512)], LATER)
            quant("vq", "vs", 0, 128, r("vt", 0, 512))
        for k in range(2):
            send(k, t, LATER)
        act(r("sb", 0, C), r("so", 0, C), F.Copy, off=SBL)
        tt(r("sg", 2, 4 * C, 4), r("bv", 0, C), r("sb", 0, C), A.is_lt)
        tt(r("sg", 3, 4 * C, 4), r("bv", 0, C), r("sb", 0, C), A.is_le)
        for x, (lo, n, blocks) in enumerate(TILES):
            for e, k in enumerate(blocks):
                v, s = r("sg", 4 * lo + e, 4 * (lo + 16 * k), 4), r("so", 16 * k + 15, 16 * k + 16)
                if k in VC:
                    ts(v, r("bv", 0, 16 * k), s, A.is_lt)
                    act(r("junk", 8 * k * (k - 1), 8 * k * (k + 1)), v, F.Copy, acc=r("rsum", k, k + 1))
                else:
                    act(v, r("bs", 0, 16 * k), F.Sign, s, -1.0)
                    act(v, v, F.Relu, acc=r("rsum", k, k + 1))
            if x < 3:
                quant("fq", "fs", lo, lo + n, r("sg", 4 * lo, 4 * (lo + n)))
        quant("fq", "fs", 704, 880, r("sg", 4 * 704, 4 * 880))
        for x, (lo, n, blocks) in enumerate(TILES):
            mm("bk", n, "rq", "rs", 128 if x else 0, "fq", "fs", lo, x == 0, x == 4)
        for e in range(2):
            act(r("cap", e, C, 16), r("rsum", 0, 18), F.Identity, r("pf", 26 + e, 27 + e), r("pf", 24 + e, 25 + e))
        for lo in (0, HALF):
            tt(r("sm2", lo, lo + HALF), r("bk", lo, lo + HALF), r("cap", lo, lo + HALF), A.min)
            scan(r("po", lo, lo + HALF), r("keep", 0, HALF), r("sm2", lo, lo + HALF))
        ts(r("pl", 0, 18), r("po", 15, C, 16), FAR, A.add)
        tt(r("w1", 0, C), r("io", 3 * C, 4 * C), r("io", 2 * C, 3 * C), A.add, CL)
        tt(r("w2", 0, C), r("w1", 0, C), r("io", C, 2 * C), A.add, CL)
        tt(r("w3", 0, C), r("w2", 0, C), r("io", 0, C), A.add, CL)
        act(r("pq", C, 2 * C), r("w3", 0, C), F.Copy, off=r("ll", 18, 36))
        copy(r("pq", 0, C), r("w3", 0, C), r("ll", 0, 18))
        turn(r("tpq", 0, C), r("pq", 0, C))
        turn(r("tpq", C, 2 * C), r("pq", C, 2 * C))
        tt(r("ne", 0, C), r("tpq", 0, C), r("tpq", C, 2 * C), A.not_equal, NEL)
        scan(r("ij", 0, C), r("ne", 0, C), r("ci", 0, C))
        scan(r("ij", C, 2 * C), r("ne", 0, C), r("cj", 0, C))
        P = [r("tpq", ROW + k, C, 16) for k in range(L)]
        U = [r("tpq", C + ROW + k, 2 * C, 16) for k in range(L)]
        I = r("ij", 15, C, 16)

        def role(name, k):
            return r(name, k, C, 16)

        for k in range(1, L):
            o = 72 * k - 72
            tt(r("q3", o, o + 18), P[k], P[k - 1], A.subtract)
            tt(r("q3", o + 18, o + 36), U[k - 1], U[k], A.subtract)
            ts(r("q3", o + 36, o + 72), r("ij", 15, 2 * C, 16), float(k), A.is_ge)
            tt(role("mt", k), r("q3", o, o + 18), r("q3", o + 36, o + 54), A.mult)
            tt(role("mt", 7 - k), r("q3", o + 18, o + 36), r("q3", o + 54, o + 72), A.mult)
        tt(role("mt", 7), r("tpq", C, 2 * C, 16), r("tpq", 0, C, 16), A.is_gt)
        tt(r("q3", 216, 234), P[0], U[0], A.is_equal)
        act(r("q3", 234, 252), r("q3", 216, 234), F.Copy, None, -FLAG)
        tt(r("q3", 252, 270), r("q3", 234, 252), P[0], A.add)
        ts(r("q3", 270, 288), I, 0.0, A.is_lt, -FLAG, A.mult)
        tt(role("mt", 0), r("q3", 252, 270), r("q3", 270, 288), A.add)
        scan(r("tb", 0, C), r("keep", 0, C), r("mt", 0, C))
        turn(r("tr", 0, C), r("tb", 0, C))
        picked[0] = SCAT * C
        call("v", lambda: g.vector.tensor_copy(T.st[:, 0:C].indirect(T.pl[:, 0:18]), T.tr[:, 0:C]), [r("tr", 0, C), r("pl", 0, 18)], [r("st", 0, C)], 0.05 + SCAT * C)
        scan(r("cn", 0, C), r("st", 0, C), r("fl", 0, C), 0.0, A.add, A.add)
        for c in (0, 1, 4):
            act(r("jc", C * c, C * c + C), r("cn", 0, C), F.Sign, r("kf", 20 + c, 21 + c), -1.0, acc=r("acc", 8 * (c // 4) + c % 4, 8 * (c // 4) + c % 4 + 1))
        for c in (2, 3):
            ts(r("jc", C * c, C * c + C), r("cn", 0, C), r("kf", 20 + c, 21 + c), A.is_le, 0.5, A.subtract)
            scan(r("jd", 144 * c - C, 144 * c - 144), r("jc", C * c, C * c + 144), r("jc", C * c + 144, C * c + C), 0.0, A.add, A.add)
        ts(r("ordl", 0, 16), r("acc", 0, 8), 0.5, A.mult, C / 2, A.add, ORL)
        ts(r("ordl", 16, 32), r("jd", 0, C), C / 2, A.add, off=ORV)
        act(r("gt", 0, 64), r("st", 0, 304), F.Copy, off=r("ordl", 12, 16))
        copy(r("gt", 64, 128), r("st", 0, 304), r("ordl", 16, 20))
        turn(r("tg", 0, 128), r("gt", 0, 128))
        ts(r("al%d" % t, 0, 32), r("tg", 0, 128), MID, A.add, off=r("ko", 46, 48))
        send(2, t)
        copy(r("ab", 0, 64), r("tg", 0, 128), SELL)
        tt(r("ab", 96, 128, 2), r("ab", 32, 48), r("ab", 48, 64), A.subtract)
        tt(r("ab", 65, 96, 2), r("ab", 16, 32), r("ab", 0, 16), A.subtract)
        act(r("ab", 97, 128, 2), r("ab", 0, 16), F.Copy)
        scan(r("ab", 128, 160), r("ab", 64, 96), r("ab", 96, 128))
        ts(r("bnl", 0, 16), r("ab", 129, 160, 2), MID, A.add)
        act(r("bnr", 0, NZ), r("iob", 0, 304), F.Copy, off=r("bnl", 0, 16))
        tt(r("ks", 0, NZ), r("tabk", 0, 304), r("slot", 0, NZ), A.add, r("bnl", 0, 16))
        for k in range(18):
            o = (NE + 2) * k
            if k in VE:
                ts(r("ea", o, o + NE), r("bnr", 0, NE), r("kf", 44 + k, 45 + k), A.not_equal, 512.0, A.mult)
                scan(r("eo", o, o + NE + 1), r("dl", 0, NE + 1), r("ea", o, o + NE + 1), 1024.0, A.add, A.min)
            else:
                act(r("ea", o, o + NE), r("ks", 0, NE), F.Abs, r("kf", 26 + k, 27 + k))
                scan(r("eo", o + NE // 2 + 1, o + NE + 1), r("ea", o, o + NE // 2), r("ea", o + NE // 2, o + NE), 1024.0, A.min, A.min)
        E = r("eo", NE, 18 * (NE + 2), NE + 2)
        ts(r("ki", 48, 66), E, float(NS), A.min)
        ts(r("kf", 120, 138), E, float(NS), A.min, 64.0, A.mult)
        ts(r("ki", 66, 84), r("ki", 48, 66), 2, A.logical_shift_right)
        ts(r("kf", 138, 156), r("ki", 66, 84), -255.0, A.mult)
        tt(r("em", 0, 18), r("kf", 120, 138), r("kf", 138, 156), A.add)
        copy(r("el", 0, 18), r("em", 0, 18))
        o = 288
        ts(r("q3", o, o + 18), role("tb", 0), -FLAG / 2, A.is_ge)
        tt(r("q3", o + 18, o + 36), r("q3", o, o + 18), role("mt", 7), A.mult)
        tt(r("q3", o + 36, o + 54), r("q3", o, o + 18), r("q3", o + 18, o + 36), A.subtract)
        tt(r("q3", o + 54, o + 72), role("tb", 3), role("tb", 0), A.subtract)
        tt(r("q3", o + 72, o + 90), role("tb", 3), role("tb", 6), A.subtract)
        tt(r("dk", 0, 18), r("q3", o + 54, o + 72), r("q3", o + 18, o + 36), A.mult)
        tt(r("dk", 18, 36), r("q3", o + 72, o + 90), r("q3", o + 36, o + 54), A.mult)
        dma("y", "db%d" % t, T.dk[16:128, 36:72], T.dk[0:112, 0:36], [r("dk", 0, 36)], [r("dk", 36, 72)])
        dma("y", "dc%d" % t, T.dk[0:112, 72:108], T.dk[16:128, 0:36], [r("dk", 0, 36)], [r("dk", 72, 108)])
        ts(THR, r("acc", 8, 9), 0.5, A.mult, C / 2 - FAR, A.add)
        ts(r("tk", 0, 48), r("po", 0, C), THR, A.is_le, off=TKL)
        tt(r("tk", 48, 96), r("dk", 0, 108), r("tk", 0, 48), A.mult, DKL)
        tt(r("lf", 0, 36), r("lf", 0, 36), r("tk", 48, 84), A.add)
        copy(r("ll", 0, 36), r("lf", 0, 36))
        if t < R - 1:
            copy(r("fb", 1, 36, 2), r("lf", 0, 18))
            tt(r("fa", 1, 36, 2), r("lf", 18, 36), r("lf", 0, 18), A.subtract)
        else:
            act(r("lof", 0, 2 * C), r("iob", 0, 304), F.Identity, MID, off=r("ll", 0, 36))
            dma("y", "done", T.ol[:, :], T.lof[0:128:16, :], [r("lof", 0, 2 * C)], [])
        for b in range(4):
            mm("bf%d" % b, C, "eq", "es", 128 * b, "yq%d" % t, "ys%d" % t, 0)
            act(r("fh", 304 * b, 304 * b + C), r("bf%d" % b, 0, C), F.Copy, None, 0.5)
        for b in range(4):
            HB = r("fh", 304 * b, 304 * b + 304)
            act(r("ga", NZ * b, NZ * b + 192), HB, F.Copy, off=r("ysl%d" % t, 0, 12))
            tt(r("zt", b, 768, 4), HB, r("ga", NZ * b, NZ * b + 192), A.add, r("ysl%d" % t, 16, 28))
            if b < FIRST:
                ts(r("zt", 768 + b, 4 * NZ, 4), HB, 2.0, A.mult, off=r("ysl%d" % t, 12, 16))
            else:
                act(r("zt", 768 + b, 4 * NZ, 4), HB, F.Copy, None, 2.0, r("ysl%d" % t, 12, 16))
        for lo, bank in ((0, "bf0"), (128, "bf1")):
            quant("zq", "zs", lo, lo + 128, r("zt", 4 * lo, 4 * lo + 512))
            mm(bank, 128, "wq", "wp", 0, "zq", "zs", lo)
            act(r("hs", lo, lo + 128), r(bank, 0, 128), F.Copy, None, 0.03125)
        for b in range(4):
            if b:
                mm(BANKS[b - 1], NZ, "wq", "wp", 128 * b, "zq", "zs", 0)
                act(r("hs", NZ * b, NZ * b + NZ), r(BANKS[b - 1], 0, NZ), F.Copy, None, 0.03125)
            if b < KEPT:
                tt(r("xt", b, 4 * C, 4), r("hs", NZ * b, NZ * b + NZ), r("ff", C * b, C * b + C), A.add, r("el", 0, 18))
            else:
                act(r("gp", 0, C), r("hs", NZ * b, NZ * b + NZ), F.Copy, off=r("el", 0, 18))
                mm("bf%d" % b, C, "eq", "es", 128 * b, XQ, XS, 0)
                tt(r("xt", b, 4 * C, 4), r("bf%d" % b, 0, C), r("gp", 0, C), A.add)

    for lo, bank in ((0, "bk"), (HALF, "bx")):
        quant("xq3", "xs3", lo, lo + HALF, r("xt", 4 * lo, 4 * (lo + HALF)))
        mm(bank, HALF, "vq", "vs", 0, "xq3", "xs3", lo)
    act(r("yo", 0, HALF), r("bk", 0, HALF), F.Copy)
    copy(r("yo", HALF, C), r("bx", 0, HALF))
    dma("y", "done", T.oc[:, :], T.xq3[:, 0:C].bitcast(dt.uint8), [r("xq3", 0, C)], [])
    for k in range(4):
        dma("ys"[k % 2], "done", T.osc[4 * k:4 * k + 4, :], T.xs3[32 * k:32 * k + 4, 0:C], [r("xs3", 0, C)], [])
    dma("y", "done", T.y[:, :], T.yo[:, :], [r("yo", 0, C)], [])
    issue()
